import numpy as np
import ml_dtypes


def mxq(x, axis, fmt="e4m3"):
    dtype, down = {"e4m3": (ml_dtypes.float8_e4m3fn, 7), "e5m2": (ml_dtypes.float8_e5m2, 14)}[fmt]
    v = np.moveaxis(np.asarray(x, np.float32).astype(ml_dtypes.bfloat16).astype(np.float64), axis, -1)
    blocks = v.reshape(v.shape[:-1] + (-1, 32))
    amax = np.abs(blocks).max(-1, keepdims=True)
    byte = np.maximum(np.where(amax > 0, np.frexp(amax)[1] - 1 + 127, 0) - down, 1)
    scale = np.exp2(byte - 127.0)
    codes = (blocks / scale).astype(np.float32).astype(dtype).astype(np.float64)
    return np.moveaxis((codes * scale).reshape(v.shape), -1, axis)


WIDE = False


def mx_kscale(k):
    if not WIDE:
        return np.ones(k)
    levels = np.array([10, -10, 5, -5, 0])
    if k % 512:
        return np.exp2(np.random.permutation(np.resize(levels, k // 32))).repeat(32)
    a = np.empty((k // 512, 16))
    for p in range(k // 512):
        a[p, :8] = np.random.permutation(np.resize(levels, 8))
        for g in range(8):
            far = levels[np.abs(levels - a[p, g]) >= 10]
            a[p, g + 8] = far[np.random.randint(len(far))]
    return np.exp2(a.ravel()).repeat(32)


def f64(x):
    return np.asarray(x).astype(np.float64)


def striped(idx):
    return np.tile(idx.reshape(-1, 16).T, (8, 1)).astype(np.uint16)


def unstriped(offs):
    return offs[:16].T.reshape(-1).astype(np.int64)


E2M1 = np.array([0.0, 0.5, 1.0, 1.5, 2.0, 3.0, 4.0, 6.0, -0.0, -0.5, -1.0, -1.5, -2.0, -3.0, -4.0, -6.0])


def pack_weight(w, fmt):
    k, n = w.shape
    w = f64(np.asarray(w, np.float32).astype(ml_dtypes.bfloat16)).reshape(k // 32, 32, n)
    amax = np.abs(w).max(1)
    if fmt == "e4m3":
        byte = np.frexp(amax)[1] - 1 + 127 - 7
    else:
        mant, ex = np.frexp(amax / 6.0)
        byte = np.where(mant > 0.5, ex, ex - 1) + 127
    byte = np.clip(np.where(amax > 0, byte, 1), 1, 254)
    scaled = (w * np.exp2(127.0 - byte)[:, None, :]).reshape(k, n).astype(np.float32)
    by_word = np.ascontiguousarray(scaled.reshape(k // 512, 128, 4, n).transpose(0, 1, 3, 2))
    if fmt == "e4m3":
        words = by_word.astype(ml_dtypes.float8_e4m3fn).view(np.uint8)
    else:
        c = by_word.astype(ml_dtypes.float4_e2m1fn).view(np.uint8) & 0xF
        words = (c[..., 0::2] | (c[..., 1::2] << 4)).reshape(k // 512, 128, 2 * n)
    return np.ascontiguousarray(words), np.ascontiguousarray(byte.astype(np.uint8).reshape(k // 512, 16, n))


def unpack_weight(words, scales, fmt):
    g, _, n = scales.shape
    words = np.ascontiguousarray(words).reshape(g, 128, n, -1)
    if fmt == "e4m3":
        vals = words.view(ml_dtypes.float8_e4m3fn).astype(np.float64)
    else:
        nib = np.empty((g, 128, n, 4), np.uint8)
        nib[..., 0::2] = words & 0xF
        nib[..., 1::2] = words >> 4
        vals = E2M1[nib]
    vals = vals * np.repeat(np.exp2(scales.astype(np.float64) - 127.0), 8, axis=1)[..., None]
    return vals.transpose(0, 1, 3, 2).reshape(g * 512, n)


def gelu(v):
    return 0.5 * v * (1.0 + np.tanh(np.sqrt(2.0 / np.pi) * (v + 0.044715 * v**3)))


K, T, E, C, H, N = 1536, 768, 3, 256, 512, 256


def by_expert(wq, xq):
    return np.concatenate([wq[e].T @ xq[:, e * C:(e + 1) * C] for e in range(E)], axis=1)


def setup_inputs():
    n = np.random.standard_normal
    s = mx_kscale(K)
    u = mx_kscale(H)
    slot_token = np.random.permutation(T)[:E * C]
    x = pack_weight(n((K, T)) * s[:, None], "e4m3")
    w = [pack_weight(m, "e2m1") for m in n((E, K, N)) / np.sqrt(K) / s[None, :, None]]
    return {
        "x_words": x[0],
        "x_scales": x[1],
        "w_words": np.stack([m[0] for m in w]),
        "w_scales": np.stack([m[1] for m in w]),
        "wa": (n((E, K, H)) / np.sqrt(K) / s[None, :, None] * u).astype(np.float32),
        "wb": (n((E, H, N)) / np.sqrt(H) / u[None, :, None]).astype(np.float32),
        "gate": np.tile(np.random.uniform(0.2, 1.0, E * C), (128, 1)).astype(np.float32),
        "offs": striped(slot_token),
    }


def reference(x_words, x_scales, w_words, w_scales, wa, wb, gate, offs):
    w = np.stack([unpack_weight(w_words[e], w_scales[e], "e2m1") for e in range(E)])
    waq = mxq(f64(wa), 1, "e4m3")
    wbq = mxq(f64(wb), 1, "e4m3")
    idx = unstriped(offs)
    xq = unpack_weight(x_words, x_scales, "e4m3")[:, idx]
    h = gelu(by_expert(waq, xq))
    y = by_expert(w, xq) + by_expert(wbq, mxq(h, 0, "e4m3"))
    out = np.zeros((N, T))
    out[:, idx] = f64(gate[:1]) * y
    return out

@@ -1,0 +1,240 @@
+from contextlib import ExitStack
+
+import concourse.mybir as mybir
+
+K, T, E, C, H, N = 1536, 768, 3, 256, 512, 256
+FLOPS = 2 * E * C * (K * N + K * H + H * N)
+
+F32 = mybir.dt.float32
+BF16 = mybir.dt.bfloat16
+I32 = mybir.dt.int32
+U32 = mybir.dt.uint32
+U16 = mybir.dt.uint16
+U8 = mybir.dt.uint8
+FP8X4 = mybir.dt.float8_e4m3fn_x4
+FP4X4 = mybir.dt.float4_e2m1fn_x4
+GELU = mybir.ActivationFunctionType.Gelu_apprx_tanh
+MULT = mybir.AluOpType.mult
+
+P = 128
+PACK = 4
+K_PASS = P * PACK
+PASSES = K // K_PASS
+UNIT = 128
+UNITS = C // UNIT
+N_TILES = N // P
+QUADS = 4
+ROWS = 4
+MOVED_ROWS = 112
+
+VECTOR_SHARE = [[0, 0, 48], [0, 0, 48], [0, 0, 84]]
+
+
+def tile_moe_elr_gelu_kernel(
+    tc, x_words, x_scales, w_words, w_scales, wa, wb, gate, offs, out
+):
+    nc = tc.nc
+    with ExitStack() as ctx:
+        keep = ctx.enter_context(tc.tile_pool(name="keep", bufs=1))
+        stream = ctx.enter_context(tc.tile_pool(name="stream", bufs=3))
+        h_psum = ctx.enter_context(tc.psum_pool(name="h_psum", bufs=4))
+        y_psum = ctx.enter_context(tc.psum_pool(name="y_psum", bufs=2))
+
+        def sb(name, shape, dtype):
+            return keep.tile(shape, dtype, name=name, align_bytes=64)
+
+        offsets = keep.tile([P, T // 16], U16, name="offsets")
+        token_words = [sb("token_words%d" % s, [P, T], I32) for s in range(PASSES)]
+        token_scales = sb("token_scales", [P, T], U8)
+        slot_words = [sb("slot_words%d" % s, [P, T], U32) for s in range(PASSES)]
+        slot_scales = sb("slot_scales", [P, T], U8)
+        moved_scales = [sb("moved_scales%d" % s, [P, T], U8) for s in range(1, PASSES)]
+        frozen_words = [sb("frozen_words%d" % e, [P, PASSES, 2 * N], U8) for e in range(E)]
+        frozen_scales = sb("frozen_scales", [P, E * PASSES, N], U8)
+        wa_raw = [
+            [stream.tile([P, PACK, H], F32, name="wa_raw%d_%d" % (e, s), tag="wa_raw") for s in range(PASSES)]
+            for e in range(E)
+        ]
+        wa_bf = [[sb("wa_bf%d_%d" % (e, s), [P, PACK * H], BF16) for s in range(PASSES)] for e in range(E)]
+        wa_codes = [[sb("wa_codes%d_%d" % (e, s), [P, H], U32) for s in range(PASSES)] for e in range(E)]
+        wa_scales = [[sb("wa_scales%d_%d" % (e, s), [P, H], U8) for s in range(PASSES)] for e in range(E)]
+        wb_raw = [sb("wb_raw%d" % e, [P, PACK, N], F32) for e in range(E)]
+        wb_bf = [sb("wb_bf%d" % e, [P, PACK * N], BF16) for e in range(E)]
+        wb_codes = [sb("wb_codes%d" % e, [P, N], U32) for e in range(E)]
+        wb_scales = [sb("wb_scales%d" % e, [P, N], U8) for e in range(E)]
+        gates = [sb("gates%d" % e, [P, C], F32) for e in range(E)]
+        results = [sb("results%d" % nt, [P, T], F32) for nt in range(N_TILES)]
+        warm = sb("warm", [P, 2], F32)
+
+        nc.vector.memset(token_scales[:].bitcast(I32), 0)
+        nc.vector.memset(warm[:, 0:1], 0.0)
+        nc.vector.memset(frozen_scales[:].rearrange("p g n -> p (g n)").bitcast(I32), 0)
+        for moved in moved_scales:
+            nc.vector.memset(moved[:].bitcast(I32), 0)
+
+        nc.scalar.activation(out=warm[:, 1:2], in_=warm[:, 0:1], func=GELU)
+        for q in range(QUADS):
+            nc.gpsimd.dma_start(
+                out=frozen_scales[32 * q : 32 * q + ROWS, :, :].bitcast(I32),
+                in_=w_scales[:, :, ROWS * q : ROWS * (q + 1), :].rearrange("e s r n -> r (e s) n").bitcast(I32),
+            )
+
+        def load_tokens(s):
+            nc.sync.dma_start(out=token_words[s][:], in_=x_words[s].rearrange("p t d -> p (t d)").bitcast(I32))
+
+        def load_wa(e, s):
+            rows = wa[e, s * K_PASS : (s + 1) * K_PASS, :].rearrange("(p j) i -> p j i", j=PACK)
+            if (e, s) == (E - 1, PASSES - 1):
+                for c0 in (0, H // 2):
+                    nc.sync.dma_start(out=wa_raw[e][s][:, :, c0 : c0 + H // 2], in_=rows[:, :, c0 : c0 + H // 2])
+            else:
+                nc.sync.dma_start(out=wa_raw[e][s][:], in_=rows)
+
+        def load_rest(e):
+            nc.sync.dma_start(out=wb_raw[e][:], in_=wb[e].rearrange("(p j) n -> p j n", j=PACK))
+            nc.sync.dma_start(
+                out=frozen_words[e][:].bitcast(I32), in_=w_words[e].rearrange("s p b -> p s b").bitcast(I32)
+            )
+            nc.sync.dma_start(out=gates[e][:], in_=gate[:, e * C : (e + 1) * C])
+
+        nc.sync.dma_start(offsets[:], offs)
+        load_tokens(0)
+        load_wa(0, 0)
+        for q in range(QUADS):
+            nc.sync.dma_start(
+                out=token_scales[32 * q : 32 * q + ROWS * PASSES, :].bitcast(I32),
+                in_=x_scales[:, ROWS * q : ROWS * (q + 1), :].bitcast(I32),
+            )
+        load_tokens(1)
+        load_tokens(2)
+        load_wa(0, 1)
+        load_wa(0, 2)
+        load_rest(0)
+
+        def slot_list(first, count):
+            return offsets[:, first // 16 : (first + count) // 16]
+
+        def gather_words(e, s):
+            nc.vector.tensor_copy(
+                out=slot_words[s][:, e * C : (e + 1) * C],
+                in_=token_words[s][:].bitcast(U32).indirect(slot_list(e * C, C)),
+            )
+
+        def gather_scales(first, count):
+            nc.vector.tensor_copy(
+                out=slot_scales[:, first : first + count], in_=token_scales[:].indirect(slot_list(first, count))
+            )
+
+        def round_wa(e, s):
+            src = wa_raw[e][s][:].rearrange("p j (m t) -> p m j t", t=PACK)
+            dst = wa_bf[e][s][:].rearrange("p (t m j) -> p m j t", t=PACK, j=PACK)
+            share = VECTOR_SHARE[e][s]
+            if (e, s) == (E - 1, PASSES - 1):
+                for m0 in (0, P // 2):
+                    cut = m0 + share // 2
+                    nc.vector.tensor_copy(out=dst[:, m0:cut], in_=src[:, m0:cut])
+                    nc.scalar.copy(out=dst[:, cut : m0 + P // 2], in_=src[:, cut : m0 + P // 2])
+            else:
+                if share > 0:
+                    nc.vector.tensor_copy(out=dst[:, :share], in_=src[:, :share])
+                nc.scalar.copy(out=dst[:, share:], in_=src[:, share:])
+            nc.vector.quantize_mx(out=wa_codes[e][s][:].bitcast(FP8X4), scales=wa_scales[e][s][:], in_=wa_bf[e][s][:])
+
+        def round_wb(e):
+            nc.vector.tensor_copy(
+                out=wb_bf[e][:].rearrange("p (c i j) -> p c j i", i=4, j=PACK),
+                in_=wb_raw[e][:].rearrange("p j (c i) -> p c j i", i=4),
+            )
+            nc.vector.quantize_mx(out=wb_codes[e][:].bitcast(FP8X4), scales=wb_scales[e][:], in_=wb_bf[e][:])
+
+        gather_words(0, 0)
+        gather_scales(0, C)
+        gather_scales(C, T - C)
+        for s in range(1, PASSES):
+            nc.sync.dma_start(
+                out=moved_scales[s - 1][0:MOVED_ROWS, :].bitcast(I32),
+                in_=slot_scales[ROWS * s : ROWS * s + MOVED_ROWS, :].bitcast(I32),
+            )
+        planes_at_zero = [slot_scales] + moved_scales
+        for s in range(1, PASSES):
+            gather_words(0, s)
+
+        for e in range(E):
+            for s in range(PASSES):
+                round_wa(e, s)
+                if e + 1 < E:
+                    load_wa(e + 1, s)
+            if e + 1 < E:
+                load_rest(e + 1)
+            round_wb(e)
+            if e == 0:
+                for later in range(1, E):
+                    for s in range(PASSES):
+                        gather_words(later, s)
+
+            sums = [sb("sums%d_%d" % (e, nt), [P, C], F32) for nt in range(N_TILES)]
+            for u in range(UNITS):
+                first = e * C + u * UNIT
+                slots = slice(first, first + UNIT)
+                local = slice(u * UNIT, (u + 1) * UNIT)
+
+                h_bank = h_psum.tile([P, PACK, UNIT], F32, name="h_bank")
+                for t in range(PACK):
+                    cols = slice(t * P, (t + 1) * P)
+                    for s in range(PASSES):
+                        nc.tensor.matmul_mx(
+                            out=h_bank[:, t, :],
+                            lhsT=wa_codes[e][s][:, cols].bitcast(FP8X4),
+                            lhsT_scale=wa_scales[e][s][:, cols],
+                            rhs=slot_words[s][:, slots].bitcast(FP8X4),
+                            rhs_scale=slot_scales[ROWS * s :, slots],
+                            start=(s == 0),
+                            stop=(s == PASSES - 1),
+                        )
+                y_banks = [y_psum.tile([P, UNIT], F32, name="y_bank%d" % nt) for nt in range(N_TILES)]
+                for nt in range(N_TILES):
+                    for s in range(PASSES):
+                        nc.tensor.matmul_mx(
+                            out=y_banks[nt][:],
+                            lhsT=frozen_words[e][:, s, 2 * P * nt : 2 * P * (nt + 1)].bitcast(FP4X4),
+                            lhsT_scale=frozen_scales[:, e * PASSES + s, P * nt : P * (nt + 1)],
+                            rhs=slot_words[s][:, slots].bitcast(FP8X4),
+                            rhs_scale=planes_at_zero[s][:, slots],
+                            start=(s == 0),
+                            stop=False,
+                        )
+
+                h_bf = sb("h_bf%d_%d" % (e, u), [P, PACK * UNIT], BF16)
+                h_codes = sb("h_codes%d_%d" % (e, u), [P, UNIT], U32)
+                h_scales = sb("h_scales%d_%d" % (e, u), [P, UNIT], U8)
+                nc.scalar.activation(
+                    out=h_bf[:].rearrange("p (u t) -> p u t", t=PACK),
+                    in_=h_bank[:].rearrange("p t u -> p u t"),
+                    func=GELU,
+                )
+                nc.vector.quantize_mx(out=h_codes[:].bitcast(FP8X4), scales=h_scales[:], in_=h_bf[:])
+
+                for nt in range(N_TILES):
+                    cols = slice(nt * P, (nt + 1) * P)
+                    nc.tensor.matmul_mx(
+                        out=y_banks[nt][:],
+                        lhsT=wb_codes[e][:, cols].bitcast(FP8X4),
+                        lhsT_scale=wb_scales[e][:, cols],
+                        rhs=h_codes[:].bitcast(FP8X4),
+                        rhs_scale=h_scales[:],
+                        start=False,
+                        stop=True,
+                    )
+                    nc.scalar.copy(out=sums[nt][:, local], in_=y_banks[nt][:])
+                    if e == E - 1:
+                        nc.vector.tensor_tensor(
+                            results[nt][:].indirect(slot_list(first, UNIT)), sums[nt][:, local], gates[e][:, local], MULT
+                        )
+            if e < E - 1:
+                for nt in range(N_TILES):
+                    nc.vector.tensor_tensor(
+                        results[nt][:].indirect(slot_list(e * C, C)), sums[nt][:], gates[e][:], MULT
+                    )
+
+        for nt in range(N_TILES):
+            nc.sync.dma_start(out=out[nt * P : (nt + 1) * P, :], in_=results[nt][:])

@@ -27,7 +27,10 @@ QUADS = 4
 ROWS = 4
 MOVED_ROWS = 112
 
-VECTOR_SHARE = [[0, 0, 48], [0, 0, 48], [0, 0, 84]]
+VECTOR_SHARE = [[0,32,64],[0,0,48],[0,0,64]]
+LAST_CUT = 64
+WB_ON_VECTOR = [1,1,0]
+LOAD_ORDER = ["xw0","wa00","xs","wa01","xw1","ws","wa02","xw2","w0","wa10","wb0","gate0","wa11","wa12","w1","wa20","wb1","gate1","wa21","wa22","w2","wb2","gate2"]
 
 
 def tile_moe_elr_gelu_kernel(
@@ -36,9 +39,8 @@ def tile_moe_elr_gelu_kernel(
     nc = tc.nc
     with ExitStack() as ctx:
         keep = ctx.enter_context(tc.tile_pool(name="keep", bufs=1))
-        stream = ctx.enter_context(tc.tile_pool(name="stream", bufs=3))
-        h_psum = ctx.enter_context(tc.psum_pool(name="h_psum", bufs=4))
-        y_psum = ctx.enter_context(tc.psum_pool(name="y_psum", bufs=2))
+        h_psum = ctx.enter_context(tc.psum_pool(name="h_psum", bufs=2))
+        y_psum = ctx.enter_context(tc.psum_pool(name="y_psum", bufs=3))
 
         def sb(name, shape, dtype):
             return keep.tile(shape, dtype, name=name, align_bytes=64)
@@ -51,10 +53,7 @@ def tile_moe_elr_gelu_kernel(
         moved_scales = [sb("moved_scales%d" % s, [P, T], U8) for s in range(1, PASSES)]
         frozen_words = [sb("frozen_words%d" % e, [P, PASSES, 2 * N], U8) for e in range(E)]
         frozen_scales = sb("frozen_scales", [P, E * PASSES, N], U8)
-        wa_raw = [
-            [stream.tile([P, PACK, H], F32, name="wa_raw%d_%d" % (e, s), tag="wa_raw") for s in range(PASSES)]
-            for e in range(E)
-        ]
+        wa_raw = [[sb("wa_raw%d_%d" % (e, s), [P, PACK, H], F32) for s in range(PASSES)] for e in range(E)]
         wa_bf = [[sb("wa_bf%d_%d" % (e, s), [P, PACK * H], BF16) for s in range(PASSES)] for e in range(E)]
         wa_codes = [[sb("wa_codes%d_%d" % (e, s), [P, H], U32) for s in range(PASSES)] for e in range(E)]
         wa_scales = [[sb("wa_scales%d_%d" % (e, s), [P, H], U8) for s in range(PASSES)] for e in range(E)]
@@ -73,11 +72,6 @@ def tile_moe_elr_gelu_kernel(
             nc.vector.memset(moved[:].bitcast(I32), 0)
 
         nc.scalar.activation(out=warm[:, 1:2], in_=warm[:, 0:1], func=GELU)
-        for q in range(QUADS):
-            nc.gpsimd.dma_start(
-                out=frozen_scales[32 * q : 32 * q + ROWS, :, :].bitcast(I32),
-                in_=w_scales[:, :, ROWS * q : ROWS * (q + 1), :].rearrange("e s r n -> r (e s) n").bitcast(I32),
-            )
 
         def load_tokens(s):
             nc.sync.dma_start(out=token_words[s][:], in_=x_words[s].rearrange("p t d -> p (t d)").bitcast(I32))
@@ -85,31 +79,43 @@ def tile_moe_elr_gelu_kernel(
         def load_wa(e, s):
             rows = wa[e, s * K_PASS : (s + 1) * K_PASS, :].rearrange("(p j) i -> p j i", j=PACK)
             if (e, s) == (E - 1, PASSES - 1):
-                for c0 in (0, H // 2):
-                    nc.sync.dma_start(out=wa_raw[e][s][:, :, c0 : c0 + H // 2], in_=rows[:, :, c0 : c0 + H // 2])
+                for c0, c1 in ((0, PACK * LAST_CUT), (PACK * LAST_CUT, H)):
+                    nc.sync.dma_start(out=wa_raw[e][s][:, :, c0:c1], in_=rows[:, :, c0:c1])
             else:
                 nc.sync.dma_start(out=wa_raw[e][s][:], in_=rows)
 
-        def load_rest(e):
-            nc.sync.dma_start(out=wb_raw[e][:], in_=wb[e].rearrange("(p j) n -> p j n", j=PACK))
-            nc.sync.dma_start(
-                out=frozen_words[e][:].bitcast(I32), in_=w_words[e].rearrange("s p b -> p s b").bitcast(I32)
-            )
-            nc.sync.dma_start(out=gates[e][:], in_=gate[:, e * C : (e + 1) * C])
+        def load(name):
+            if name == "xs":
+                for q in range(QUADS):
+                    nc.sync.dma_start(
+                        out=token_scales[32 * q : 32 * q + ROWS * PASSES, :].bitcast(I32),
+                        in_=x_scales[:, ROWS * q : ROWS * (q + 1), :].bitcast(I32),
+                    )
+            elif name == "ws":
+                for q in range(QUADS):
+                    rows = w_scales[:, :, ROWS * q : ROWS * (q + 1), :].rearrange("e s r n -> r (e s) n")
+                    nc.sync.dma_start(
+                        out=frozen_scales[32 * q : 32 * q + ROWS, :, :].bitcast(I32), in_=rows.bitcast(I32)
+                    )
+            elif name.startswith("xw"):
+                load_tokens(int(name[2]))
+            elif name.startswith("wa"):
+                load_wa(int(name[2]), int(name[3]))
+            elif name.startswith("wb"):
+                e = int(name[2])
+                nc.sync.dma_start(out=wb_raw[e][:], in_=wb[e].rearrange("(p j) n -> p j n", j=PACK))
+            elif name.startswith("gate"):
+                e = int(name[4])
+                nc.sync.dma_start(out=gates[e][:], in_=gate[:, e * C : (e + 1) * C])
+            else:
+                e = int(name[1])
+                nc.sync.dma_start(
+                    out=frozen_words[e][:].bitcast(I32), in_=w_words[e].rearrange("s p b -> p s b").bitcast(I32)
+                )
 
         nc.sync.dma_start(offsets[:], offs)
-        load_tokens(0)
-        load_wa(0, 0)
-        for q in range(QUADS):
-            nc.sync.dma_start(
-                out=token_scales[32 * q : 32 * q + ROWS * PASSES, :].bitcast(I32),
-                in_=x_scales[:, ROWS * q : ROWS * (q + 1), :].bitcast(I32),
-            )
-        load_tokens(1)
-        load_tokens(2)
-        load_wa(0, 1)
-        load_wa(0, 2)
-        load_rest(0)
+        for name in LOAD_ORDER:
+            load(name)
 
         def slot_list(first, count):
             return offsets[:, first // 16 : (first + count) // 16]
@@ -130,10 +136,10 @@ def tile_moe_elr_gelu_kernel(
             dst = wa_bf[e][s][:].rearrange("p (t m j) -> p m j t", t=PACK, j=PACK)
             share = VECTOR_SHARE[e][s]
             if (e, s) == (E - 1, PASSES - 1):
-                for m0 in (0, P // 2):
-                    cut = m0 + share // 2
+                for m0, m1 in ((0, LAST_CUT), (LAST_CUT, P)):
+                    cut = m0 + 2 * ((m1 - m0) * share // (2 * P))
                     nc.vector.tensor_copy(out=dst[:, m0:cut], in_=src[:, m0:cut])
-                    nc.scalar.copy(out=dst[:, cut : m0 + P // 2], in_=src[:, cut : m0 + P // 2])
+                    nc.scalar.copy(out=dst[:, cut:m1], in_=src[:, cut:m1])
             else:
                 if share > 0:
                     nc.vector.tensor_copy(out=dst[:, :share], in_=src[:, :share])
@@ -141,17 +147,18 @@ def tile_moe_elr_gelu_kernel(
             nc.vector.quantize_mx(out=wa_codes[e][s][:].bitcast(FP8X4), scales=wa_scales[e][s][:], in_=wa_bf[e][s][:])
 
         def round_wb(e):
-            nc.vector.tensor_copy(
+            copy = nc.vector.tensor_copy if WB_ON_VECTOR[e] else nc.scalar.copy
+            copy(
                 out=wb_bf[e][:].rearrange("p (c i j) -> p c j i", i=4, j=PACK),
                 in_=wb_raw[e][:].rearrange("p j (c i) -> p c j i", i=4),
             )
             nc.vector.quantize_mx(out=wb_codes[e][:].bitcast(FP8X4), scales=wb_scales[e][:], in_=wb_bf[e][:])
 
-        gather_words(0, 0)
         gather_scales(0, C)
         gather_scales(C, T - C)
+        gather_words(0, 0)
         for s in range(1, PASSES):
-            nc.sync.dma_start(
+            nc.gpsimd.dma_start(
                 out=moved_scales[s - 1][0:MOVED_ROWS, :].bitcast(I32),
                 in_=slot_scales[ROWS * s : ROWS * s + MOVED_ROWS, :].bitcast(I32),
             )
@@ -162,10 +169,6 @@ def tile_moe_elr_gelu_kernel(
         for e in range(E):
             for s in range(PASSES):
                 round_wa(e, s)
-                if e + 1 < E:
-                    load_wa(e + 1, s)
-            if e + 1 < E:
-                load_rest(e + 1)
             round_wb(e)
             if e == 0:
                 for later in range(1, E):
@@ -225,16 +228,15 @@ def tile_moe_elr_gelu_kernel(
                         start=False,
                         stop=True,
                     )
-                    nc.scalar.copy(out=sums[nt][:, local], in_=y_banks[nt][:])
-                    if e == E - 1:
-                        nc.vector.tensor_tensor(
-                            results[nt][:].indirect(slot_list(first, UNIT)), sums[nt][:, local], gates[e][:, local], MULT
+                    nc.vector.tensor_tensor(sums[nt][:, local], y_banks[nt][:], gates[e][:, local], MULT)
+                if e == E - 1:
+                    for nt in range(N_TILES):
+                        nc.vector.tensor_copy(
+                            out=results[nt][:].indirect(slot_list(first, UNIT)), in_=sums[nt][:, local]
                         )
             if e < E - 1:
                 for nt in range(N_TILES):
-                    nc.vector.tensor_tensor(
-                        results[nt][:].indirect(slot_list(e * C, C)), sums[nt][:], gates[e][:], MULT
-                    )
+                    nc.vector.tensor_copy(out=results[nt][:].indirect(slot_list(e * C, C)), in_=sums[nt][:])
 
         for nt in range(N_TILES):
             nc.sync.dma_start(out=out[nt * P : (nt + 1) * P, :], in_=results[nt][:])

@@ -25,12 +25,62 @@ UNITS = C // UNIT
 N_TILES = N // P
 QUADS = 4
 ROWS = 4
+GROUPS = H // 16
 MOVED_ROWS = 112
 
-VECTOR_SHARE = [[0,32,64],[0,0,48],[0,0,64]]
-LAST_CUT = 64
+VECTOR_SHARE = [[20,0,0],[0,16,0],[0,16,0]]
+LAST_CUT = 32
 WB_ON_VECTOR = [1,1,0]
-LOAD_ORDER = ["xw0","wa00","xs","wa01","xw1","ws","wa02","xw2","w0","wa10","wb0","gate0","wa11","wa12","w1","wa20","wb1","gate1","wa21","wa22","w2","wb2","gate2"]
+FINE = [0,1,0]
+HOST = {"HB11":"R21","HB10":"R21","Q10":"HQ01","B10":"B01","X02":"R01","HQ20":"Q21","Q12":"S01"}
+ORDER = ["ms_ts","ms_w","ms_ws","ms_m1","ms_m2","warm","wa00","offs","xw0","xs0","xs1","xs2","xs3","wa02","xw1","wa01","ws0","ws1","ws2","ws3","cv00","c00","c02","g10","gs1","g00","wa10","xw2","wb0_0","wb0_1","wb0_2","wb0_3","wa11","q00","q02","g11","g01","gs0","mv1","mv2","h00_0","w0","wb1_0","wb1_1","wb1_2","wb1_3","wa12","gate0","c01","q01","c10","h00_1","g02","h00_2","h00_3","h00_4","h00_5","h00_6","h00_7","h00_8","h00_9","h00_10","h00_11","cb0","qb0","h01_0","h01_1","h01_2","h01_3","h01_4","h01_5","h01_6","h01_7","h01_8","h01_9","h01_10","h01_11","f000_0","f000_1","f000_2","f001_0","f001_1","f001_2","f010_0","f010_1","f010_2","f011_0","f011_1","f011_2","g12","ge00","hq00","b000","b001","ge01","hq01","b010","b011","q10","h10_0","h11_0","cv11","c11","m001","m010","m011","sc011","cb1","q11","h10_1","h11_1","qb1","c12","q12","h10_2","h10_3","h10_4","h10_5","h10_6","h10_7","h10_8","h10_9","h10_10","h10_11","h11_2","h11_3","h11_4","h11_5","h11_6","h11_7","h11_8","h11_9","h11_10","h11_11","m000","sc010","wa20","c20","q20","wa22a","c22a","w1","f110_0","f110_1","f110_2","f111_0","f111_1","f111_2","wa21","cv21","c21","ge11","q21","ge10","hq11","wb2_0","wb2_1","wb2_2","wb2_3","cb2","w2","gate2","gate1","q22","qb2","hq10","b110","m110","sc110","b111","m111","sc111","h20_0","h20_1","h20_2","h20_3","h20_4","h20_5","h20_6","h20_7","h20_8","h20_9","h20_10","h20_11","ge20","h21_0","h21_1","h21_2","h21_3","h21_4","h21_5","h21_6","h21_7","h21_8","h21_9","h21_10","hq20","h21_11","ge21","hq21","f100_0","f100_1","f100_2","b100","m100","sc100","f101_0","f101_1","f101_2","b101","m101","sc101","f200_0","f200_1","f200_2","b200","m200","f201_0","f201_1","f201_2","b201","m201","f210_0","f210_1","f210_2","b210","m210","sc210","f211_0","f211_1","f211_2","b211","m211","sc211","st0","st1"]
+
+SHAPES = {
+    "TS": ([P, T], U8, 1),
+    "TW": ([P, T], I32, 4),
+    "RB": ([P, PACK, N], F32, 4),
+    "R": ([P, PACK, H], F32, 4),
+    "W": ([P, PASSES, 2 * N], U8, 1),
+    "G": ([P, C], F32, 4),
+    "X": ([P, C], U32, 4),
+    "BB": ([P, PACK * N], BF16, 2),
+    "B": ([P, PACK * H], BF16, 2),
+    "QB": ([P, N], U32, 4),
+    "Q": ([P, H], U32, 4),
+    "HB": ([P, PACK * UNIT], BF16, 2),
+    "HQ": ([P, UNIT], U32, 4),
+}
+
+
+def shape_of(name):
+    kind = "".join([ch for ch in name if ch not in "0123456789"])
+    if kind == "X" and name[1] == "1":
+        return ([P, 2 * C], U32, 4)
+    if kind == "S":
+        return ([P, UNIT if len(name) == 4 else C], F32, 4)
+    return SHAPES[kind]
+
+
+def size_of(name):
+    shape, dtype, width = shape_of(name)
+    for n in shape[1:]:
+        width = width * n
+    return width
+
+
+def guests_of(name):
+    return sorted([g for g in HOST if HOST[g] == name], key=extent)
+
+
+def extent(name):
+    return max(size_of(name), sum([extent(g) for g in guests_of(name)]))
+
+
+def lay_out(name, offset, place):
+    place[name] = offset
+    for g in guests_of(name):
+        lay_out(g, offset, place)
+        offset = offset + extent(g)
 
 
 def tile_moe_elr_gelu_kernel(
@@ -39,204 +89,228 @@ def tile_moe_elr_gelu_kernel(
     nc = tc.nc
     with ExitStack() as ctx:
         keep = ctx.enter_context(tc.tile_pool(name="keep", bufs=1))
-        h_psum = ctx.enter_context(tc.psum_pool(name="h_psum", bufs=2))
-        y_psum = ctx.enter_context(tc.psum_pool(name="y_psum", bufs=3))
+        shared = ctx.enter_context(tc.tile_pool(name="shared", bufs=1))
+        h_psum = ctx.enter_context(tc.psum_pool(name="h_psum", bufs=4))
+        y_psum = ctx.enter_context(tc.psum_pool(name="y_psum", bufs=2))
 
-        def sb(name, shape, dtype):
-            return keep.tile(shape, dtype, name=name, align_bytes=64)
+        place = {}
+        top = 0
+        for root in sorted(set(HOST.values()) - set(HOST)):
+            lay_out(root, top, place)
+            top = top + extent(root)
+        tiles = {}
+
+        def sb(name):
+            if name not in tiles:
+                shape, dtype, width = shape_of(name)
+                if name in place:
+                    tiles[name] = shared.tile(shape, dtype, name=name, align_bytes=64, offset=place[name])
+                else:
+                    tiles[name] = keep.tile(shape, dtype, name=name, align_bytes=64)
+            return tiles[name]
+
+        def own(name, shape, dtype):
+            if name not in tiles:
+                tiles[name] = keep.tile(shape, dtype, name=name, align_bytes=64)
+            return tiles[name]
 
         offsets = keep.tile([P, T // 16], U16, name="offsets")
-        token_words = [sb("token_words%d" % s, [P, T], I32) for s in range(PASSES)]
-        token_scales = sb("token_scales", [P, T], U8)
-        slot_words = [sb("slot_words%d" % s, [P, T], U32) for s in range(PASSES)]
-        slot_scales = sb("slot_scales", [P, T], U8)
-        moved_scales = [sb("moved_scales%d" % s, [P, T], U8) for s in range(1, PASSES)]
-        frozen_words = [sb("frozen_words%d" % e, [P, PASSES, 2 * N], U8) for e in range(E)]
-        frozen_scales = sb("frozen_scales", [P, E * PASSES, N], U8)
-        wa_raw = [[sb("wa_raw%d_%d" % (e, s), [P, PACK, H], F32) for s in range(PASSES)] for e in range(E)]
-        wa_bf = [[sb("wa_bf%d_%d" % (e, s), [P, PACK * H], BF16) for s in range(PASSES)] for e in range(E)]
-        wa_codes = [[sb("wa_codes%d_%d" % (e, s), [P, H], U32) for s in range(PASSES)] for e in range(E)]
-        wa_scales = [[sb("wa_scales%d_%d" % (e, s), [P, H], U8) for s in range(PASSES)] for e in range(E)]
-        wb_raw = [sb("wb_raw%d" % e, [P, PACK, N], F32) for e in range(E)]
-        wb_bf = [sb("wb_bf%d" % e, [P, PACK * N], BF16) for e in range(E)]
-        wb_codes = [sb("wb_codes%d" % e, [P, N], U32) for e in range(E)]
-        wb_scales = [sb("wb_scales%d" % e, [P, N], U8) for e in range(E)]
-        gates = [sb("gates%d" % e, [P, C], F32) for e in range(E)]
-        results = [sb("results%d" % nt, [P, T], F32) for nt in range(N_TILES)]
-        warm = sb("warm", [P, 2], F32)
-
-        nc.vector.memset(token_scales[:].bitcast(I32), 0)
-        nc.vector.memset(warm[:, 0:1], 0.0)
-        nc.vector.memset(frozen_scales[:].rearrange("p g n -> p (g n)").bitcast(I32), 0)
-        for moved in moved_scales:
-            nc.vector.memset(moved[:].bitcast(I32), 0)
-
-        nc.scalar.activation(out=warm[:, 1:2], in_=warm[:, 0:1], func=GELU)
-
-        def load_tokens(s):
-            nc.sync.dma_start(out=token_words[s][:], in_=x_words[s].rearrange("p t d -> p (t d)").bitcast(I32))
-
-        def load_wa(e, s):
-            rows = wa[e, s * K_PASS : (s + 1) * K_PASS, :].rearrange("(p j) i -> p j i", j=PACK)
-            if (e, s) == (E - 1, PASSES - 1):
-                for c0, c1 in ((0, PACK * LAST_CUT), (PACK * LAST_CUT, H)):
-                    nc.sync.dma_start(out=wa_raw[e][s][:, :, c0:c1], in_=rows[:, :, c0:c1])
-            else:
-                nc.sync.dma_start(out=wa_raw[e][s][:], in_=rows)
-
-        def load(name):
-            if name == "xs":
-                for q in range(QUADS):
-                    nc.sync.dma_start(
-                        out=token_scales[32 * q : 32 * q + ROWS * PASSES, :].bitcast(I32),
-                        in_=x_scales[:, ROWS * q : ROWS * (q + 1), :].bitcast(I32),
-                    )
-            elif name == "ws":
-                for q in range(QUADS):
-                    rows = w_scales[:, :, ROWS * q : ROWS * (q + 1), :].rearrange("e s r n -> r (e s) n")
-                    nc.sync.dma_start(
-                        out=frozen_scales[32 * q : 32 * q + ROWS, :, :].bitcast(I32), in_=rows.bitcast(I32)
-                    )
-            elif name.startswith("xw"):
-                load_tokens(int(name[2]))
-            elif name.startswith("wa"):
-                load_wa(int(name[2]), int(name[3]))
-            elif name.startswith("wb"):
-                e = int(name[2])
-                nc.sync.dma_start(out=wb_raw[e][:], in_=wb[e].rearrange("(p j) n -> p j n", j=PACK))
-            elif name.startswith("gate"):
-                e = int(name[4])
-                nc.sync.dma_start(out=gates[e][:], in_=gate[:, e * C : (e + 1) * C])
-            else:
-                e = int(name[1])
-                nc.sync.dma_start(
-                    out=frozen_words[e][:].bitcast(I32), in_=w_words[e].rearrange("s p b -> p s b").bitcast(I32)
-                )
-
-        nc.sync.dma_start(offsets[:], offs)
-        for name in LOAD_ORDER:
-            load(name)
+        slot_scales = own("slot_scales", [P, T], U8)
+        planes_at_zero = [slot_scales] + [own("moved%d" % s, [P, T], U8) for s in range(1, PASSES)]
+        frozen_scales = own("frozen_scales", [P, E * PASSES, N], U8)
+        results = [own("results%d" % nt, [P, T], F32) for nt in range(N_TILES)]
+        warm = own("warm", [P, 2], F32)
 
         def slot_list(first, count):
             return offsets[:, first // 16 : (first + count) // 16]
 
-        def gather_words(e, s):
-            nc.vector.tensor_copy(
-                out=slot_words[s][:, e * C : (e + 1) * C],
-                in_=token_words[s][:].bitcast(U32).indirect(slot_list(e * C, C)),
-            )
+        def slot_words(e, s, u):
+            first = max(e - 1, 0) * C + u * UNIT
+            return sb("X%d%d" % (min(e, 1), s))[:, first : first + UNIT]
 
-        def gather_scales(first, count):
-            nc.vector.tensor_copy(
-                out=slot_scales[:, first : first + count], in_=token_scales[:].indirect(slot_list(first, count))
-            )
+        def piece(name):
+            if name[-1] == "a":
+                return 0, LAST_CUT
+            if name[-1] == "b":
+                return LAST_CUT, GROUPS
+            return 0, GROUPS
 
-        def round_wa(e, s):
-            src = wa_raw[e][s][:].rearrange("p j (m t) -> p m j t", t=PACK)
-            dst = wa_bf[e][s][:].rearrange("p (t m j) -> p m j t", t=PACK, j=PACK)
-            share = VECTOR_SHARE[e][s]
-            if (e, s) == (E - 1, PASSES - 1):
-                for m0, m1 in ((0, LAST_CUT), (LAST_CUT, P)):
-                    cut = m0 + 2 * ((m1 - m0) * share // (2 * P))
-                    nc.vector.tensor_copy(out=dst[:, m0:cut], in_=src[:, m0:cut])
-                    nc.scalar.copy(out=dst[:, cut:m1], in_=src[:, cut:m1])
-            else:
-                if share > 0:
-                    nc.vector.tensor_copy(out=dst[:, :share], in_=src[:, :share])
-                nc.scalar.copy(out=dst[:, share:], in_=src[:, share:])
-            nc.vector.quantize_mx(out=wa_codes[e][s][:].bitcast(FP8X4), scales=wa_scales[e][s][:], in_=wa_bf[e][s][:])
+        def bank(name, pool, shape, tag):
+            if name not in tiles:
+                tiles[name] = pool.tile(shape, F32, name=name, tag=tag)
+            return tiles[name]
 
-        def round_wb(e):
-            copy = nc.vector.tensor_copy if WB_ON_VECTOR[e] else nc.scalar.copy
-            copy(
-                out=wb_bf[e][:].rearrange("p (c i j) -> p c j i", i=4, j=PACK),
-                in_=wb_raw[e][:].rearrange("p j (c i) -> p c j i", i=4),
-            )
-            nc.vector.quantize_mx(out=wb_codes[e][:].bitcast(FP8X4), scales=wb_scales[e][:], in_=wb_bf[e][:])
-
-        gather_scales(0, C)
-        gather_scales(C, T - C)
-        gather_words(0, 0)
-        for s in range(1, PASSES):
-            nc.gpsimd.dma_start(
-                out=moved_scales[s - 1][0:MOVED_ROWS, :].bitcast(I32),
-                in_=slot_scales[ROWS * s : ROWS * s + MOVED_ROWS, :].bitcast(I32),
-            )
-        planes_at_zero = [slot_scales] + moved_scales
-        for s in range(1, PASSES):
-            gather_words(0, s)
-
-        for e in range(E):
-            for s in range(PASSES):
-                round_wa(e, s)
-            round_wb(e)
-            if e == 0:
-                for later in range(1, E):
-                    for s in range(PASSES):
-                        gather_words(later, s)
-
-            sums = [sb("sums%d_%d" % (e, nt), [P, C], F32) for nt in range(N_TILES)]
-            for u in range(UNITS):
+        def step(name):
+            digits = [int(ch) for ch in name if ch in "0123456789"]
+            kind = "".join([ch for ch in name.split("_")[0] if ch not in "0123456789"])
+            if name == "ms_ts":
+                nc.vector.memset(sb("TS")[:].bitcast(I32), 0)
+            elif name == "ms_w":
+                nc.vector.memset(warm[:, 0:1], 0.0)
+            elif name == "ms_ws":
+                nc.vector.memset(frozen_scales[:].rearrange("p g n -> p (g n)").bitcast(I32), 0)
+            elif kind == "ms":
+                nc.vector.memset(planes_at_zero[digits[0]][:].bitcast(I32), 0)
+            elif name == "warm":
+                nc.scalar.activation(out=warm[:, 1:2], in_=warm[:, 0:1], func=GELU)
+            elif name == "offs":
+                nc.sync.dma_start(offsets[:], offs)
+            elif kind == "xs":
+                q = digits[0]
+                nc.sync.dma_start(
+                    out=sb("TS")[32 * q : 32 * q + ROWS * PASSES, :].bitcast(I32),
+                    in_=x_scales[:, ROWS * q : ROWS * (q + 1), :].bitcast(I32),
+                )
+            elif kind == "ws":
+                r = digits[0]
+                rows = w_scales.rearrange("e s (q r) n -> r q (e s) n", r=ROWS)[r]
+                nc.sync.dma_start(out=frozen_scales[r:P:32, :, :].bitcast(I32), in_=rows.bitcast(I32))
+            elif kind == "xw":
+                s = digits[0]
+                nc.sync.dma_start(out=sb("TW%d" % s)[:], in_=x_words[s].rearrange("p t d -> p (t d)").bitcast(I32))
+            elif kind in ("wa", "waa", "wab"):
+                e, s = digits
+                q0, q1 = piece(name[2:])
+                rows = wa[e, s * K_PASS : (s + 1) * K_PASS, :].rearrange("(p j) i -> p j i", j=PACK)
+                nc.sync.dma_start(
+                    out=sb("R%d%d" % (e, s))[:, :, 16 * q0 : 16 * q1], in_=rows[:, :, 16 * q0 : 16 * q1]
+                )
+            elif kind == "wb":
+                e, t = digits
+                rows = wb[e].rearrange("(q t r) n -> t q r n", t=PACK, r=4)
+                nc.sync.dma_start(out=sb("RB%d" % e)[:, t, :], in_=rows[t])
+            elif kind == "w":
+                e = digits[0]
+                nc.sync.dma_start(
+                    out=sb("W%d" % e)[:].bitcast(I32), in_=w_words[e].rearrange("s p b -> p s b").bitcast(I32)
+                )
+            elif kind == "gate":
+                e = digits[0]
+                nc.sync.dma_start(out=sb("G%d" % e)[:], in_=gate[:, e * C : (e + 1) * C])
+            elif kind == "gs":
+                first, count = (0, C) if digits[0] == 0 else (C, T - C)
+                nc.vector.tensor_copy(
+                    out=slot_scales[:, first : first + count], in_=sb("TS")[:].indirect(slot_list(first, count))
+                )
+            elif kind == "mv":
+                s = digits[0]
+                nc.sync.dma_start(
+                    out=planes_at_zero[s][0:MOVED_ROWS, :].bitcast(I32),
+                    in_=slot_scales[ROWS * s : ROWS * s + MOVED_ROWS, :].bitcast(I32),
+                )
+            elif kind == "g":
+                e, s = digits
+                nc.vector.tensor_copy(
+                    out=sb("X%d%d" % (e, s))[:],
+                    in_=sb("TW%d" % s)[:].bitcast(U32).indirect(slot_list(e * C, C if e == 0 else 2 * C)),
+                )
+            elif kind in ("c", "ca", "cv", "cva", "cvb") or name == "c22b":
+                e, s = digits
+                q0, q1 = piece(name)
+                cut = q0 + 2 * ((q1 - q0) * VECTOR_SHARE[e][s] // (2 * GROUPS))
+                src = sb("R%d%d" % (e, s))[:].rearrange("p j (q t r) -> p q t j r", t=PACK, r=4)
+                dst = sb("B%d%d" % (e, s))[:].rearrange("p (t q r j) -> p q t j r", t=PACK, r=4, j=PACK)
+                if kind.startswith("cv"):
+                    nc.vector.tensor_copy(out=dst[:, q0:cut], in_=src[:, q0:cut])
+                else:
+                    nc.scalar.copy(out=dst[:, cut:q1], in_=src[:, cut:q1])
+            elif kind == "q":
+                e, s = digits
+                nc.vector.quantize_mx(
+                    out=sb("Q%d%d" % (e, s))[:].bitcast(FP8X4),
+                    scales=own("qs%d%d" % (e, s), [P, H], U8)[:],
+                    in_=sb("B%d%d" % (e, s))[:],
+                )
+            elif kind == "cb":
+                e = digits[0]
+                copy = nc.vector.tensor_copy if WB_ON_VECTOR[e] else nc.scalar.copy
+                copy(
+                    out=sb("BB%d" % e)[:].rearrange("p (c i j) -> p c j i", i=4, j=PACK),
+                    in_=sb("RB%d" % e)[:].rearrange("p j (c i) -> p c j i", i=4),
+                )
+            elif kind == "qb":
+                e = digits[0]
+                nc.vector.quantize_mx(
+                    out=sb("QB%d" % e)[:].bitcast(FP8X4),
+                    scales=own("qbs%d" % e, [P, N], U8)[:],
+                    in_=sb("BB%d" % e)[:],
+                )
+            elif kind == "h":
+                e, u = digits[:2]
+                t, s = divmod(int(name.split("_")[1]), PASSES)
+                cols = slice(t * P, (t + 1) * P)
                 first = e * C + u * UNIT
-                slots = slice(first, first + UNIT)
-                local = slice(u * UNIT, (u + 1) * UNIT)
-
-                h_bank = h_psum.tile([P, PACK, UNIT], F32, name="h_bank")
-                for t in range(PACK):
-                    cols = slice(t * P, (t + 1) * P)
-                    for s in range(PASSES):
-                        nc.tensor.matmul_mx(
-                            out=h_bank[:, t, :],
-                            lhsT=wa_codes[e][s][:, cols].bitcast(FP8X4),
-                            lhsT_scale=wa_scales[e][s][:, cols],
-                            rhs=slot_words[s][:, slots].bitcast(FP8X4),
-                            rhs_scale=slot_scales[ROWS * s :, slots],
-                            start=(s == 0),
-                            stop=(s == PASSES - 1),
-                        )
-                y_banks = [y_psum.tile([P, UNIT], F32, name="y_bank%d" % nt) for nt in range(N_TILES)]
-                for nt in range(N_TILES):
-                    for s in range(PASSES):
-                        nc.tensor.matmul_mx(
-                            out=y_banks[nt][:],
-                            lhsT=frozen_words[e][:, s, 2 * P * nt : 2 * P * (nt + 1)].bitcast(FP4X4),
-                            lhsT_scale=frozen_scales[:, e * PASSES + s, P * nt : P * (nt + 1)],
-                            rhs=slot_words[s][:, slots].bitcast(FP8X4),
-                            rhs_scale=planes_at_zero[s][:, slots],
-                            start=(s == 0),
-                            stop=False,
-                        )
-
-                h_bf = sb("h_bf%d_%d" % (e, u), [P, PACK * UNIT], BF16)
-                h_codes = sb("h_codes%d_%d" % (e, u), [P, UNIT], U32)
-                h_scales = sb("h_scales%d_%d" % (e, u), [P, UNIT], U8)
+                nc.tensor.matmul_mx(
+                    out=bank("H%d%d" % (e, u), h_psum, [P, PACK, UNIT], "h")[:, t, :],
+                    lhsT=sb("Q%d%d" % (e, s))[:, cols].bitcast(FP8X4),
+                    lhsT_scale=tiles["qs%d%d" % (e, s)][:, cols],
+                    rhs=slot_words(e, s, u).bitcast(FP8X4),
+                    rhs_scale=slot_scales[ROWS * s :, first : first + UNIT],
+                    start=(s == 0),
+                    stop=(s == PASSES - 1),
+                )
+            elif kind == "f":
+                e, u, nt, s = digits
+                first = e * C + u * UNIT
+                nc.tensor.matmul_mx(
+                    out=bank("Y%d%d%d" % (e, u, nt), y_psum, [P, UNIT], "y%d" % nt)[:],
+                    lhsT=sb("W%d" % e)[:, s, 2 * P * nt : 2 * P * (nt + 1)].bitcast(FP4X4),
+                    lhsT_scale=frozen_scales[:, e * PASSES + s, P * nt : P * (nt + 1)],
+                    rhs=slot_words(e, s, u).bitcast(FP8X4),
+                    rhs_scale=planes_at_zero[s][:, first : first + UNIT],
+                    start=(s == 0),
+                    stop=False,
+                )
+            elif kind == "ge":
+                e, u = digits
                 nc.scalar.activation(
-                    out=h_bf[:].rearrange("p (u t) -> p u t", t=PACK),
-                    in_=h_bank[:].rearrange("p t u -> p u t"),
+                    out=sb("HB%d%d" % (e, u))[:].rearrange("p (u t) -> p u t", t=PACK),
+                    in_=tiles["H%d%d" % (e, u)][:].rearrange("p t u -> p u t"),
                     func=GELU,
                 )
-                nc.vector.quantize_mx(out=h_codes[:].bitcast(FP8X4), scales=h_scales[:], in_=h_bf[:])
-
-                for nt in range(N_TILES):
-                    cols = slice(nt * P, (nt + 1) * P)
-                    nc.tensor.matmul_mx(
-                        out=y_banks[nt][:],
-                        lhsT=wb_codes[e][:, cols].bitcast(FP8X4),
-                        lhsT_scale=wb_scales[e][:, cols],
-                        rhs=h_codes[:].bitcast(FP8X4),
-                        rhs_scale=h_scales[:],
-                        start=False,
-                        stop=True,
+            elif kind == "hq":
+                e, u = digits
+                nc.vector.quantize_mx(
+                    out=sb("HQ%d%d" % (e, u))[:].bitcast(FP8X4),
+                    scales=own("hs%d%d" % (e, u), [P, UNIT], U8)[:],
+                    in_=sb("HB%d%d" % (e, u))[:],
+                )
+            elif kind == "b":
+                e, u, nt = digits
+                cols = slice(nt * P, (nt + 1) * P)
+                nc.tensor.matmul_mx(
+                    out=tiles["Y%d%d%d" % (e, u, nt)][:],
+                    lhsT=sb("QB%d" % e)[:, cols].bitcast(FP8X4),
+                    lhsT_scale=tiles["qbs%d" % e][:, cols],
+                    rhs=sb("HQ%d%d" % (e, u))[:].bitcast(FP8X4),
+                    rhs_scale=tiles["hs%d%d" % (e, u)][:],
+                    start=False,
+                    stop=True,
+                )
+            elif kind == "m":
+                e, u, nt = digits
+                if FINE[e]:
+                    dst = sb("S%d%d%d" % (e, u, nt))[:]
+                else:
+                    dst = sb("S%d%d" % (e, nt))[:, u * UNIT : (u + 1) * UNIT]
+                nc.scalar.copy(out=dst, in_=tiles["Y%d%d%d" % (e, u, nt)][:])
+            elif kind == "sc":
+                e, u, nt = digits
+                if FINE[e]:
+                    nc.vector.tensor_tensor(
+                        results[nt][:].indirect(slot_list(e * C + u * UNIT, UNIT)),
+                        sb("S%d%d%d" % (e, u, nt))[:],
+                        sb("G%d" % e)[:, u * UNIT : (u + 1) * UNIT],
+                        MULT,
                     )
-                    nc.vector.tensor_tensor(sums[nt][:, local], y_banks[nt][:], gates[e][:, local], MULT)
-                if e == E - 1:
-                    for nt in range(N_TILES):
-                        nc.vector.tensor_copy(
-                            out=results[nt][:].indirect(slot_list(first, UNIT)), in_=sums[nt][:, local]
-                        )
-            if e < E - 1:
-                for nt in range(N_TILES):
-                    nc.vector.tensor_copy(out=results[nt][:].indirect(slot_list(e * C, C)), in_=sums[nt][:])
+                else:
+                    nc.vector.tensor_tensor(
+                        results[nt][:].indirect(slot_list(e * C, C)), sb("S%d%d" % (e, nt))[:], sb("G%d" % e)[:], MULT
+                    )
+            else:
+                assert kind == "st"
+                nt = digits[0]
+                nc.sync.dma_start(out=out[nt * P : (nt + 1) * P, :], in_=results[nt][:])
 
-        for nt in range(N_TILES):
-            nc.sync.dma_start(out=out[nt * P : (nt + 1) * P, :], in_=results[nt][:])
+        for name in ORDER:
+            step(name)

@@ -27,60 +27,7 @@ QUADS = 4
 ROWS = 4
 GROUPS = H // 16
 MOVED_ROWS = 112
-
-VECTOR_SHARE = [[20,0,0],[0,16,0],[0,16,0]]
-LAST_CUT = 32
-WB_ON_VECTOR = [1,1,0]
-FINE = [0,1,0]
-HOST = {"HB11":"R21","HB10":"R21","Q10":"HQ01","B10":"B01","X02":"R01","HQ20":"Q21","Q12":"S01"}
-ORDER = ["ms_ts","ms_w","ms_ws","ms_m1","ms_m2","warm","wa00","offs","xw0","xs0","xs1","xs2","xs3","wa02","xw1","wa01","ws0","ws1","ws2","ws3","cv00","c00","c02","g10","gs1","g00","wa10","xw2","wb0_0","wb0_1","wb0_2","wb0_3","wa11","q00","q02","g11","g01","gs0","mv1","mv2","h00_0","w0","wb1_0","wb1_1","wb1_2","wb1_3","wa12","gate0","c01","q01","c10","h00_1","g02","h00_2","h00_3","h00_4","h00_5","h00_6","h00_7","h00_8","h00_9","h00_10","h00_11","cb0","qb0","h01_0","h01_1","h01_2","h01_3","h01_4","h01_5","h01_6","h01_7","h01_8","h01_9","h01_10","h01_11","f000_0","f000_1","f000_2","f001_0","f001_1","f001_2","f010_0","f010_1","f010_2","f011_0","f011_1","f011_2","g12","ge00","hq00","b000","b001","ge01","hq01","b010","b011","q10","h10_0","h11_0","cv11","c11","m001","m010","m011","sc011","cb1","q11","h10_1","h11_1","qb1","c12","q12","h10_2","h10_3","h10_4","h10_5","h10_6","h10_7","h10_8","h10_9","h10_10","h10_11","h11_2","h11_3","h11_4","h11_5","h11_6","h11_7","h11_8","h11_9","h11_10","h11_11","m000","sc010","wa20","c20","q20","wa22a","c22a","w1","f110_0","f110_1","f110_2","f111_0","f111_1","f111_2","wa21","cv21","c21","ge11","q21","ge10","hq11","wb2_0","wb2_1","wb2_2","wb2_3","cb2","w2","gate2","gate1","q22","qb2","hq10","b110","m110","sc110","b111","m111","sc111","h20_0","h20_1","h20_2","h20_3","h20_4","h20_5","h20_6","h20_7","h20_8","h20_9","h20_10","h20_11","ge20","h21_0","h21_1","h21_2","h21_3","h21_4","h21_5","h21_6","h21_7","h21_8","h21_9","h21_10","hq20","h21_11","ge21","hq21","f100_0","f100_1","f100_2","b100","m100","sc100","f101_0","f101_1","f101_2","b101","m101","sc101","f200_0","f200_1","f200_2","b200","m200","f201_0","f201_1","f201_2","b201","m201","f210_0","f210_1","f210_2","b210","m210","sc210","f211_0","f211_1","f211_2","b211","m211","sc211","st0","st1"]
-
-SHAPES = {
-    "TS": ([P, T], U8, 1),
-    "TW": ([P, T], I32, 4),
-    "RB": ([P, PACK, N], F32, 4),
-    "R": ([P, PACK, H], F32, 4),
-    "W": ([P, PASSES, 2 * N], U8, 1),
-    "G": ([P, C], F32, 4),
-    "X": ([P, C], U32, 4),
-    "BB": ([P, PACK * N], BF16, 2),
-    "B": ([P, PACK * H], BF16, 2),
-    "QB": ([P, N], U32, 4),
-    "Q": ([P, H], U32, 4),
-    "HB": ([P, PACK * UNIT], BF16, 2),
-    "HQ": ([P, UNIT], U32, 4),
-}
-
-
-def shape_of(name):
-    kind = "".join([ch for ch in name if ch not in "0123456789"])
-    if kind == "X" and name[1] == "1":
-        return ([P, 2 * C], U32, 4)
-    if kind == "S":
-        return ([P, UNIT if len(name) == 4 else C], F32, 4)
-    return SHAPES[kind]
-
-
-def size_of(name):
-    shape, dtype, width = shape_of(name)
-    for n in shape[1:]:
-        width = width * n
-    return width
-
-
-def guests_of(name):
-    return sorted([g for g in HOST if HOST[g] == name], key=extent)
-
-
-def extent(name):
-    return max(size_of(name), sum([extent(g) for g in guests_of(name)]))
-
-
-def lay_out(name, offset, place):
-    place[name] = offset
-    for g in guests_of(name):
-        lay_out(g, offset, place)
-        offset = offset + extent(g)
+VECTOR_GROUPS = (8, 12, 20)
 
 
 def tile_moe_elr_gelu_kernel(
@@ -89,228 +36,242 @@ def tile_moe_elr_gelu_kernel(
     nc = tc.nc
     with ExitStack() as ctx:
         keep = ctx.enter_context(tc.tile_pool(name="keep", bufs=1))
-        shared = ctx.enter_context(tc.tile_pool(name="shared", bufs=1))
-        h_psum = ctx.enter_context(tc.psum_pool(name="h_psum", bufs=4))
-        y_psum = ctx.enter_context(tc.psum_pool(name="y_psum", bufs=2))
+        psum = ctx.enter_context(tc.psum_pool(name="psum", bufs=2))
 
-        place = {}
-        top = 0
-        for root in sorted(set(HOST.values()) - set(HOST)):
-            lay_out(root, top, place)
-            top = top + extent(root)
-        tiles = {}
+        def sbuf(name, shape, dtype):
+            return keep.tile(shape, dtype, name=name, align_bytes=64)
 
-        def sb(name):
-            if name not in tiles:
-                shape, dtype, width = shape_of(name)
-                if name in place:
-                    tiles[name] = shared.tile(shape, dtype, name=name, align_bytes=64, offset=place[name])
-                else:
-                    tiles[name] = keep.tile(shape, dtype, name=name, align_bytes=64)
-            return tiles[name]
+        def per_tile(name, shape, dtype):
+            return [[sbuf("%s%d%d" % (name, e, s), shape, dtype) for s in range(PASSES)] for e in range(E)]
 
-        def own(name, shape, dtype):
-            if name not in tiles:
-                tiles[name] = keep.tile(shape, dtype, name=name, align_bytes=64)
-            return tiles[name]
+        def per_expert(name, shape, dtype):
+            return [sbuf("%s%d" % (name, e), shape, dtype) for e in range(E)]
 
         offsets = keep.tile([P, T // 16], U16, name="offsets")
-        slot_scales = own("slot_scales", [P, T], U8)
-        planes_at_zero = [slot_scales] + [own("moved%d" % s, [P, T], U8) for s in range(1, PASSES)]
-        frozen_scales = own("frozen_scales", [P, E * PASSES, N], U8)
-        results = [own("results%d" % nt, [P, T], F32) for nt in range(N_TILES)]
-        warm = own("warm", [P, 2], F32)
+        token_scales = sbuf("token_scales", [P, T], U8)
+        token_words = [sbuf("token_words%d" % s, [P, T], I32) for s in range(PASSES)]
+        slot_scales = sbuf("slot_scales", [P, T], U8)
+        planes_at_zero = [slot_scales] + [sbuf("moved%d" % s, [P, T], U8) for s in range(1, PASSES)]
+        first_words = [sbuf("first_words%d" % s, [P, C], U32) for s in range(PASSES)]
+        later_words = [sbuf("later_words%d" % s, [P, T - C], U32) for s in range(PASSES)]
+        frozen_scales = sbuf("frozen_scales", [P, E * PASSES, N], U8)
+        frozen_words = per_expert("frozen_words", [P, PASSES, 2 * N], U8)
+        wa_bf16 = per_tile("wa_bf16", [P, PACK * H], BF16)
+        wa_codes = per_tile("wa_codes", [P, H], U32)
+        wa_scales = per_tile("wa_scales", [P, H], U8)
+        wb_raw = [keep.tile([P, PACK, N], F32, name="wb_raw%d" % e, tag="wb_h%d" % e, align_bytes=64) for e in range(E)]
+        wb_bf16 = per_expert("wb_bf16", [P, PACK * N], BF16)
+        wb_codes = per_expert("wb_codes", [P, N], U32)
+        wb_scales = per_expert("wb_scales", [P, N], U8)
+        gates = per_expert("gates", [P, C], F32)
+        results = [sbuf("results%d" % nt, [P, T], F32) for nt in range(N_TILES)]
+        warm = sbuf("warm", [P, 2], F32)
+        wa_raw = {}
+        hidden = {}
+        banks = {}
+        sums = {}
+        rounded = {}
 
         def slot_list(first, count):
             return offsets[:, first // 16 : (first + count) // 16]
 
         def slot_words(e, s, u):
-            first = max(e - 1, 0) * C + u * UNIT
-            return sb("X%d%d" % (min(e, 1), s))[:, first : first + UNIT]
+            if e == 0:
+                return first_words[s][:, u * UNIT : (u + 1) * UNIT]
+            first = (e - 1) * C + u * UNIT
+            return later_words[s][:, first : first + UNIT]
 
-        def piece(name):
-            if name[-1] == "a":
-                return 0, LAST_CUT
-            if name[-1] == "b":
-                return LAST_CUT, GROUPS
-            return 0, GROUPS
+        def pieces(e, s):
+            return [(0, GROUPS)]
 
-        def bank(name, pool, shape, tag):
-            if name not in tiles:
-                tiles[name] = pool.tile(shape, F32, name=name, tag=tag)
-            return tiles[name]
+        def load_wa(e, s, piece):
+            q0, q1 = piece
+            raw = keep.tile([P, PACK, H], F32, name="wa_raw%d%d" % (e, s), tag="raw%d%d" % (e, s), align_bytes=64)
+            wa_raw[e, s, q0] = raw
+            rows = wa[e, s * K_PASS : (s + 1) * K_PASS, :].rearrange("(p j) i -> p j i", j=PACK)
+            nc.sync.dma_start(out=raw[:], in_=rows[:, :, 16 * q0 : 16 * q1])
 
-        def step(name):
-            digits = [int(ch) for ch in name if ch in "0123456789"]
-            kind = "".join([ch for ch in name.split("_")[0] if ch not in "0123456789"])
-            if name == "ms_ts":
-                nc.vector.memset(sb("TS")[:].bitcast(I32), 0)
-            elif name == "ms_w":
-                nc.vector.memset(warm[:, 0:1], 0.0)
-            elif name == "ms_ws":
-                nc.vector.memset(frozen_scales[:].rearrange("p g n -> p (g n)").bitcast(I32), 0)
-            elif kind == "ms":
-                nc.vector.memset(planes_at_zero[digits[0]][:].bitcast(I32), 0)
-            elif name == "warm":
-                nc.scalar.activation(out=warm[:, 1:2], in_=warm[:, 0:1], func=GELU)
-            elif name == "offs":
-                nc.sync.dma_start(offsets[:], offs)
-            elif kind == "xs":
-                q = digits[0]
-                nc.sync.dma_start(
-                    out=sb("TS")[32 * q : 32 * q + ROWS * PASSES, :].bitcast(I32),
-                    in_=x_scales[:, ROWS * q : ROWS * (q + 1), :].bitcast(I32),
-                )
-            elif kind == "ws":
-                r = digits[0]
-                rows = w_scales.rearrange("e s (q r) n -> r q (e s) n", r=ROWS)[r]
-                nc.sync.dma_start(out=frozen_scales[r:P:32, :, :].bitcast(I32), in_=rows.bitcast(I32))
-            elif kind == "xw":
-                s = digits[0]
-                nc.sync.dma_start(out=sb("TW%d" % s)[:], in_=x_words[s].rearrange("p t d -> p (t d)").bitcast(I32))
-            elif kind in ("wa", "waa", "wab"):
-                e, s = digits
-                q0, q1 = piece(name[2:])
-                rows = wa[e, s * K_PASS : (s + 1) * K_PASS, :].rearrange("(p j) i -> p j i", j=PACK)
-                nc.sync.dma_start(
-                    out=sb("R%d%d" % (e, s))[:, :, 16 * q0 : 16 * q1], in_=rows[:, :, 16 * q0 : 16 * q1]
-                )
-            elif kind == "wb":
-                e, t = digits
-                rows = wb[e].rearrange("(q t r) n -> t q r n", t=PACK, r=4)
-                nc.sync.dma_start(out=sb("RB%d" % e)[:, t, :], in_=rows[t])
-            elif kind == "w":
-                e = digits[0]
-                nc.sync.dma_start(
-                    out=sb("W%d" % e)[:].bitcast(I32), in_=w_words[e].rearrange("s p b -> p s b").bitcast(I32)
-                )
-            elif kind == "gate":
-                e = digits[0]
-                nc.sync.dma_start(out=sb("G%d" % e)[:], in_=gate[:, e * C : (e + 1) * C])
-            elif kind == "gs":
-                first, count = (0, C) if digits[0] == 0 else (C, T - C)
-                nc.vector.tensor_copy(
-                    out=slot_scales[:, first : first + count], in_=sb("TS")[:].indirect(slot_list(first, count))
-                )
-            elif kind == "mv":
-                s = digits[0]
+        def load_words(s):
+            nc.sync.dma_start(out=token_words[s][:], in_=x_words[s].rearrange("p t d -> p (t d)").bitcast(I32))
+
+        def load_second_stage(e):
+            rows = wb[e].rearrange("(q t r) n -> t q r n", t=PACK, r=4)
+            for t in range(PACK):
+                nc.sync.dma_start(out=wb_raw[e][:, t, :], in_=rows[t])
+            nc.sync.dma_start(
+                out=frozen_words[e][:].bitcast(I32), in_=w_words[e].rearrange("s p b -> p s b").bitcast(I32)
+            )
+            nc.sync.dma_start(out=gates[e][:], in_=gate[:, e * C : (e + 1) * C])
+
+        def gather_words(s, later):
+            dst, first, count = (later_words[s], C, T - C) if later else (first_words[s], 0, C)
+            nc.vector.tensor_copy(out=dst[:], in_=token_words[s][:].bitcast(U32).indirect(slot_list(first, count)))
+
+        def gather_scales(later):
+            first, count = (C, T - C) if later else (0, C)
+            nc.vector.tensor_copy(
+                out=slot_scales[:, first : first + count], in_=token_scales[:].indirect(slot_list(first, count))
+            )
+
+        def move_planes():
+            for s in range(1, PASSES):
                 nc.sync.dma_start(
                     out=planes_at_zero[s][0:MOVED_ROWS, :].bitcast(I32),
                     in_=slot_scales[ROWS * s : ROWS * s + MOVED_ROWS, :].bitcast(I32),
                 )
-            elif kind == "g":
-                e, s = digits
-                nc.vector.tensor_copy(
-                    out=sb("X%d%d" % (e, s))[:],
-                    in_=sb("TW%d" % s)[:].bitcast(U32).indirect(slot_list(e * C, C if e == 0 else 2 * C)),
-                )
-            elif kind in ("c", "ca", "cv", "cva", "cvb") or name == "c22b":
-                e, s = digits
-                q0, q1 = piece(name)
-                cut = q0 + 2 * ((q1 - q0) * VECTOR_SHARE[e][s] // (2 * GROUPS))
-                src = sb("R%d%d" % (e, s))[:].rearrange("p j (q t r) -> p q t j r", t=PACK, r=4)
-                dst = sb("B%d%d" % (e, s))[:].rearrange("p (t q r j) -> p q t j r", t=PACK, r=4, j=PACK)
-                if kind.startswith("cv"):
-                    nc.vector.tensor_copy(out=dst[:, q0:cut], in_=src[:, q0:cut])
-                else:
-                    nc.scalar.copy(out=dst[:, cut:q1], in_=src[:, cut:q1])
-            elif kind == "q":
-                e, s = digits
+
+        def round_wa(e, s):
+            dst = wa_bf16[e][s][:].rearrange("p (t q r j) -> p q t j r", t=PACK, r=4, j=PACK)
+            for q0, q1 in pieces(e, s):
+                src = wa_raw[e, s, q0][:].rearrange("p j (q t r) -> p q t j r", t=PACK, r=4)
+                share = VECTOR_GROUPS[s] if (e > 0 or s == PASSES - 1) else 0
+                if share:
+                    nc.vector.tensor_copy(out=dst[:, q0 : q0 + share], in_=src[:, 0:share])
+                nc.scalar.copy(out=dst[:, q0 + share : q1], in_=src[:, share : q1 - q0])
+
+        def first_products(e, s):
+            if s == 0:
+                for u in range(UNITS):
+                    hidden[e, u] = psum.tile([P, PACK, UNIT], F32, name="h%d%d" % (e, u), tag="h%d" % u)
+            width = P if s == PASSES - 1 else H
+            for c0 in range(0, H, width):
                 nc.vector.quantize_mx(
-                    out=sb("Q%d%d" % (e, s))[:].bitcast(FP8X4),
-                    scales=own("qs%d%d" % (e, s), [P, H], U8)[:],
-                    in_=sb("B%d%d" % (e, s))[:],
+                    out=wa_codes[e][s][:, c0 : c0 + width].bitcast(FP8X4),
+                    scales=wa_scales[e][s][:, c0 : c0 + width],
+                    in_=wa_bf16[e][s][:, PACK * c0 : PACK * (c0 + width)],
                 )
-            elif kind == "cb":
-                e = digits[0]
-                copy = nc.vector.tensor_copy if WB_ON_VECTOR[e] else nc.scalar.copy
-                copy(
-                    out=sb("BB%d" % e)[:].rearrange("p (c i j) -> p c j i", i=4, j=PACK),
-                    in_=sb("RB%d" % e)[:].rearrange("p j (c i) -> p c j i", i=4),
-                )
-            elif kind == "qb":
-                e = digits[0]
-                nc.vector.quantize_mx(
-                    out=sb("QB%d" % e)[:].bitcast(FP8X4),
-                    scales=own("qbs%d" % e, [P, N], U8)[:],
-                    in_=sb("BB%d" % e)[:],
-                )
-            elif kind == "h":
-                e, u = digits[:2]
-                t, s = divmod(int(name.split("_")[1]), PASSES)
-                cols = slice(t * P, (t + 1) * P)
+            for u in range(UNITS):
                 first = e * C + u * UNIT
-                nc.tensor.matmul_mx(
-                    out=bank("H%d%d" % (e, u), h_psum, [P, PACK, UNIT], "h")[:, t, :],
-                    lhsT=sb("Q%d%d" % (e, s))[:, cols].bitcast(FP8X4),
-                    lhsT_scale=tiles["qs%d%d" % (e, s)][:, cols],
-                    rhs=slot_words(e, s, u).bitcast(FP8X4),
-                    rhs_scale=slot_scales[ROWS * s :, first : first + UNIT],
-                    start=(s == 0),
-                    stop=(s == PASSES - 1),
-                )
-            elif kind == "f":
-                e, u, nt, s = digits
-                first = e * C + u * UNIT
-                nc.tensor.matmul_mx(
-                    out=bank("Y%d%d%d" % (e, u, nt), y_psum, [P, UNIT], "y%d" % nt)[:],
-                    lhsT=sb("W%d" % e)[:, s, 2 * P * nt : 2 * P * (nt + 1)].bitcast(FP4X4),
-                    lhsT_scale=frozen_scales[:, e * PASSES + s, P * nt : P * (nt + 1)],
-                    rhs=slot_words(e, s, u).bitcast(FP8X4),
-                    rhs_scale=planes_at_zero[s][:, first : first + UNIT],
-                    start=(s == 0),
-                    stop=False,
-                )
-            elif kind == "ge":
-                e, u = digits
-                nc.scalar.activation(
-                    out=sb("HB%d%d" % (e, u))[:].rearrange("p (u t) -> p u t", t=PACK),
-                    in_=tiles["H%d%d" % (e, u)][:].rearrange("p t u -> p u t"),
-                    func=GELU,
-                )
-            elif kind == "hq":
-                e, u = digits
-                nc.vector.quantize_mx(
-                    out=sb("HQ%d%d" % (e, u))[:].bitcast(FP8X4),
-                    scales=own("hs%d%d" % (e, u), [P, UNIT], U8)[:],
-                    in_=sb("HB%d%d" % (e, u))[:],
-                )
-            elif kind == "b":
-                e, u, nt = digits
+                for t in range(PACK):
+                    cols = slice(t * P, (t + 1) * P)
+                    nc.tensor.matmul_mx(
+                        out=hidden[e, u][:, t, :],
+                        lhsT=wa_codes[e][s][:, cols].bitcast(FP8X4),
+                        lhsT_scale=wa_scales[e][s][:, cols],
+                        rhs=slot_words(e, s, u).bitcast(FP8X4),
+                        rhs_scale=slot_scales[ROWS * s :, first : first + UNIT],
+                        start=(s == 0 and t == 0),
+                        stop=(s == PASSES - 1 and t == PACK - 1),
+                    )
+
+        def round_wb(e):
+            nc.scalar.copy(
+                out=wb_bf16[e][:].rearrange("p (c i j) -> p c j i", i=4, j=PACK),
+                in_=wb_raw[e][:].rearrange("p j (c i) -> p c j i", i=4),
+            )
+
+        def quantise_wb(e):
+            nc.vector.quantize_mx(out=wb_codes[e][:].bitcast(FP8X4), scales=wb_scales[e][:], in_=wb_bf16[e][:])
+
+        def frozen_products(e, u):
+            first = e * C + u * UNIT
+            banks[e, u] = psum.tile([P, N_TILES, UNIT], F32, name="y%d%d" % (e, u), tag="y%d" % u)
+            for s in range(PASSES):
+                for nt in range(N_TILES):
+                    nc.tensor.matmul_mx(
+                        out=banks[e, u][:, nt, :],
+                        lhsT=frozen_words[e][:, s, 2 * P * nt : 2 * P * (nt + 1)].bitcast(FP4X4),
+                        lhsT_scale=frozen_scales[:, e * PASSES + s, P * nt : P * (nt + 1)],
+                        rhs=slot_words(e, s, u).bitcast(FP8X4),
+                        rhs_scale=planes_at_zero[s][:, first : first + UNIT],
+                        start=(s == 0 and nt == 0),
+                        stop=False,
+                    )
+
+        def second_products(e, u):
+            if u == 0:
+                rounded[e] = keep.tile([P, UNITS, PACK * UNIT], BF16, name="h_bf16%d" % e, tag="wb_h%d" % e, align_bytes=64)
+            h_bf16 = rounded[e][:, u, :]
+            h_codes = sbuf("h_codes%d%d" % (e, u), [P, UNIT], U32)
+            h_scales = sbuf("h_scales%d%d" % (e, u), [P, UNIT], U8)
+            nc.scalar.activation(
+                out=h_bf16.rearrange("p (u t) -> p u t", t=PACK),
+                in_=hidden[e, u][:].rearrange("p t u -> p u t"),
+                func=GELU,
+            )
+            nc.vector.quantize_mx(out=h_codes[:].bitcast(FP8X4), scales=h_scales[:], in_=h_bf16)
+            for nt in range(N_TILES):
                 cols = slice(nt * P, (nt + 1) * P)
                 nc.tensor.matmul_mx(
-                    out=tiles["Y%d%d%d" % (e, u, nt)][:],
-                    lhsT=sb("QB%d" % e)[:, cols].bitcast(FP8X4),
-                    lhsT_scale=tiles["qbs%d" % e][:, cols],
-                    rhs=sb("HQ%d%d" % (e, u))[:].bitcast(FP8X4),
-                    rhs_scale=tiles["hs%d%d" % (e, u)][:],
+                    out=banks[e, u][:, nt, :],
+                    lhsT=wb_codes[e][:, cols].bitcast(FP8X4),
+                    lhsT_scale=wb_scales[e][:, cols],
+                    rhs=h_codes[:].bitcast(FP8X4),
+                    rhs_scale=h_scales[:],
                     start=False,
-                    stop=True,
+                    stop=(nt == N_TILES - 1),
                 )
-            elif kind == "m":
-                e, u, nt = digits
-                if FINE[e]:
-                    dst = sb("S%d%d%d" % (e, u, nt))[:]
-                else:
-                    dst = sb("S%d%d" % (e, nt))[:, u * UNIT : (u + 1) * UNIT]
-                nc.scalar.copy(out=dst, in_=tiles["Y%d%d%d" % (e, u, nt)][:])
-            elif kind == "sc":
-                e, u, nt = digits
-                if FINE[e]:
-                    nc.vector.tensor_tensor(
-                        results[nt][:].indirect(slot_list(e * C + u * UNIT, UNIT)),
-                        sb("S%d%d%d" % (e, u, nt))[:],
-                        sb("G%d" % e)[:, u * UNIT : (u + 1) * UNIT],
-                        MULT,
-                    )
-                else:
-                    nc.vector.tensor_tensor(
-                        results[nt][:].indirect(slot_list(e * C, C)), sb("S%d%d" % (e, nt))[:], sb("G%d" % e)[:], MULT
-                    )
-            else:
-                assert kind == "st"
-                nt = digits[0]
-                nc.sync.dma_start(out=out[nt * P : (nt + 1) * P, :], in_=results[nt][:])
 
-        for name in ORDER:
-            step(name)
+        def leave_psum(e, u):
+            tag = "raw%d%d" % (e + 1, PASSES - 1) if (u == UNITS - 1 and e < E - 1) else "sums%d%d" % (e, u)
+            sums[e, u] = keep.tile([P, N_TILES, UNIT], F32, name="sums%d%d" % (e, u), tag=tag, align_bytes=64)
+            nc.scalar.copy(out=sums[e, u][:], in_=banks[e, u][:])
+
+        def scatter(e, u):
+            for nt in range(N_TILES):
+                window = results[nt][:].indirect(slot_list(e * C + u * UNIT, UNIT))
+                nc.vector.tensor_tensor(window, sums[e, u][:, nt, :], gates[e][:, u * UNIT : (u + 1) * UNIT], MULT)
+
+        nc.vector.memset(token_scales[:].bitcast(I32), 0)
+        nc.vector.memset(warm[:, 0:1], 0.0)
+        nc.vector.memset(frozen_scales[:].rearrange("p g n -> p (g n)").bitcast(I32), 0)
+        for s in range(1, PASSES):
+            nc.vector.memset(planes_at_zero[s][:].bitcast(I32), 0)
+
+        for q in range(QUADS):
+            nc.scalar.dma_start(
+                out=token_scales[32 * q : 32 * q + ROWS * PASSES, :].bitcast(I32),
+                in_=x_scales[:, ROWS * q : ROWS * (q + 1), :].bitcast(I32),
+            )
+        nc.scalar.activation(out=warm[:, 1:2], in_=warm[:, 0:1], func=GELU)
+        nc.sync.dma_start(offsets[:], offs)
+        load_words(0)
+        load_words(1)
+        load_wa(0, 0, pieces(0, 0)[0])
+        for r in range(ROWS):
+            rows = w_scales.rearrange("e s (q r) n -> r q (e s) n", r=ROWS)[r]
+            nc.sync.dma_start(out=frozen_scales[r:P:32, :, :].bitcast(I32), in_=rows.bitcast(I32))
+        load_wa(0, 1, pieces(0, 1)[0])
+        load_words(2)
+        load_wa(0, 2, pieces(0, 2)[0])
+
+        gather_words(0, False)
+        gather_scales(False)
+        gather_words(0, True)
+        gather_scales(True)
+        move_planes()
+        load_second_stage(0)
+        for e in range(1, E):
+            for s in range(PASSES):
+                load_wa(e, s, pieces(e, s)[0])
+            load_second_stage(e)
+        for s in range(PASSES - 1):
+            round_wa(0, s)
+            gather_words(s + 1, False)
+            first_products(0, s)
+            gather_words(s + 1, True)
+
+        for e in range(E):
+            round_wa(e, 2)
+            if e > 0:
+                leave_psum(e - 1, 1)
+            round_wb(e)
+            first_products(e, 2)
+            if e > 0:
+                scatter(e - 1, 1)
+            quantise_wb(e)
+            for u in range(UNITS):
+                frozen_products(e, u)
+            for u in range(UNITS):
+                second_products(e, u)
+            leave_psum(e, 0)
+            scatter(e, 0)
+            if e < E - 1:
+                for s in range(PASSES - 1):
+                    round_wa(e + 1, s)
+                    first_products(e + 1, s)
+        leave_psum(E - 1, 1)
+        scatter(E - 1, 1)
+
+        for nt in range(N_TILES):
+            nc.sync.dma_start(out=out[nt * P : (nt + 1) * P, :], in_=results[nt][:])

@@ -27,7 +27,7 @@ QUADS = 4
 ROWS = 4
 GROUPS = H // 16
 MOVED_ROWS = 112
-VECTOR_GROUPS = (8, 12, 20)
+VECTOR_GROUPS = (0, 8, 16)
 
 
 def tile_moe_elr_gelu_kernel(
@@ -133,7 +133,7 @@ def tile_moe_elr_gelu_kernel(
             if s == 0:
                 for u in range(UNITS):
                     hidden[e, u] = psum.tile([P, PACK, UNIT], F32, name="h%d%d" % (e, u), tag="h%d" % u)
-            width = P if s == PASSES - 1 else H
+            width = P if False else H
             for c0 in range(0, H, width):
                 nc.vector.quantize_mx(
                     out=wa_codes[e][s][:, c0 : c0 + width].bitcast(FP8X4),
@@ -202,15 +202,25 @@ def tile_moe_elr_gelu_kernel(
                     stop=(nt == N_TILES - 1),
                 )
 
+        def on_vector(e, u):
+            return u == 0 and e < E - 1
+
         def leave_psum(e, u):
             tag = "raw%d%d" % (e + 1, PASSES - 1) if (u == UNITS - 1 and e < E - 1) else "sums%d%d" % (e, u)
             sums[e, u] = keep.tile([P, N_TILES, UNIT], F32, name="sums%d%d" % (e, u), tag=tag, align_bytes=64)
-            nc.scalar.copy(out=sums[e, u][:], in_=banks[e, u][:])
+            if on_vector(e, u):
+                weights = gates[e][:, u * UNIT : (u + 1) * UNIT].unsqueeze(1).to_broadcast([P, N_TILES, UNIT])
+                nc.vector.tensor_tensor(sums[e, u][:], banks[e, u][:], weights, MULT)
+            else:
+                nc.scalar.copy(out=sums[e, u][:], in_=banks[e, u][:])
 
         def scatter(e, u):
             for nt in range(N_TILES):
                 window = results[nt][:].indirect(slot_list(e * C + u * UNIT, UNIT))
-                nc.vector.tensor_tensor(window, sums[e, u][:, nt, :], gates[e][:, u * UNIT : (u + 1) * UNIT], MULT)
+                if on_vector(e, u):
+                    nc.vector.tensor_copy(out=window, in_=sums[e, u][:, nt, :])
+                else:
+                    nc.vector.tensor_tensor(window, sums[e, u][:, nt, :], gates[e][:, u * UNIT : (u + 1) * UNIT], MULT)
 
         nc.vector.memset(token_scales[:].bitcast(I32), 0)
         nc.vector.memset(warm[:, 0:1], 0.0)
@@ -224,13 +234,13 @@ def tile_moe_elr_gelu_kernel(
                 in_=x_scales[:, ROWS * q : ROWS * (q + 1), :].bitcast(I32),
             )
         nc.scalar.activation(out=warm[:, 1:2], in_=warm[:, 0:1], func=GELU)
-        nc.sync.dma_start(offsets[:], offs)
-        load_words(0)
-        load_words(1)
-        load_wa(0, 0, pieces(0, 0)[0])
         for r in range(ROWS):
             rows = w_scales.rearrange("e s (q r) n -> r q (e s) n", r=ROWS)[r]
-            nc.sync.dma_start(out=frozen_scales[r:P:32, :, :].bitcast(I32), in_=rows.bitcast(I32))
+            nc.gpsimd.dma_start(out=frozen_scales[r:P:32, :, :].bitcast(I32), in_=rows.bitcast(I32))
+        load_words(0)
+        nc.sync.dma_start(offsets[:], offs)
+        load_words(1)
+        load_wa(0, 0, pieces(0, 0)[0])
         load_wa(0, 1, pieces(0, 1)[0])
         load_words(2)
         load_wa(0, 2, pieces(0, 2)[0])
@@ -239,8 +249,8 @@ def tile_moe_elr_gelu_kernel(
         gather_scales(False)
         gather_words(0, True)
         gather_scales(True)
-        move_planes()
         load_second_stage(0)
+        move_planes()
         for e in range(1, E):
             for s in range(PASSES):
                 load_wa(e, s, pieces(e, s)[0])

@@ -27,7 +27,7 @@ QUADS = 4
 ROWS = 4
 GROUPS = H // 16
 MOVED_ROWS = 112
-VECTOR_GROUPS = (0, 8, 16)
+VECTOR_GROUPS = (0, 12, 20)
 
 
 def tile_moe_elr_gelu_kernel(
@@ -37,6 +37,7 @@ def tile_moe_elr_gelu_kernel(
     with ExitStack() as ctx:
         keep = ctx.enter_context(tc.tile_pool(name="keep", bufs=1))
         psum = ctx.enter_context(tc.psum_pool(name="psum", bufs=2))
+        psum_once = ctx.enter_context(tc.psum_pool(name="psum_once", bufs=1))
 
         def sbuf(name, shape, dtype):
             return keep.tile(shape, dtype, name=name, align_bytes=64)
@@ -60,7 +61,7 @@ def tile_moe_elr_gelu_kernel(
         wa_codes = per_tile("wa_codes", [P, H], U32)
         wa_scales = per_tile("wa_scales", [P, H], U8)
         wb_raw = [keep.tile([P, PACK, N], F32, name="wb_raw%d" % e, tag="wb_h%d" % e, align_bytes=64) for e in range(E)]
-        wb_bf16 = per_expert("wb_bf16", [P, PACK * N], BF16)
+        wb_bf16 = [keep.tile([P, PACK * N], BF16, name="wb_bf16%d" % e, tag="wb_bf16_%d" % e, align_bytes=64) for e in range(E)]
         wb_codes = per_expert("wb_codes", [P, N], U32)
         wb_scales = per_expert("wb_scales", [P, N], U8)
         gates = per_expert("gates", [P, C], F32)
@@ -70,6 +71,8 @@ def tile_moe_elr_gelu_kernel(
         hidden = {}
         banks = {}
         sums = {}
+        h_mx = {}
+        late = {}
         rounded = {}
 
         def slot_list(first, count):
@@ -132,7 +135,10 @@ def tile_moe_elr_gelu_kernel(
         def first_products(e, s):
             if s == 0:
                 for u in range(UNITS):
-                    hidden[e, u] = psum.tile([P, PACK, UNIT], F32, name="h%d%d" % (e, u), tag="h%d" % u)
+                    if u == 0:
+                        hidden[e, u] = psum.tile([P, PACK, UNIT], F32, name="h%d%d" % (e, u), tag="h")
+                    else:
+                        hidden[e, u] = psum_once.tile([P, PACK, UNIT], F32, name="h%d%d" % (e, u), tag="second%d" % e)
             width = P if False else H
             for c0 in range(0, H, width):
                 nc.vector.quantize_mx(
@@ -165,7 +171,10 @@ def tile_moe_elr_gelu_kernel(
 
         def frozen_products(e, u):
             first = e * C + u * UNIT
-            banks[e, u] = psum.tile([P, N_TILES, UNIT], F32, name="y%d%d" % (e, u), tag="y%d" % u)
+            if u == 0:
+                banks[e, u] = psum.tile([P, N_TILES, UNIT], F32, name="y%d%d" % (e, u), tag="y")
+            else:
+                banks[e, u] = psum_once.tile([P, N_TILES, UNIT], F32, name="y%d%d" % (e, u), tag="second%d" % e)
             for s in range(PASSES):
                 for nt in range(N_TILES):
                     nc.tensor.matmul_mx(
@@ -178,7 +187,7 @@ def tile_moe_elr_gelu_kernel(
                         stop=False,
                     )
 
-        def second_products(e, u):
+        def quantise_hidden(e, u):
             if u == 0:
                 rounded[e] = keep.tile([P, UNITS, PACK * UNIT], BF16, name="h_bf16%d" % e, tag="wb_h%d" % e, align_bytes=64)
             h_bf16 = rounded[e][:, u, :]
@@ -190,6 +199,10 @@ def tile_moe_elr_gelu_kernel(
                 func=GELU,
             )
             nc.vector.quantize_mx(out=h_codes[:].bitcast(FP8X4), scales=h_scales[:], in_=h_bf16)
+            h_mx[e, u] = (h_codes, h_scales)
+
+        def second_products(e, u):
+            h_codes, h_scales = h_mx[e, u]
             for nt in range(N_TILES):
                 cols = slice(nt * P, (nt + 1) * P)
                 nc.tensor.matmul_mx(
@@ -206,8 +219,7 @@ def tile_moe_elr_gelu_kernel(
             return u == 0 and e < E - 1
 
         def leave_psum(e, u):
-            tag = "raw%d%d" % (e + 1, PASSES - 1) if (u == UNITS - 1 and e < E - 1) else "sums%d%d" % (e, u)
-            sums[e, u] = keep.tile([P, N_TILES, UNIT], F32, name="sums%d%d" % (e, u), tag=tag, align_bytes=64)
+            sums[e, u] = sbuf("sums%d%d" % (e, u), [P, N_TILES, UNIT], F32)
             if on_vector(e, u):
                 weights = gates[e][:, u * UNIT : (u + 1) * UNIT].unsqueeze(1).to_broadcast([P, N_TILES, UNIT])
                 nc.vector.tensor_tensor(sums[e, u][:], banks[e, u][:], weights, MULT)
@@ -221,6 +233,16 @@ def tile_moe_elr_gelu_kernel(
                     nc.vector.tensor_copy(out=window, in_=sums[e, u][:, nt, :])
                 else:
                     nc.vector.tensor_tensor(window, sums[e, u][:, nt, :], gates[e][:, u * UNIT : (u + 1) * UNIT], MULT)
+
+        def late_rows(e, nt):
+            tag = "raw%d%d" % (e + 1, PASSES - 1) if nt == 0 else "wb_bf16_%d" % (e + 1)
+            late[e, nt] = keep.tile([P, UNIT], F32, name="late%d%d" % (e, nt), tag=tag, align_bytes=64)
+            nc.scalar.copy(out=late[e, nt][:], in_=banks[e, UNITS - 1][:, nt, :])
+
+        def scatter_late(e, nt):
+            u = UNITS - 1
+            window = results[nt][:].indirect(slot_list(e * C + u * UNIT, UNIT))
+            nc.vector.tensor_tensor(window, late[e, nt][:], gates[e][:, u * UNIT : (u + 1) * UNIT], MULT)
 
         nc.vector.memset(token_scales[:].bitcast(I32), 0)
         nc.vector.memset(warm[:, 0:1], 0.0)
@@ -264,16 +286,21 @@ def tile_moe_elr_gelu_kernel(
         for e in range(E):
             round_wa(e, 2)
             if e > 0:
-                leave_psum(e - 1, 1)
+                late_rows(e - 1, 0)
             round_wb(e)
             first_products(e, 2)
             if e > 0:
-                scatter(e - 1, 1)
+                scatter_late(e - 1, 0)
             quantise_wb(e)
-            for u in range(UNITS):
-                frozen_products(e, u)
-            for u in range(UNITS):
-                second_products(e, u)
+            frozen_products(e, 0)
+            quantise_hidden(e, 0)
+            second_products(e, 0)
+            if e > 0:
+                late_rows(e - 1, 1)
+                scatter_late(e - 1, 1)
+            quantise_hidden(e, 1)
+            frozen_products(e, 1)
+            second_products(e, 1)
             leave_psum(e, 0)
             scatter(e, 0)
             if e < E - 1:

@@ -20,14 +20,17 @@ P = 128
 PACK = 4
 K_PASS = P * PACK
 PASSES = K // K_PASS
+LAST_PASS = PASSES - 1
+LAST_EXPERT = E - 1
 UNIT = 128
-UNITS = C // UNIT
 N_TILES = N // P
-QUADS = 4
-ROWS = 4
-GROUPS = H // 16
-MOVED_ROWS = 112
-VECTOR_GROUPS = (0, 12, 20)
+QUADRANT = 32
+QUADRANTS = P // QUADRANT
+SCALE_ROWS = 4
+MOVED_ROWS = QUADRANT * (QUADRANTS - 1) + SCALE_ROWS
+RUN = 2
+GROUPS = H // (PACK * RUN)
+VECTOR_GROUPS = (0, 28, 36)
 
 
 def tile_moe_elr_gelu_kernel(
@@ -39,8 +42,8 @@ def tile_moe_elr_gelu_kernel(
         psum = ctx.enter_context(tc.psum_pool(name="psum", bufs=2))
         psum_once = ctx.enter_context(tc.psum_pool(name="psum_once", bufs=1))
 
-        def sbuf(name, shape, dtype):
-            return keep.tile(shape, dtype, name=name, align_bytes=64)
+        def sbuf(name, shape, dtype, tag=None):
+            return keep.tile(shape, dtype, name=name, tag=tag or name, align_bytes=64)
 
         def per_tile(name, shape, dtype):
             return [[sbuf("%s%d%d" % (name, e, s), shape, dtype) for s in range(PASSES)] for e in range(E)]
@@ -48,11 +51,17 @@ def tile_moe_elr_gelu_kernel(
         def per_expert(name, shape, dtype):
             return [sbuf("%s%d" % (name, e), shape, dtype) for e in range(E)]
 
+        def bank(kind, e, u, width):
+            name = "%s%d%d" % (kind, e, u)
+            if u == 0:
+                return psum.tile([P, width, UNIT], F32, name=name, tag=kind)
+            return psum_once.tile([P, width, UNIT], F32, name=name, tag="second%d" % e)
+
         offsets = keep.tile([P, T // 16], U16, name="offsets")
         token_scales = sbuf("token_scales", [P, T], U8)
         token_words = [sbuf("token_words%d" % s, [P, T], I32) for s in range(PASSES)]
         slot_scales = sbuf("slot_scales", [P, T], U8)
-        planes_at_zero = [slot_scales] + [sbuf("moved%d" % s, [P, T], U8) for s in range(1, PASSES)]
+        scales_from_zero = [slot_scales] + [sbuf("moved%d" % s, [P, T], U8) for s in range(1, PASSES)]
         first_words = [sbuf("first_words%d" % s, [P, C], U32) for s in range(PASSES)]
         later_words = [sbuf("later_words%d" % s, [P, T - C], U32) for s in range(PASSES)]
         frozen_scales = sbuf("frozen_scales", [P, E * PASSES, N], U8)
@@ -60,45 +69,48 @@ def tile_moe_elr_gelu_kernel(
         wa_bf16 = per_tile("wa_bf16", [P, PACK * H], BF16)
         wa_codes = per_tile("wa_codes", [P, H], U32)
         wa_scales = per_tile("wa_scales", [P, H], U8)
-        wb_raw = [keep.tile([P, PACK, N], F32, name="wb_raw%d" % e, tag="wb_h%d" % e, align_bytes=64) for e in range(E)]
-        wb_bf16 = [keep.tile([P, PACK * N], BF16, name="wb_bf16%d" % e, tag="wb_bf16_%d" % e, align_bytes=64) for e in range(E)]
+        wb_raw = [sbuf("wb_raw%d" % e, [P, PACK, N], F32, tag="wb_h%d" % e) for e in range(E)]
+        wb_bf16 = [sbuf("wb_bf16%d" % e, [P, PACK * N], BF16, tag="wb_bf16_%d" % e) for e in range(E)]
         wb_codes = per_expert("wb_codes", [P, N], U32)
         wb_scales = per_expert("wb_scales", [P, N], U8)
         gates = per_expert("gates", [P, C], F32)
         results = [sbuf("results%d" % nt, [P, T], F32) for nt in range(N_TILES)]
         warm = sbuf("warm", [P, 2], F32)
         wa_raw = {}
-        hidden = {}
-        banks = {}
-        sums = {}
+        h_banks = {}
+        y_banks = {}
+        h_bf16 = {}
         h_mx = {}
-        late = {}
-        rounded = {}
+        sums = {}
+        late_sums = {}
 
         def slot_list(first, count):
             return offsets[:, first // 16 : (first + count) // 16]
 
-        def slot_words(e, s, u):
+        def unit_slots(e, u):
+            return slice(e * C + u * UNIT, e * C + (u + 1) * UNIT)
+
+        def unit_words(e, s, u):
             if e == 0:
-                return first_words[s][:, u * UNIT : (u + 1) * UNIT]
-            first = (e - 1) * C + u * UNIT
-            return later_words[s][:, first : first + UNIT]
+                return first_words[s][:, unit_slots(0, u)]
+            return later_words[s][:, unit_slots(e - 1, u)]
 
-        def pieces(e, s):
-            return [(0, GROUPS)]
+        def unit_gate(e, u):
+            return gates[e][:, unit_slots(0, u)]
 
-        def load_wa(e, s, piece):
-            q0, q1 = piece
-            raw = keep.tile([P, PACK, H], F32, name="wa_raw%d%d" % (e, s), tag="raw%d%d" % (e, s), align_bytes=64)
-            wa_raw[e, s, q0] = raw
+        def unit_window(e, u, nt):
+            return results[nt][:].indirect(slot_list(e * C + u * UNIT, UNIT))
+
+        def load_wa(e, s):
+            wa_raw[e, s] = sbuf("wa_raw%d%d" % (e, s), [P, PACK, H], F32, tag="raw%d%d" % (e, s))
             rows = wa[e, s * K_PASS : (s + 1) * K_PASS, :].rearrange("(p j) i -> p j i", j=PACK)
-            nc.sync.dma_start(out=raw[:], in_=rows[:, :, 16 * q0 : 16 * q1])
+            nc.sync.dma_start(out=wa_raw[e, s][:], in_=rows)
 
         def load_words(s):
             nc.sync.dma_start(out=token_words[s][:], in_=x_words[s].rearrange("p t d -> p (t d)").bitcast(I32))
 
         def load_second_stage(e):
-            rows = wb[e].rearrange("(q t r) n -> t q r n", t=PACK, r=4)
+            rows = wb[e].rearrange("(q t r) n -> t q r n", t=PACK, r=RUN)
             for t in range(PACK):
                 nc.sync.dma_start(out=wb_raw[e][:, t, :], in_=rows[t])
             nc.sync.dma_start(
@@ -106,99 +118,86 @@ def tile_moe_elr_gelu_kernel(
             )
             nc.sync.dma_start(out=gates[e][:], in_=gate[:, e * C : (e + 1) * C])
 
-        def gather_words(s, later):
-            dst, first, count = (later_words[s], C, T - C) if later else (first_words[s], 0, C)
-            nc.vector.tensor_copy(out=dst[:], in_=token_words[s][:].bitcast(U32).indirect(slot_list(first, count)))
+        def gather_first_words(s):
+            window = token_words[s][:].bitcast(U32)
+            nc.vector.tensor_copy(out=first_words[s][:], in_=window.indirect(slot_list(0, C)))
 
-        def gather_scales(later):
-            first, count = (C, T - C) if later else (0, C)
+        def gather_later_words(s):
+            window = token_words[s][:].bitcast(U32)
+            nc.vector.tensor_copy(out=later_words[s][:], in_=window.indirect(slot_list(C, T - C)))
+
+        def gather_scales(first, count):
             nc.vector.tensor_copy(
                 out=slot_scales[:, first : first + count], in_=token_scales[:].indirect(slot_list(first, count))
             )
 
-        def move_planes():
+        def move_scales():
             for s in range(1, PASSES):
                 nc.sync.dma_start(
-                    out=planes_at_zero[s][0:MOVED_ROWS, :].bitcast(I32),
-                    in_=slot_scales[ROWS * s : ROWS * s + MOVED_ROWS, :].bitcast(I32),
+                    out=scales_from_zero[s][0:MOVED_ROWS, :].bitcast(I32),
+                    in_=slot_scales[SCALE_ROWS * s : SCALE_ROWS * s + MOVED_ROWS, :].bitcast(I32),
                 )
 
         def round_wa(e, s):
-            dst = wa_bf16[e][s][:].rearrange("p (t q r j) -> p q t j r", t=PACK, r=4, j=PACK)
-            for q0, q1 in pieces(e, s):
-                src = wa_raw[e, s, q0][:].rearrange("p j (q t r) -> p q t j r", t=PACK, r=4)
-                share = VECTOR_GROUPS[s] if (e > 0 or s == PASSES - 1) else 0
-                if share:
-                    nc.vector.tensor_copy(out=dst[:, q0 : q0 + share], in_=src[:, 0:share])
-                nc.scalar.copy(out=dst[:, q0 + share : q1], in_=src[:, share : q1 - q0])
+            dst = wa_bf16[e][s][:].rearrange("p (t q r j) -> p q t j r", t=PACK, r=RUN, j=PACK)
+            src = wa_raw[e, s][:].rearrange("p j (q t r) -> p q t j r", t=PACK, r=RUN)
+            share = VECTOR_GROUPS[s] if (e > 0 or s == LAST_PASS) else 0
+            if share:
+                nc.vector.tensor_copy(out=dst[:, 0:share], in_=src[:, 0:share])
+            nc.scalar.copy(out=dst[:, share:GROUPS], in_=src[:, share:GROUPS])
 
         def first_products(e, s):
             if s == 0:
-                for u in range(UNITS):
-                    if u == 0:
-                        hidden[e, u] = psum.tile([P, PACK, UNIT], F32, name="h%d%d" % (e, u), tag="h")
-                    else:
-                        hidden[e, u] = psum_once.tile([P, PACK, UNIT], F32, name="h%d%d" % (e, u), tag="second%d" % e)
-            width = P if False else H
-            for c0 in range(0, H, width):
-                nc.vector.quantize_mx(
-                    out=wa_codes[e][s][:, c0 : c0 + width].bitcast(FP8X4),
-                    scales=wa_scales[e][s][:, c0 : c0 + width],
-                    in_=wa_bf16[e][s][:, PACK * c0 : PACK * (c0 + width)],
-                )
-            for u in range(UNITS):
-                first = e * C + u * UNIT
+                for u in range(2):
+                    h_banks[e, u] = bank("h", e, u, PACK)
+            nc.vector.quantize_mx(out=wa_codes[e][s][:].bitcast(FP8X4), scales=wa_scales[e][s][:], in_=wa_bf16[e][s][:])
+            for u in range(2):
                 for t in range(PACK):
                     cols = slice(t * P, (t + 1) * P)
                     nc.tensor.matmul_mx(
-                        out=hidden[e, u][:, t, :],
+                        out=h_banks[e, u][:, t, :],
                         lhsT=wa_codes[e][s][:, cols].bitcast(FP8X4),
                         lhsT_scale=wa_scales[e][s][:, cols],
-                        rhs=slot_words(e, s, u).bitcast(FP8X4),
-                        rhs_scale=slot_scales[ROWS * s :, first : first + UNIT],
+                        rhs=unit_words(e, s, u).bitcast(FP8X4),
+                        rhs_scale=slot_scales[SCALE_ROWS * s :, unit_slots(e, u)],
                         start=(s == 0 and t == 0),
-                        stop=(s == PASSES - 1 and t == PACK - 1),
+                        stop=(s == LAST_PASS and t == PACK - 1),
                     )
 
         def round_wb(e):
             nc.scalar.copy(
-                out=wb_bf16[e][:].rearrange("p (c i j) -> p c j i", i=4, j=PACK),
-                in_=wb_raw[e][:].rearrange("p j (c i) -> p c j i", i=4),
+                out=wb_bf16[e][:].rearrange("p (c r j) -> p c j r", r=RUN, j=PACK),
+                in_=wb_raw[e][:].rearrange("p j (c r) -> p c j r", r=RUN),
             )
 
         def quantise_wb(e):
             nc.vector.quantize_mx(out=wb_codes[e][:].bitcast(FP8X4), scales=wb_scales[e][:], in_=wb_bf16[e][:])
 
         def frozen_products(e, u):
-            first = e * C + u * UNIT
-            if u == 0:
-                banks[e, u] = psum.tile([P, N_TILES, UNIT], F32, name="y%d%d" % (e, u), tag="y")
-            else:
-                banks[e, u] = psum_once.tile([P, N_TILES, UNIT], F32, name="y%d%d" % (e, u), tag="second%d" % e)
+            y_banks[e, u] = bank("y", e, u, N_TILES)
             for s in range(PASSES):
                 for nt in range(N_TILES):
                     nc.tensor.matmul_mx(
-                        out=banks[e, u][:, nt, :],
+                        out=y_banks[e, u][:, nt, :],
                         lhsT=frozen_words[e][:, s, 2 * P * nt : 2 * P * (nt + 1)].bitcast(FP4X4),
                         lhsT_scale=frozen_scales[:, e * PASSES + s, P * nt : P * (nt + 1)],
-                        rhs=slot_words(e, s, u).bitcast(FP8X4),
-                        rhs_scale=planes_at_zero[s][:, first : first + UNIT],
+                        rhs=unit_words(e, s, u).bitcast(FP8X4),
+                        rhs_scale=scales_from_zero[s][:, unit_slots(e, u)],
                         start=(s == 0 and nt == 0),
                         stop=False,
                     )
 
         def quantise_hidden(e, u):
             if u == 0:
-                rounded[e] = keep.tile([P, UNITS, PACK * UNIT], BF16, name="h_bf16%d" % e, tag="wb_h%d" % e, align_bytes=64)
-            h_bf16 = rounded[e][:, u, :]
+                h_bf16[e] = sbuf("h_bf16%d" % e, [P, 2, PACK * UNIT], BF16, tag="wb_h%d" % e)
             h_codes = sbuf("h_codes%d%d" % (e, u), [P, UNIT], U32)
             h_scales = sbuf("h_scales%d%d" % (e, u), [P, UNIT], U8)
             nc.scalar.activation(
-                out=h_bf16.rearrange("p (u t) -> p u t", t=PACK),
-                in_=hidden[e, u][:].rearrange("p t u -> p u t"),
+                out=h_bf16[e][:, u, :].rearrange("p (c t) -> p c t", t=PACK),
+                in_=h_banks[e, u][:].rearrange("p t c -> p c t"),
                 func=GELU,
             )
-            nc.vector.quantize_mx(out=h_codes[:].bitcast(FP8X4), scales=h_scales[:], in_=h_bf16)
+            nc.vector.quantize_mx(out=h_codes[:].bitcast(FP8X4), scales=h_scales[:], in_=h_bf16[e][:, u, :])
             h_mx[e, u] = (h_codes, h_scales)
 
         def second_products(e, u):
@@ -206,7 +205,7 @@ def tile_moe_elr_gelu_kernel(
             for nt in range(N_TILES):
                 cols = slice(nt * P, (nt + 1) * P)
                 nc.tensor.matmul_mx(
-                    out=banks[e, u][:, nt, :],
+                    out=y_banks[e, u][:, nt, :],
                     lhsT=wb_codes[e][:, cols].bitcast(FP8X4),
                     lhsT_scale=wb_scales[e][:, cols],
                     rhs=h_codes[:].bitcast(FP8X4),
@@ -215,80 +214,73 @@ def tile_moe_elr_gelu_kernel(
                     stop=(nt == N_TILES - 1),
                 )
 
-        def on_vector(e, u):
-            return u == 0 and e < E - 1
-
-        def leave_psum(e, u):
-            sums[e, u] = sbuf("sums%d%d" % (e, u), [P, N_TILES, UNIT], F32)
-            if on_vector(e, u):
-                weights = gates[e][:, u * UNIT : (u + 1) * UNIT].unsqueeze(1).to_broadcast([P, N_TILES, UNIT])
-                nc.vector.tensor_tensor(sums[e, u][:], banks[e, u][:], weights, MULT)
-            else:
-                nc.scalar.copy(out=sums[e, u][:], in_=banks[e, u][:])
-
-        def scatter(e, u):
+        def return_by_vector(e):
+            sums[e, 0] = sbuf("sums%d0" % e, [P, N_TILES, UNIT], F32)
+            weights = unit_gate(e, 0).unsqueeze(1).to_broadcast([P, N_TILES, UNIT])
+            nc.vector.tensor_tensor(sums[e, 0][:], y_banks[e, 0][:], weights, MULT)
             for nt in range(N_TILES):
-                window = results[nt][:].indirect(slot_list(e * C + u * UNIT, UNIT))
-                if on_vector(e, u):
-                    nc.vector.tensor_copy(out=window, in_=sums[e, u][:, nt, :])
-                else:
-                    nc.vector.tensor_tensor(window, sums[e, u][:, nt, :], gates[e][:, u * UNIT : (u + 1) * UNIT], MULT)
+                nc.vector.tensor_copy(out=unit_window(e, 0, nt), in_=sums[e, 0][:, nt, :])
 
-        def late_rows(e, nt):
-            tag = "raw%d%d" % (e + 1, PASSES - 1) if nt == 0 else "wb_bf16_%d" % (e + 1)
-            late[e, nt] = keep.tile([P, UNIT], F32, name="late%d%d" % (e, nt), tag=tag, align_bytes=64)
-            nc.scalar.copy(out=late[e, nt][:], in_=banks[e, UNITS - 1][:, nt, :])
+        def return_by_scalar(e, u):
+            sums[e, u] = sbuf("sums%d%d" % (e, u), [P, N_TILES, UNIT], F32)
+            nc.scalar.copy(out=sums[e, u][:], in_=y_banks[e, u][:])
+            for nt in range(N_TILES):
+                nc.vector.tensor_tensor(unit_window(e, u, nt), sums[e, u][:, nt, :], unit_gate(e, u), MULT)
+
+        def copy_late(e, nt):
+            tag = "raw%d%d" % (e + 1, LAST_PASS) if nt == 0 else "wb_bf16_%d" % (e + 1)
+            late_sums[e, nt] = sbuf("late%d%d" % (e, nt), [P, UNIT], F32, tag=tag)
+            nc.scalar.copy(out=late_sums[e, nt][:], in_=y_banks[e, 1][:, nt, :])
 
         def scatter_late(e, nt):
-            u = UNITS - 1
-            window = results[nt][:].indirect(slot_list(e * C + u * UNIT, UNIT))
-            nc.vector.tensor_tensor(window, late[e, nt][:], gates[e][:, u * UNIT : (u + 1) * UNIT], MULT)
+            nc.vector.tensor_tensor(unit_window(e, 1, nt), late_sums[e, nt][:], unit_gate(e, 1), MULT)
 
         nc.vector.memset(token_scales[:].bitcast(I32), 0)
         nc.vector.memset(warm[:, 0:1], 0.0)
         nc.vector.memset(frozen_scales[:].rearrange("p g n -> p (g n)").bitcast(I32), 0)
         for s in range(1, PASSES):
-            nc.vector.memset(planes_at_zero[s][:].bitcast(I32), 0)
+            nc.vector.memset(scales_from_zero[s][:].bitcast(I32), 0)
 
-        for q in range(QUADS):
+        for q in range(QUADRANTS):
             nc.scalar.dma_start(
-                out=token_scales[32 * q : 32 * q + ROWS * PASSES, :].bitcast(I32),
-                in_=x_scales[:, ROWS * q : ROWS * (q + 1), :].bitcast(I32),
+                out=token_scales[QUADRANT * q : QUADRANT * q + SCALE_ROWS * PASSES, :].bitcast(I32),
+                in_=x_scales[:, SCALE_ROWS * q : SCALE_ROWS * (q + 1), :].bitcast(I32),
             )
         nc.scalar.activation(out=warm[:, 1:2], in_=warm[:, 0:1], func=GELU)
-        for r in range(ROWS):
-            rows = w_scales.rearrange("e s (q r) n -> r q (e s) n", r=ROWS)[r]
-            nc.gpsimd.dma_start(out=frozen_scales[r:P:32, :, :].bitcast(I32), in_=rows.bitcast(I32))
+        for r in range(SCALE_ROWS):
+            rows = w_scales.rearrange("e s (q r) n -> r q (e s) n", r=SCALE_ROWS)[r]
+            nc.gpsimd.dma_start(out=frozen_scales[r:P:QUADRANT, :, :].bitcast(I32), in_=rows.bitcast(I32))
+
         load_words(0)
         nc.sync.dma_start(offsets[:], offs)
         load_words(1)
-        load_wa(0, 0, pieces(0, 0)[0])
-        load_wa(0, 1, pieces(0, 1)[0])
+        load_wa(0, 0)
+        load_wa(0, 1)
         load_words(2)
-        load_wa(0, 2, pieces(0, 2)[0])
+        load_wa(0, 2)
 
-        gather_words(0, False)
-        gather_scales(False)
-        gather_words(0, True)
-        gather_scales(True)
+        gather_first_words(0)
+        gather_scales(0, C)
+        gather_later_words(0)
+        gather_scales(C, T - C)
         load_second_stage(0)
-        move_planes()
+        move_scales()
         for e in range(1, E):
             for s in range(PASSES):
-                load_wa(e, s, pieces(e, s)[0])
+                load_wa(e, s)
             load_second_stage(e)
-        for s in range(PASSES - 1):
+        for s in range(LAST_PASS):
             round_wa(0, s)
-            gather_words(s + 1, False)
+            gather_first_words(s + 1)
             first_products(0, s)
-            gather_words(s + 1, True)
+            gather_later_words(s + 1)
 
         for e in range(E):
-            round_wa(e, 2)
+            round_wa(e, LAST_PASS)
             if e > 0:
-                late_rows(e - 1, 0)
+                copy_late(e - 1, 0)
             round_wb(e)
-            first_products(e, 2)
+            first_products(e, LAST_PASS)
             if e > 0:
                 scatter_late(e - 1, 0)
             quantise_wb(e)
@@ -296,19 +288,18 @@ def tile_moe_elr_gelu_kernel(
             quantise_hidden(e, 0)
             second_products(e, 0)
             if e > 0:
-                late_rows(e - 1, 1)
+                copy_late(e - 1, 1)
                 scatter_late(e - 1, 1)
             quantise_hidden(e, 1)
             frozen_products(e, 1)
             second_products(e, 1)
-            leave_psum(e, 0)
-            scatter(e, 0)
-            if e < E - 1:
-                for s in range(PASSES - 1):
+            if e < LAST_EXPERT:
+                return_by_vector(e)
+                for s in range(LAST_PASS):
                     round_wa(e + 1, s)
                     first_products(e + 1, s)
-        leave_psum(E - 1, 1)
-        scatter(E - 1, 1)
+        for u in range(2):
+            return_by_scalar(LAST_EXPERT, u)
 
         for nt in range(N_TILES):
             nc.sync.dma_start(out=out[nt * P : (nt + 1) * P, :], in_=results[nt][:])

@@ -29,8 +29,8 @@ QUADRANTS = P // QUADRANT
 SCALE_ROWS = 4
 MOVED_ROWS = QUADRANT * (QUADRANTS - 1) + SCALE_ROWS
 RUN = 2
-GROUPS = H // (PACK * RUN)
-VECTOR_GROUPS = (0, 28, 36)
+VECTOR_GROUPS = (0, 48)
+HALF = PACK // 2
 
 
 def tile_moe_elr_gelu_kernel(
@@ -51,8 +51,8 @@ def tile_moe_elr_gelu_kernel(
         def per_expert(name, shape, dtype):
             return [sbuf("%s%d" % (name, e), shape, dtype) for e in range(E)]
 
-        def bank(kind, e, u, width):
-            name = "%s%d%d" % (kind, e, u)
+        def bank(kind, e, u, width, nt=0):
+            name = "%s%d%d%d" % (kind, e, u, nt)
             if u == 0:
                 return psum.tile([P, width, UNIT], F32, name=name, tag=kind)
             return psum_once.tile([P, width, UNIT], F32, name=name, tag="second%d" % e)
@@ -69,16 +69,19 @@ def tile_moe_elr_gelu_kernel(
         wa_bf16 = per_tile("wa_bf16", [P, PACK * H], BF16)
         wa_codes = per_tile("wa_codes", [P, H], U32)
         wa_scales = per_tile("wa_scales", [P, H], U8)
-        wb_raw = [sbuf("wb_raw%d" % e, [P, PACK, N], F32, tag="wb_h%d" % e) for e in range(E)]
+        wb_raw = [sbuf("wb_raw%d" % e, [P, PACK, N], F32, tag="wb_raw%d" % e) for e in range(E)]
         wb_bf16 = [sbuf("wb_bf16%d" % e, [P, PACK * N], BF16, tag="wb_bf16_%d" % e) for e in range(E)]
         wb_codes = per_expert("wb_codes", [P, N], U32)
         wb_scales = per_expert("wb_scales", [P, N], U8)
-        gates = per_expert("gates", [P, C], F32)
+        gate_ends = [e * C + UNIT for e in range(LAST_EXPERT)] + [T]
+        gate_starts = [0] + gate_ends[:-1]
+        gates = [sbuf("gates%d" % e, [P, gate_ends[e] - gate_starts[e]], F32) for e in range(E)]
         results = [sbuf("results%d" % nt, [P, T], F32) for nt in range(N_TILES)]
         warm = sbuf("warm", [P, 2], F32)
         wa_raw = {}
         h_banks = {}
         y_banks = {}
+        y_tiles = {}
         h_bf16 = {}
         h_mx = {}
         sums = {}
@@ -96,7 +99,9 @@ def tile_moe_elr_gelu_kernel(
             return later_words[s][:, unit_slots(e - 1, u)]
 
         def unit_gate(e, u):
-            return gates[e][:, unit_slots(0, u)]
+            load = min(e + u, LAST_EXPERT)
+            first = e * C + u * UNIT - gate_starts[load]
+            return gates[load][:, first : first + UNIT]
 
         def unit_window(e, u, nt):
             return results[nt][:].indirect(slot_list(e * C + u * UNIT, UNIT))
@@ -110,13 +115,11 @@ def tile_moe_elr_gelu_kernel(
             nc.sync.dma_start(out=token_words[s][:], in_=x_words[s].rearrange("p t d -> p (t d)").bitcast(I32))
 
         def load_second_stage(e):
-            rows = wb[e].rearrange("(q t r) n -> t q r n", t=PACK, r=RUN)
-            for t in range(PACK):
-                nc.sync.dma_start(out=wb_raw[e][:, t, :], in_=rows[t])
+            nc.sync.dma_start(out=wb_raw[e][:], in_=wb[e].rearrange("(p t) n -> p t n", t=PACK))
+            nc.sync.dma_start(out=gates[e][:], in_=gate[:, gate_starts[e] : gate_ends[e]])
             nc.sync.dma_start(
                 out=frozen_words[e][:].bitcast(I32), in_=w_words[e].rearrange("s p b -> p s b").bitcast(I32)
             )
-            nc.sync.dma_start(out=gates[e][:], in_=gate[:, e * C : (e + 1) * C])
 
         def gather_first_words(s):
             window = token_words[s][:].bitcast(U32)
@@ -139,18 +142,29 @@ def tile_moe_elr_gelu_kernel(
                 )
 
         def round_wa(e, s):
-            dst = wa_bf16[e][s][:].rearrange("p (t q r j) -> p q t j r", t=PACK, r=RUN, j=PACK)
-            src = wa_raw[e, s][:].rearrange("p j (q t r) -> p q t j r", t=PACK, r=RUN)
-            share = VECTOR_GROUPS[s] if (e > 0 or s == LAST_PASS) else 0
-            if share:
-                nc.vector.tensor_copy(out=dst[:, 0:share], in_=src[:, 0:share])
-            nc.scalar.copy(out=dst[:, share:GROUPS], in_=src[:, share:GROUPS])
+            dst = wa_bf16[e][s][:].rearrange("p (t m j) -> p m j t", t=PACK, j=PACK)
+            src = wa_raw[e, s][:].rearrange("p j (m t) -> p m j t", t=PACK)
+            if s == LAST_PASS:
+                nc.vector.tensor_copy(out=dst[:, :, :, 0:HALF], in_=src[:, :, :, 0:HALF])
+                nc.scalar.copy(out=dst[:, :, :, HALF:PACK], in_=src[:, :, :, HALF:PACK])
+                return
+            share = VECTOR_GROUPS[s] if e > 0 else 0
+            for t in range(0, PACK, HALF):
+                if share:
+                    nc.vector.tensor_copy(out=dst[:, 0:share, :, t : t + HALF], in_=src[:, 0:share, :, t : t + HALF])
+                nc.scalar.copy(out=dst[:, share:P, :, t : t + HALF], in_=src[:, share:P, :, t : t + HALF])
 
         def first_products(e, s):
             if s == 0:
                 for u in range(2):
                     h_banks[e, u] = bank("h", e, u, PACK)
-            nc.vector.quantize_mx(out=wa_codes[e][s][:].bitcast(FP8X4), scales=wa_scales[e][s][:], in_=wa_bf16[e][s][:])
+            width = HALF * P if s == LAST_PASS else H
+            for first in range(0, H, width):
+                nc.vector.quantize_mx(
+                    out=wa_codes[e][s][:, first : first + width].bitcast(FP8X4),
+                    scales=wa_scales[e][s][:, first : first + width],
+                    in_=wa_bf16[e][s][:, PACK * first : PACK * (first + width)],
+                )
             for u in range(2):
                 for t in range(PACK):
                     cols = slice(t * P, (t + 1) * P)
@@ -174,22 +188,27 @@ def tile_moe_elr_gelu_kernel(
             nc.vector.quantize_mx(out=wb_codes[e][:].bitcast(FP8X4), scales=wb_scales[e][:], in_=wb_bf16[e][:])
 
         def frozen_products(e, u):
-            y_banks[e, u] = bank("y", e, u, N_TILES)
-            for s in range(PASSES):
-                for nt in range(N_TILES):
+            apart = e == LAST_EXPERT and u == 0
+            if apart:
+                y_tiles[e, u] = [bank("y", e, u, 1, nt)[:, 0, :] for nt in range(N_TILES)]
+            else:
+                y_banks[e, u] = bank("y", e, u, N_TILES)
+                y_tiles[e, u] = [y_banks[e, u][:, nt, :] for nt in range(N_TILES)]
+            for nt in range(N_TILES):
+                for s in range(PASSES):
                     nc.tensor.matmul_mx(
-                        out=y_banks[e, u][:, nt, :],
+                        out=y_tiles[e, u][nt],
                         lhsT=frozen_words[e][:, s, 2 * P * nt : 2 * P * (nt + 1)].bitcast(FP4X4),
                         lhsT_scale=frozen_scales[:, e * PASSES + s, P * nt : P * (nt + 1)],
                         rhs=unit_words(e, s, u).bitcast(FP8X4),
                         rhs_scale=scales_from_zero[s][:, unit_slots(e, u)],
-                        start=(s == 0 and nt == 0),
+                        start=(s == 0 and (nt == 0 or apart)),
                         stop=False,
                     )
 
         def quantise_hidden(e, u):
             if u == 0:
-                h_bf16[e] = sbuf("h_bf16%d" % e, [P, 2, PACK * UNIT], BF16, tag="wb_h%d" % e)
+                h_bf16[e] = sbuf("h_bf16%d" % e, [P, 2, PACK * UNIT], BF16)
             h_codes = sbuf("h_codes%d%d" % (e, u), [P, UNIT], U32)
             h_scales = sbuf("h_scales%d%d" % (e, u), [P, UNIT], U8)
             nc.scalar.activation(
@@ -205,13 +224,13 @@ def tile_moe_elr_gelu_kernel(
             for nt in range(N_TILES):
                 cols = slice(nt * P, (nt + 1) * P)
                 nc.tensor.matmul_mx(
-                    out=y_banks[e, u][:, nt, :],
+                    out=y_tiles[e, u][nt],
                     lhsT=wb_codes[e][:, cols].bitcast(FP8X4),
                     lhsT_scale=wb_scales[e][:, cols],
                     rhs=h_codes[:].bitcast(FP8X4),
                     rhs_scale=h_scales[:],
                     start=False,
-                    stop=(nt == N_TILES - 1),
+                    stop=(nt == N_TILES - 1 or (e == LAST_EXPERT and u == 0)),
                 )
 
         def return_by_vector(e):
@@ -223,12 +242,12 @@ def tile_moe_elr_gelu_kernel(
 
         def return_by_scalar(e, u):
             sums[e, u] = sbuf("sums%d%d" % (e, u), [P, N_TILES, UNIT], F32)
-            nc.scalar.copy(out=sums[e, u][:], in_=y_banks[e, u][:])
             for nt in range(N_TILES):
+                nc.scalar.copy(out=sums[e, u][:, nt, :], in_=y_tiles[e, u][nt])
                 nc.vector.tensor_tensor(unit_window(e, u, nt), sums[e, u][:, nt, :], unit_gate(e, u), MULT)
 
         def copy_late(e, nt):
-            tag = "raw%d%d" % (e + 1, LAST_PASS) if nt == 0 else "wb_bf16_%d" % (e + 1)
+            tag = "wa_bf16%d0" % (e + 1) if nt == 0 else "wb_raw%d" % (e + 1)
             late_sums[e, nt] = sbuf("late%d%d" % (e, nt), [P, UNIT], F32, tag=tag)
             nc.scalar.copy(out=late_sums[e, nt][:], in_=y_banks[e, 1][:, nt, :])
 
@@ -277,8 +296,6 @@ def tile_moe_elr_gelu_kernel(
 
         for e in range(E):
             round_wa(e, LAST_PASS)
-            if e > 0:
-                copy_late(e - 1, 0)
             round_wb(e)
             first_products(e, LAST_PASS)
             if e > 0:
@@ -298,6 +315,7 @@ def tile_moe_elr_gelu_kernel(
                 for s in range(LAST_PASS):
                     round_wa(e + 1, s)
                     first_products(e + 1, s)
+                copy_late(e, 0)
         for u in range(2):
             return_by_scalar(LAST_EXPERT, u)
 

@@ -29,7 +29,7 @@ QUADRANTS = P // QUADRANT
 SCALE_ROWS = 4
 MOVED_ROWS = QUADRANT * (QUADRANTS - 1) + SCALE_ROWS
 RUN = 2
-VECTOR_GROUPS = (0, 48)
+MIDDLE_SHARE = 96
 HALF = PACK // 2
 
 
@@ -114,9 +114,13 @@ def tile_moe_elr_gelu_kernel(
         def load_words(s):
             nc.sync.dma_start(out=token_words[s][:], in_=x_words[s].rearrange("p t d -> p (t d)").bitcast(I32))
 
-        def load_second_stage(e):
+        def load_wb(e):
             nc.sync.dma_start(out=wb_raw[e][:], in_=wb[e].rearrange("(p t) n -> p t n", t=PACK))
+
+        def load_gate(e):
             nc.sync.dma_start(out=gates[e][:], in_=gate[:, gate_starts[e] : gate_ends[e]])
+
+        def load_frozen(e):
             nc.sync.dma_start(
                 out=frozen_words[e][:].bitcast(I32), in_=w_words[e].rearrange("s p b -> p s b").bitcast(I32)
             )
@@ -148,17 +152,17 @@ def tile_moe_elr_gelu_kernel(
                 nc.vector.tensor_copy(out=dst[:, :, :, 0:HALF], in_=src[:, :, :, 0:HALF])
                 nc.scalar.copy(out=dst[:, :, :, HALF:PACK], in_=src[:, :, :, HALF:PACK])
                 return
-            share = VECTOR_GROUPS[s] if e > 0 else 0
-            for t in range(0, PACK, HALF):
-                if share:
-                    nc.vector.tensor_copy(out=dst[:, 0:share, :, t : t + HALF], in_=src[:, 0:share, :, t : t + HALF])
-                nc.scalar.copy(out=dst[:, share:P, :, t : t + HALF], in_=src[:, share:P, :, t : t + HALF])
+            share = MIDDLE_SHARE if (e > 0 and s > 0) else 0
+            if share:
+                nc.vector.tensor_copy(out=dst[:, 0:share, :, HALF:PACK], in_=src[:, 0:share, :, HALF:PACK])
+            nc.scalar.copy(out=dst[:, :, :, 0:HALF], in_=src[:, :, :, 0:HALF])
+            nc.scalar.copy(out=dst[:, share:P, :, HALF:PACK], in_=src[:, share:P, :, HALF:PACK])
 
         def first_products(e, s):
             if s == 0:
                 for u in range(2):
                     h_banks[e, u] = bank("h", e, u, PACK)
-            width = HALF * P if s == LAST_PASS else H
+            width = HALF * P
             for first in range(0, H, width):
                 nc.vector.quantize_mx(
                     out=wa_codes[e][s][:, first : first + width].bitcast(FP8X4),
@@ -166,7 +170,8 @@ def tile_moe_elr_gelu_kernel(
                     in_=wa_bf16[e][s][:, PACK * first : PACK * (first + width)],
                 )
             for u in range(2):
-                for t in range(PACK):
+                for step in range(PACK):
+                    t = (step + HALF * u) % PACK if s == LAST_PASS else step
                     cols = slice(t * P, (t + 1) * P)
                     nc.tensor.matmul_mx(
                         out=h_banks[e, u][:, t, :],
@@ -174,8 +179,8 @@ def tile_moe_elr_gelu_kernel(
                         lhsT_scale=wa_scales[e][s][:, cols],
                         rhs=unit_words(e, s, u).bitcast(FP8X4),
                         rhs_scale=slot_scales[SCALE_ROWS * s :, unit_slots(e, u)],
-                        start=(s == 0 and t == 0),
-                        stop=(s == LAST_PASS and t == PACK - 1),
+                        start=(s == 0 and step == 0),
+                        stop=(s == LAST_PASS and step == PACK - 1),
                     )
 
         def round_wb(e):
@@ -235,8 +240,8 @@ def tile_moe_elr_gelu_kernel(
 
         def return_by_vector(e):
             sums[e, 0] = sbuf("sums%d0" % e, [P, N_TILES, UNIT], F32)
-            weights = unit_gate(e, 0).unsqueeze(1).to_broadcast([P, N_TILES, UNIT])
-            nc.vector.tensor_tensor(sums[e, 0][:], y_banks[e, 0][:], weights, MULT)
+            for nt in range(N_TILES):
+                nc.vector.tensor_tensor(sums[e, 0][:, nt, :], y_banks[e, 0][:, nt, :], unit_gate(e, 0), MULT)
             for nt in range(N_TILES):
                 nc.vector.tensor_copy(out=unit_window(e, 0, nt), in_=sums[e, 0][:, nt, :])
 
@@ -282,12 +287,16 @@ def tile_moe_elr_gelu_kernel(
         gather_scales(0, C)
         gather_later_words(0)
         gather_scales(C, T - C)
-        load_second_stage(0)
+        load_wb(0)
         move_scales()
+        load_frozen(0)
+        load_gate(0)
         for e in range(1, E):
             for s in range(PASSES):
                 load_wa(e, s)
-            load_second_stage(e)
+            load_wb(e)
+            load_gate(e)
+            load_frozen(e)
         for s in range(LAST_PASS):
             round_wa(0, s)
             gather_first_words(s + 1)

@@ -29,7 +29,7 @@ QUADRANTS = P // QUADRANT
 SCALE_ROWS = 4
 MOVED_ROWS = QUADRANT * (QUADRANTS - 1) + SCALE_ROWS
 RUN = 2
-MIDDLE_SHARE = 96
+MIDDLE_SHARE = 80
 HALF = PACK // 2
 
 
@@ -73,9 +73,9 @@ def tile_moe_elr_gelu_kernel(
         wb_bf16 = [sbuf("wb_bf16%d" % e, [P, PACK * N], BF16, tag="wb_bf16_%d" % e) for e in range(E)]
         wb_codes = per_expert("wb_codes", [P, N], U32)
         wb_scales = per_expert("wb_scales", [P, N], U8)
-        gate_ends = [e * C + UNIT for e in range(LAST_EXPERT)] + [T]
+        gate_ends = [e * C + UNIT for e in range(LAST_EXPERT)] + [LAST_EXPERT * C, T]
         gate_starts = [0] + gate_ends[:-1]
-        gates = [sbuf("gates%d" % e, [P, gate_ends[e] - gate_starts[e]], F32) for e in range(E)]
+        gates = [sbuf("gates%d" % e, [P, gate_ends[e] - gate_starts[e]], F32) for e in range(E + 1)]
         results = [sbuf("results%d" % nt, [P, T], F32) for nt in range(N_TILES)]
         warm = sbuf("warm", [P, 2], F32)
         wa_raw = {}
@@ -99,7 +99,7 @@ def tile_moe_elr_gelu_kernel(
             return later_words[s][:, unit_slots(e - 1, u)]
 
         def unit_gate(e, u):
-            load = min(e + u, LAST_EXPERT)
+            load = E if e == LAST_EXPERT else e + u
             first = e * C + u * UNIT - gate_starts[load]
             return gates[load][:, first : first + UNIT]
 
@@ -140,7 +140,7 @@ def tile_moe_elr_gelu_kernel(
 
         def move_scales():
             for s in range(1, PASSES):
-                nc.sync.dma_start(
+                nc.gpsimd.dma_start(
                     out=scales_from_zero[s][0:MOVED_ROWS, :].bitcast(I32),
                     in_=slot_scales[SCALE_ROWS * s : SCALE_ROWS * s + MOVED_ROWS, :].bitcast(I32),
                 )
@@ -162,7 +162,8 @@ def tile_moe_elr_gelu_kernel(
             if s == 0:
                 for u in range(2):
                     h_banks[e, u] = bank("h", e, u, PACK)
-            width = HALF * P
+            halves = s == LAST_PASS and e in (0, LAST_EXPERT)
+            width = HALF * P if halves else H
             for first in range(0, H, width):
                 nc.vector.quantize_mx(
                     out=wa_codes[e][s][:, first : first + width].bitcast(FP8X4),
@@ -171,7 +172,7 @@ def tile_moe_elr_gelu_kernel(
                 )
             for u in range(2):
                 for step in range(PACK):
-                    t = (step + HALF * u) % PACK if s == LAST_PASS else step
+                    t = (step + HALF * u) % PACK if halves else step
                     cols = slice(t * P, (t + 1) * P)
                     nc.tensor.matmul_mx(
                         out=h_banks[e, u][:, t, :],
@@ -297,6 +298,7 @@ def tile_moe_elr_gelu_kernel(
             load_wb(e)
             load_gate(e)
             load_frozen(e)
+        load_gate(E)
         for s in range(LAST_PASS):
             round_wa(0, s)
             gather_first_words(s + 1)

@@ -29,8 +29,9 @@ QUADRANTS = P // QUADRANT
 SCALE_ROWS = 4
 MOVED_ROWS = QUADRANT * (QUADRANTS - 1) + SCALE_ROWS
 RUN = 2
-MIDDLE_SHARE = 80
 HALF = PACK // 2
+VERY_FIRST_SHARE = 32
+MIDDLE_SHARE = 96
 
 
 def tile_moe_elr_gelu_kernel(
@@ -45,9 +46,6 @@ def tile_moe_elr_gelu_kernel(
         def sbuf(name, shape, dtype, tag=None):
             return keep.tile(shape, dtype, name=name, tag=tag or name, align_bytes=64)
 
-        def per_tile(name, shape, dtype):
-            return [[sbuf("%s%d%d" % (name, e, s), shape, dtype) for s in range(PASSES)] for e in range(E)]
-
         def per_expert(name, shape, dtype):
             return [sbuf("%s%d" % (name, e), shape, dtype) for e in range(E)]
 
@@ -60,17 +58,32 @@ def tile_moe_elr_gelu_kernel(
         offsets = keep.tile([P, T // 16], U16, name="offsets")
         token_scales = sbuf("token_scales", [P, T], U8)
         token_words = [sbuf("token_words%d" % s, [P, T], I32) for s in range(PASSES)]
-        slot_scales = sbuf("slot_scales", [P, T], U8)
-        scales_from_zero = [slot_scales] + [sbuf("moved%d" % s, [P, T], U8) for s in range(1, PASSES)]
+        scales_from_zero = {s: sbuf("moved%d" % s, [P, T], U8) for s in range(1, PASSES)}
         first_words = [sbuf("first_words%d" % s, [P, C], U32) for s in range(PASSES)]
         later_words = [sbuf("later_words%d" % s, [P, T - C], U32) for s in range(PASSES)]
-        frozen_scales = sbuf("frozen_scales", [P, E * PASSES, N], U8)
+        frozen_scales = per_expert("frozen_scales", [P, PASSES, N], U8)
         frozen_words = per_expert("frozen_words", [P, PASSES, 2 * N], U8)
-        wa_bf16 = per_tile("wa_bf16", [P, PACK * H], BF16)
-        wa_codes = per_tile("wa_codes", [P, H], U32)
-        wa_scales = per_tile("wa_scales", [P, H], U8)
-        wb_raw = [sbuf("wb_raw%d" % e, [P, PACK, N], F32, tag="wb_raw%d" % e) for e in range(E)]
-        wb_bf16 = [sbuf("wb_bf16%d" % e, [P, PACK * N], BF16, tag="wb_bf16_%d" % e) for e in range(E)]
+        wa_bf16 = {}
+        wa_codes = {}
+        wa_scales = {}
+        joint = {}
+        for e in range(E):
+            for s in range(PASSES if e == 0 else 1):
+                wa_bf16[e, s] = sbuf("wa_bf16%d%d" % (e, s), [P, PACK * H], BF16)
+                wa_codes[e, s] = sbuf("wa_codes%d%d" % (e, s), [P, H], U32)
+                wa_scales[e, s] = sbuf("wa_scales%d%d" % (e, s), [P, H], U8)
+        for e in range(1, E):
+            joint[e] = (
+                sbuf("joint_codes%d" % e, [P, 2 * H], U32),
+                sbuf("joint_scales%d" % e, [P, 2 * H], U8),
+                sbuf("joint_bf16%d" % e, [P, 2 * PACK * H], BF16),
+            )
+            for s in range(1, PASSES):
+                wa_codes[e, s] = joint[e][0][:, (s - 1) * H : s * H]
+                wa_scales[e, s] = joint[e][1][:, (s - 1) * H : s * H]
+                wa_bf16[e, s] = joint[e][2][:, (s - 1) * PACK * H : s * PACK * H]
+        wb_raw = per_expert("wb_raw", [P, PACK, N], F32)
+        wb_bf16 = per_expert("wb_bf16_", [P, PACK * N], BF16)
         wb_codes = per_expert("wb_codes", [P, N], U32)
         wb_scales = per_expert("wb_scales", [P, N], U8)
         gate_ends = [e * C + UNIT for e in range(LAST_EXPERT)] + [LAST_EXPERT * C, T]
@@ -107,7 +120,7 @@ def tile_moe_elr_gelu_kernel(
             return results[nt][:].indirect(slot_list(e * C + u * UNIT, UNIT))
 
         def load_wa(e, s):
-            wa_raw[e, s] = sbuf("wa_raw%d%d" % (e, s), [P, PACK, H], F32, tag="raw%d%d" % (e, s))
+            wa_raw[e, s] = sbuf("wa_raw%d%d" % (e, s), [P, PACK, H], F32)
             rows = wa[e, s * K_PASS : (s + 1) * K_PASS, :].rearrange("(p j) i -> p j i", j=PACK)
             nc.sync.dma_start(out=wa_raw[e, s][:], in_=rows)
 
@@ -119,6 +132,11 @@ def tile_moe_elr_gelu_kernel(
 
         def load_gate(e):
             nc.sync.dma_start(out=gates[e][:], in_=gate[:, gate_starts[e] : gate_ends[e]])
+
+        def load_frozen_scales(e, queue):
+            for r in range(SCALE_ROWS):
+                rows = w_scales[e].rearrange("s (q r) n -> r q s n", r=SCALE_ROWS)[r]
+                queue.dma_start(out=frozen_scales[e][r:P:QUADRANT, :, :].bitcast(I32), in_=rows.bitcast(I32))
 
         def load_frozen(e):
             nc.sync.dma_start(
@@ -146,13 +164,13 @@ def tile_moe_elr_gelu_kernel(
                 )
 
         def round_wa(e, s):
-            dst = wa_bf16[e][s][:].rearrange("p (t m j) -> p m j t", t=PACK, j=PACK)
+            dst = wa_bf16[e, s][:].rearrange("p (t m j) -> p m j t", t=PACK, j=PACK)
             src = wa_raw[e, s][:].rearrange("p j (m t) -> p m j t", t=PACK)
             if s == LAST_PASS:
                 nc.vector.tensor_copy(out=dst[:, :, :, 0:HALF], in_=src[:, :, :, 0:HALF])
                 nc.scalar.copy(out=dst[:, :, :, HALF:PACK], in_=src[:, :, :, HALF:PACK])
                 return
-            share = MIDDLE_SHARE if (e > 0 and s > 0) else 0
+            share = MIDDLE_SHARE if s > 0 else (VERY_FIRST_SHARE if e == 0 else 0)
             if share:
                 nc.vector.tensor_copy(out=dst[:, 0:share, :, HALF:PACK], in_=src[:, 0:share, :, HALF:PACK])
             nc.scalar.copy(out=dst[:, :, :, 0:HALF], in_=src[:, :, :, 0:HALF])
@@ -162,26 +180,34 @@ def tile_moe_elr_gelu_kernel(
             if s == 0:
                 for u in range(2):
                     h_banks[e, u] = bank("h", e, u, PACK)
-            halves = s == LAST_PASS and e in (0, LAST_EXPERT)
-            width = HALF * P if halves else H
-            for first in range(0, H, width):
+            half = HALF * P
+            todo = [(s, t) for t in range(PACK)]
+            codes, scales, values = wa_codes[e, s], wa_scales[e, s], wa_bf16[e, s]
+            cuts = [0, half, H] if (e == 0 and s == LAST_PASS) else [0, H]
+            if e > 0 and s > 0:
+                codes, scales, values = joint[e]
+                if s < LAST_PASS:
+                    cuts, todo = [0, half], todo[:HALF]
+                else:
+                    cuts, todo = [half, H + half, 2 * H], [(s - 1, t) for t in range(HALF, PACK)] + todo
+            for first, end in zip(cuts, cuts[1:]):
                 nc.vector.quantize_mx(
-                    out=wa_codes[e][s][:, first : first + width].bitcast(FP8X4),
-                    scales=wa_scales[e][s][:, first : first + width],
-                    in_=wa_bf16[e][s][:, PACK * first : PACK * (first + width)],
+                    out=codes[:, first:end].bitcast(FP8X4),
+                    scales=scales[:, first:end],
+                    in_=values[:, PACK * first : PACK * end],
                 )
             for u in range(2):
-                for step in range(PACK):
-                    t = (step + HALF * u) % PACK if halves else step
+                order = todo[-HALF:] + todo[:-HALF] if (u == 1 and len(cuts) > 2) else todo
+                for step, (k, t) in enumerate(order):
                     cols = slice(t * P, (t + 1) * P)
                     nc.tensor.matmul_mx(
                         out=h_banks[e, u][:, t, :],
-                        lhsT=wa_codes[e][s][:, cols].bitcast(FP8X4),
-                        lhsT_scale=wa_scales[e][s][:, cols],
-                        rhs=unit_words(e, s, u).bitcast(FP8X4),
-                        rhs_scale=slot_scales[SCALE_ROWS * s :, unit_slots(e, u)],
+                        lhsT=wa_codes[e, k][:, cols].bitcast(FP8X4),
+                        lhsT_scale=wa_scales[e, k][:, cols],
+                        rhs=unit_words(e, k, u).bitcast(FP8X4),
+                        rhs_scale=slot_scales[SCALE_ROWS * k :, unit_slots(e, u)],
                         start=(s == 0 and step == 0),
-                        stop=(s == LAST_PASS and step == PACK - 1),
+                        stop=(s == LAST_PASS and step == len(order) - 1),
                     )
 
         def round_wb(e):
@@ -205,7 +231,7 @@ def tile_moe_elr_gelu_kernel(
                     nc.tensor.matmul_mx(
                         out=y_tiles[e, u][nt],
                         lhsT=frozen_words[e][:, s, 2 * P * nt : 2 * P * (nt + 1)].bitcast(FP4X4),
-                        lhsT_scale=frozen_scales[:, e * PASSES + s, P * nt : P * (nt + 1)],
+                        lhsT_scale=frozen_scales[e][:, s, P * nt : P * (nt + 1)],
                         rhs=unit_words(e, s, u).bitcast(FP8X4),
                         rhs_scale=scales_from_zero[s][:, unit_slots(e, u)],
                         start=(s == 0 and (nt == 0 or apart)),
@@ -262,53 +288,60 @@ def tile_moe_elr_gelu_kernel(
 
         nc.vector.memset(token_scales[:].bitcast(I32), 0)
         nc.vector.memset(warm[:, 0:1], 0.0)
-        nc.vector.memset(frozen_scales[:].rearrange("p g n -> p (g n)").bitcast(I32), 0)
+        for e in range(E):
+            nc.vector.memset(frozen_scales[e][:].rearrange("p s n -> p (s n)").bitcast(I32), 0)
         for s in range(1, PASSES):
             nc.vector.memset(scales_from_zero[s][:].bitcast(I32), 0)
 
         for q in range(QUADRANTS):
-            nc.scalar.dma_start(
+            (nc.scalar, nc.gpsimd)[q % 2].dma_start(
                 out=token_scales[QUADRANT * q : QUADRANT * q + SCALE_ROWS * PASSES, :].bitcast(I32),
                 in_=x_scales[:, SCALE_ROWS * q : SCALE_ROWS * (q + 1), :].bitcast(I32),
             )
         nc.scalar.activation(out=warm[:, 1:2], in_=warm[:, 0:1], func=GELU)
-        for r in range(SCALE_ROWS):
-            rows = w_scales.rearrange("e s (q r) n -> r q (e s) n", r=SCALE_ROWS)[r]
-            nc.gpsimd.dma_start(out=frozen_scales[r:P:QUADRANT, :, :].bitcast(I32), in_=rows.bitcast(I32))
+        load_frozen_scales(0, nc.gpsimd)
 
         load_words(0)
         nc.sync.dma_start(offsets[:], offs)
         load_words(1)
-        load_wa(0, 0)
-        load_wa(0, 1)
-        load_words(2)
-        load_wa(0, 2)
+        for s in range(PASSES):
+            load_wa(0, s)
 
-        gather_first_words(0)
+        for s in range(LAST_PASS):
+            gather_first_words(s)
+            gather_later_words(s)
+        slot_scales = sbuf("slot_scales", [P, T], U8, tag="token_words1")
+        scales_from_zero[0] = slot_scales
         gather_scales(0, C)
-        gather_later_words(0)
         gather_scales(C, T - C)
         load_wb(0)
+        load_words(LAST_PASS)
         move_scales()
         load_frozen(0)
         load_gate(0)
         for e in range(1, E):
             for s in range(PASSES):
                 load_wa(e, s)
+                if e < LAST_EXPERT and s == LAST_PASS - 1:
+                    load_frozen_scales(e, nc.sync)
             load_wb(e)
             load_gate(e)
+            if e == LAST_EXPERT:
+                load_frozen_scales(e, nc.sync)
             load_frozen(e)
         load_gate(E)
         for s in range(LAST_PASS):
             round_wa(0, s)
-            gather_first_words(s + 1)
             first_products(0, s)
-            gather_later_words(s + 1)
 
         for e in range(E):
             round_wa(e, LAST_PASS)
             round_wb(e)
+            if e == 0:
+                gather_first_words(LAST_PASS)
             first_products(e, LAST_PASS)
+            if e == 0:
+                gather_later_words(LAST_PASS)
             if e > 0:
                 scatter_late(e - 1, 0)
             quantise_wb(e)

@@ -14,6 +14,7 @@ U8 = mybir.dt.uint8
 FP8X4 = mybir.dt.float8_e4m3fn_x4
 FP4X4 = mybir.dt.float4_e2m1fn_x4
 GELU = mybir.ActivationFunctionType.Gelu_apprx_tanh
+COPY = mybir.ActivationFunctionType.Copy
 MULT = mybir.AluOpType.mult
 
 P = 128
@@ -30,7 +31,8 @@ SCALE_ROWS = 4
 MOVED_ROWS = QUADRANT * (QUADRANTS - 1) + SCALE_ROWS
 RUN = 2
 HALF = PACK // 2
-VERY_FIRST_SHARE = 32
+VERY_FIRST_SHARE = 0
+FIRST_MIDDLE_SHARE = 64
 MIDDLE_SHARE = 96
 
 
@@ -53,6 +55,8 @@ def tile_moe_elr_gelu_kernel(
             name = "%s%d%d%d" % (kind, e, u, nt)
             if u == 0:
                 return psum.tile([P, width, UNIT], F32, name=name, tag=kind)
+            if kind == "y" and e == LAST_EXPERT:
+                return psum_once.tile([P, width, UNIT], F32, name=name, tag=("second0", "spare")[nt])
             return psum_once.tile([P, width, UNIT], F32, name=name, tag="second%d" % e)
 
         offsets = keep.tile([P, T // 16], U16, name="offsets")
@@ -60,7 +64,7 @@ def tile_moe_elr_gelu_kernel(
         token_words = [sbuf("token_words%d" % s, [P, T], I32) for s in range(PASSES)]
         scales_from_zero = {s: sbuf("moved%d" % s, [P, T], U8) for s in range(1, PASSES)}
         first_words = [sbuf("first_words%d" % s, [P, C], U32) for s in range(PASSES)]
-        later_words = [sbuf("later_words%d" % s, [P, T - C], U32) for s in range(PASSES)]
+        later_words = [sbuf("later_words%d" % s, [P, T - C], U32) for s in range(LAST_PASS)]
         frozen_scales = per_expert("frozen_scales", [P, PASSES, N], U8)
         frozen_words = per_expert("frozen_words", [P, PASSES, 2 * N], U8)
         wa_bf16 = {}
@@ -170,7 +174,7 @@ def tile_moe_elr_gelu_kernel(
                 nc.vector.tensor_copy(out=dst[:, :, :, 0:HALF], in_=src[:, :, :, 0:HALF])
                 nc.scalar.copy(out=dst[:, :, :, HALF:PACK], in_=src[:, :, :, HALF:PACK])
                 return
-            share = MIDDLE_SHARE if s > 0 else (VERY_FIRST_SHARE if e == 0 else 0)
+            share = (FIRST_MIDDLE_SHARE if e == 0 else MIDDLE_SHARE) if s > 0 else (VERY_FIRST_SHARE if e == 0 else 0)
             if share:
                 nc.vector.tensor_copy(out=dst[:, 0:share, :, HALF:PACK], in_=src[:, 0:share, :, HALF:PACK])
             nc.scalar.copy(out=dst[:, :, :, 0:HALF], in_=src[:, :, :, 0:HALF])
@@ -220,7 +224,7 @@ def tile_moe_elr_gelu_kernel(
             nc.vector.quantize_mx(out=wb_codes[e][:].bitcast(FP8X4), scales=wb_scales[e][:], in_=wb_bf16[e][:])
 
         def frozen_products(e, u):
-            apart = e == LAST_EXPERT and u == 0
+            apart = e == LAST_EXPERT
             if apart:
                 y_tiles[e, u] = [bank("y", e, u, 1, nt)[:, 0, :] for nt in range(N_TILES)]
             else:
@@ -262,7 +266,7 @@ def tile_moe_elr_gelu_kernel(
                     rhs=h_codes[:].bitcast(FP8X4),
                     rhs_scale=h_scales[:],
                     start=False,
-                    stop=(nt == N_TILES - 1 or (e == LAST_EXPERT and u == 0)),
+                    stop=(nt == N_TILES - 1 or e == LAST_EXPERT),
                 )
 
         def return_by_vector(e):
@@ -274,9 +278,10 @@ def tile_moe_elr_gelu_kernel(
 
         def return_by_scalar(e, u):
             sums[e, u] = sbuf("sums%d%d" % (e, u), [P, N_TILES, UNIT], F32)
-            for nt in range(N_TILES):
-                nc.scalar.copy(out=sums[e, u][:, nt, :], in_=y_tiles[e, u][nt])
-                nc.vector.tensor_tensor(unit_window(e, u, nt), sums[e, u][:, nt, :], unit_gate(e, u), MULT)
+            nc.scalar.copy(out=sums[e, u][:, 0, :], in_=y_tiles[e, u][0])
+            nc.vector.tensor_tensor(sums[e, u][:, 1, :], y_tiles[e, u][1], unit_gate(e, u), MULT)
+            nc.vector.tensor_tensor(unit_window(e, u, 0), sums[e, u][:, 0, :], unit_gate(e, u), MULT)
+            nc.scalar.activation(out=unit_window(e, u, 1), in_=sums[e, u][:, 1, :], func=COPY)
 
         def copy_late(e, nt):
             tag = "wa_bf16%d0" % (e + 1) if nt == 0 else "wb_raw%d" % (e + 1)
@@ -304,8 +309,10 @@ def tile_moe_elr_gelu_kernel(
         load_words(0)
         nc.sync.dma_start(offsets[:], offs)
         load_words(1)
-        for s in range(PASSES):
+        for s in range(LAST_PASS):
             load_wa(0, s)
+        load_words(LAST_PASS)
+        load_wa(0, LAST_PASS)
 
         for s in range(LAST_PASS):
             gather_first_words(s)
@@ -315,7 +322,6 @@ def tile_moe_elr_gelu_kernel(
         gather_scales(0, C)
         gather_scales(C, T - C)
         load_wb(0)
-        load_words(LAST_PASS)
         move_scales()
         load_frozen(0)
         load_gate(0)
@@ -341,6 +347,7 @@ def tile_moe_elr_gelu_kernel(
                 gather_first_words(LAST_PASS)
             first_products(e, LAST_PASS)
             if e == 0:
+                later_words.append(sbuf("later_words%d" % LAST_PASS, [P, T - C], U32, tag="wa_bf160%d" % LAST_PASS))
                 gather_later_words(LAST_PASS)
             if e > 0:
                 scatter_late(e - 1, 0)

@@ -160,11 +160,11 @@ def tile_moe_elr_gelu_kernel(
                 out=slot_scales[:, first : first + count], in_=token_scales[:].indirect(slot_list(first, count))
             )
 
-        def move_scales():
+        def move_scales(queue, first, end):
             for s in range(1, PASSES):
-                nc.gpsimd.dma_start(
-                    out=scales_from_zero[s][0:MOVED_ROWS, :].bitcast(I32),
-                    in_=slot_scales[SCALE_ROWS * s : SCALE_ROWS * s + MOVED_ROWS, :].bitcast(I32),
+                queue.dma_start(
+                    out=scales_from_zero[s][0:MOVED_ROWS, first:end].bitcast(I32),
+                    in_=slot_scales[SCALE_ROWS * s : SCALE_ROWS * s + MOVED_ROWS, first:end].bitcast(I32),
                 )
 
         def round_wa(e, s):
@@ -299,7 +299,7 @@ def tile_moe_elr_gelu_kernel(
             nc.vector.memset(scales_from_zero[s][:].bitcast(I32), 0)
 
         for q in range(QUADRANTS):
-            (nc.scalar, nc.gpsimd)[q % 2].dma_start(
+            (nc.gpsimd if q == 0 else nc.scalar).dma_start(
                 out=token_scales[QUADRANT * q : QUADRANT * q + SCALE_ROWS * PASSES, :].bitcast(I32),
                 in_=x_scales[:, SCALE_ROWS * q : SCALE_ROWS * (q + 1), :].bitcast(I32),
             )
@@ -322,7 +322,8 @@ def tile_moe_elr_gelu_kernel(
         gather_scales(0, C)
         gather_scales(C, T - C)
         load_wb(0)
-        move_scales()
+        move_scales(nc.sync, 0, C)
+        move_scales(nc.gpsimd, C, T)
         load_frozen(0)
         load_gate(0)
         for e in range(1, E):

@@ -31,7 +31,8 @@ SCALE_ROWS = 4
 MOVED_ROWS = QUADRANT * (QUADRANTS - 1) + SCALE_ROWS
 RUN = 2
 HALF = PACK // 2
-VERY_FIRST_SHARE = 0
+LAST_SHARE = 24
+VERY_FIRST_SHARE = 32
 FIRST_MIDDLE_SHARE = 64
 MIDDLE_SHARE = 96
 
@@ -87,19 +88,22 @@ def tile_moe_elr_gelu_kernel(
                 wa_scales[e, s] = joint[e][1][:, (s - 1) * H : s * H]
                 wa_bf16[e, s] = joint[e][2][:, (s - 1) * PACK * H : s * PACK * H]
         wb_raw = per_expert("wb_raw", [P, PACK, N], F32)
-        wb_bf16 = per_expert("wb_bf16_", [P, PACK * N], BF16)
-        wb_codes = per_expert("wb_codes", [P, N], U32)
-        wb_scales = per_expert("wb_scales", [P, N], U8)
+        inner_bf16 = per_expert("inner_bf16_", [P, PACK * (N + C)], BF16)
+        inner_codes = per_expert("inner_codes", [P, N + C], U32)
+        inner_scales = per_expert("inner_scales", [P, N + C], U8)
+        wb_bf16 = [values[:, 0 : PACK * N] for values in inner_bf16]
+        wb_codes = [codes[:, 0:N] for codes in inner_codes]
+        wb_scales = [scales[:, 0:N] for scales in inner_scales]
         gate_ends = [e * C + UNIT for e in range(LAST_EXPERT)] + [LAST_EXPERT * C, T]
         gate_starts = [0] + gate_ends[:-1]
         gates = [sbuf("gates%d" % e, [P, gate_ends[e] - gate_starts[e]], F32) for e in range(E + 1)]
         results = [sbuf("results%d" % nt, [P, T], F32) for nt in range(N_TILES)]
+        last_sums = [sbuf("last_sums%d" % nt, [P, C], F32) for nt in range(N_TILES)]
         warm = sbuf("warm", [P, 2], F32)
         wa_raw = {}
         h_banks = {}
         y_banks = {}
         y_tiles = {}
-        h_bf16 = {}
         h_mx = {}
         sums = {}
         late_sums = {}
@@ -172,7 +176,8 @@ def tile_moe_elr_gelu_kernel(
             src = wa_raw[e, s][:].rearrange("p j (m t) -> p m j t", t=PACK)
             if s == LAST_PASS:
                 nc.vector.tensor_copy(out=dst[:, :, :, 0:HALF], in_=src[:, :, :, 0:HALF])
-                nc.scalar.copy(out=dst[:, :, :, HALF:PACK], in_=src[:, :, :, HALF:PACK])
+                nc.vector.tensor_copy(out=dst[:, 0:LAST_SHARE, :, HALF:PACK], in_=src[:, 0:LAST_SHARE, :, HALF:PACK])
+                nc.scalar.copy(out=dst[:, LAST_SHARE:P, :, HALF:PACK], in_=src[:, LAST_SHARE:P, :, HALF:PACK])
                 return
             share = (FIRST_MIDDLE_SHARE if e == 0 else MIDDLE_SHARE) if s > 0 else (VERY_FIRST_SHARE if e == 0 else 0)
             if share:
@@ -216,12 +221,9 @@ def tile_moe_elr_gelu_kernel(
 
         def round_wb(e):
             nc.scalar.copy(
-                out=wb_bf16[e][:].rearrange("p (c r j) -> p c j r", r=RUN, j=PACK),
+                out=wb_bf16[e].rearrange("p (c r j) -> p c j r", r=RUN, j=PACK),
                 in_=wb_raw[e][:].rearrange("p j (c r) -> p c j r", r=RUN),
             )
-
-        def quantise_wb(e):
-            nc.vector.quantize_mx(out=wb_codes[e][:].bitcast(FP8X4), scales=wb_scales[e][:], in_=wb_bf16[e][:])
 
         def frozen_products(e, u):
             apart = e == LAST_EXPERT
@@ -243,17 +245,20 @@ def tile_moe_elr_gelu_kernel(
                     )
 
         def quantise_hidden(e, u):
-            if u == 0:
-                h_bf16[e] = sbuf("h_bf16%d" % e, [P, 2, PACK * UNIT], BF16)
-            h_codes = sbuf("h_codes%d%d" % (e, u), [P, UNIT], U32)
-            h_scales = sbuf("h_scales%d%d" % (e, u), [P, UNIT], U8)
+            start = N + u * UNIT
+            end = start + UNIT
             nc.scalar.activation(
-                out=h_bf16[e][:, u, :].rearrange("p (c t) -> p c t", t=PACK),
+                out=inner_bf16[e][:, PACK * start : PACK * end].rearrange("p (c t) -> p c t", t=PACK),
                 in_=h_banks[e, u][:].rearrange("p t c -> p c t"),
                 func=GELU,
             )
-            nc.vector.quantize_mx(out=h_codes[:].bitcast(FP8X4), scales=h_scales[:], in_=h_bf16[e][:, u, :])
-            h_mx[e, u] = (h_codes, h_scales)
+            first = 0 if u == 0 else start
+            nc.vector.quantize_mx(
+                out=inner_codes[e][:, first:end].bitcast(FP8X4),
+                scales=inner_scales[e][:, first:end],
+                in_=inner_bf16[e][:, PACK * first : PACK * end],
+            )
+            h_mx[e, u] = (inner_codes[e][:, start:end], inner_scales[e][:, start:end])
 
         def second_products(e, u):
             h_codes, h_scales = h_mx[e, u]
@@ -263,8 +268,8 @@ def tile_moe_elr_gelu_kernel(
                     out=y_tiles[e, u][nt],
                     lhsT=wb_codes[e][:, cols].bitcast(FP8X4),
                     lhsT_scale=wb_scales[e][:, cols],
-                    rhs=h_codes[:].bitcast(FP8X4),
-                    rhs_scale=h_scales[:],
+                    rhs=h_codes.bitcast(FP8X4),
+                    rhs_scale=h_scales,
                     start=False,
                     stop=(nt == N_TILES - 1 or e == LAST_EXPERT),
                 )
@@ -277,19 +282,21 @@ def tile_moe_elr_gelu_kernel(
                 nc.vector.tensor_copy(out=unit_window(e, 0, nt), in_=sums[e, 0][:, nt, :])
 
         def return_by_scalar(e, u):
-            sums[e, u] = sbuf("sums%d%d" % (e, u), [P, N_TILES, UNIT], F32)
-            nc.scalar.copy(out=sums[e, u][:, 0, :], in_=y_tiles[e, u][0])
-            nc.vector.tensor_tensor(sums[e, u][:, 1, :], y_tiles[e, u][1], unit_gate(e, u), MULT)
-            nc.vector.tensor_tensor(unit_window(e, u, 0), sums[e, u][:, 0, :], unit_gate(e, u), MULT)
-            nc.scalar.activation(out=unit_window(e, u, 1), in_=sums[e, u][:, 1, :], func=COPY)
+            cols = slice(u * UNIT, (u + 1) * UNIT)
+            nc.scalar.copy(out=last_sums[0][:, cols], in_=y_tiles[e, u][0])
+            nc.vector.tensor_tensor(last_sums[1][:, cols], y_tiles[e, u][1], unit_gate(e, u), MULT)
 
-        def copy_late(e, nt):
-            tag = "wa_bf16%d0" % (e + 1) if nt == 0 else "wb_raw%d" % (e + 1)
-            late_sums[e, nt] = sbuf("late%d%d" % (e, nt), [P, UNIT], F32, tag=tag)
-            nc.scalar.copy(out=late_sums[e, nt][:], in_=y_banks[e, 1][:, nt, :])
+        def scatter_last(e):
+            places = slot_list(e * C, C)
+            nc.vector.tensor_tensor(results[0][:].indirect(places), last_sums[0][:], gates[E][:], MULT)
+            nc.scalar.activation(out=results[1][:].indirect(places), in_=last_sums[1][:], func=COPY)
+
+        def copy_late(e):
+            late_sums[e] = sbuf("late%d" % e, [P, N_TILES, UNIT], F32, tag="wa_bf16%d0" % (e + 1))
+            nc.scalar.copy(out=late_sums[e][:], in_=y_banks[e, 1][:])
 
         def scatter_late(e, nt):
-            nc.vector.tensor_tensor(unit_window(e, 1, nt), late_sums[e, nt][:], unit_gate(e, 1), MULT)
+            nc.vector.tensor_tensor(unit_window(e, 1, nt), late_sums[e][:, nt, :], unit_gate(e, 1), MULT)
 
         nc.vector.memset(token_scales[:].bitcast(I32), 0)
         nc.vector.memset(warm[:, 0:1], 0.0)
@@ -351,25 +358,26 @@ def tile_moe_elr_gelu_kernel(
                 later_words.append(sbuf("later_words%d" % LAST_PASS, [P, T - C], U32, tag="wa_bf160%d" % LAST_PASS))
                 gather_later_words(LAST_PASS)
             if e > 0:
-                scatter_late(e - 1, 0)
-            quantise_wb(e)
+                for nt in range(N_TILES):
+                    scatter_late(e - 1, nt)
             frozen_products(e, 0)
+            if e == LAST_EXPERT:
+                frozen_products(e, 1)
             quantise_hidden(e, 0)
             second_products(e, 0)
-            if e > 0:
-                copy_late(e - 1, 1)
-                scatter_late(e - 1, 1)
             quantise_hidden(e, 1)
-            frozen_products(e, 1)
+            if e < LAST_EXPERT:
+                frozen_products(e, 1)
             second_products(e, 1)
             if e < LAST_EXPERT:
                 return_by_vector(e)
                 for s in range(LAST_PASS):
                     round_wa(e + 1, s)
                     first_products(e + 1, s)
-                copy_late(e, 0)
+                copy_late(e)
         for u in range(2):
             return_by_scalar(LAST_EXPERT, u)
+        scatter_last(LAST_EXPERT)
 
         for nt in range(N_TILES):
             nc.sync.dma_start(out=out[nt * P : (nt + 1) * P, :], in_=results[nt][:])

@@ -1,6 +1,7 @@
 from contextlib import ExitStack
 
 import concourse.mybir as mybir
+from concourse.masks import make_identity
 
 K, T, E, C, H, N = 1536, 768, 3, 256, 512, 256
 FLOPS = 2 * E * C * (K * N + K * H + H * N)
@@ -16,6 +17,7 @@ FP4X4 = mybir.dt.float4_e2m1fn_x4
 GELU = mybir.ActivationFunctionType.Gelu_apprx_tanh
 COPY = mybir.ActivationFunctionType.Copy
 MULT = mybir.AluOpType.mult
+ADD = mybir.AluOpType.add
 
 P = 128
 PACK = 4
@@ -31,10 +33,16 @@ SCALE_ROWS = 4
 MOVED_ROWS = QUADRANT * (QUADRANTS - 1) + SCALE_ROWS
 RUN = 2
 HALF = PACK // 2
-LAST_SHARE = 24
+LAST_SHARE = 32
+GATE_BANKS = 2
+GATE_PIECES = 8
+GATE_RUN = T // GATE_PIECES
+FIRST_SHARE = 0
+MIDDLE_SHARES = (64, 64, 64)
+GPSIMD_SHARE = 112
 VERY_FIRST_SHARE = 32
 FIRST_MIDDLE_SHARE = 64
-MIDDLE_SHARE = 96
+MIDDLE_SHARE = 0
 
 
 def tile_moe_elr_gelu_kernel(
@@ -94,9 +102,10 @@ def tile_moe_elr_gelu_kernel(
         wb_bf16 = [values[:, 0 : PACK * N] for values in inner_bf16]
         wb_codes = [codes[:, 0:N] for codes in inner_codes]
         wb_scales = [scales[:, 0:N] for scales in inner_scales]
-        gate_ends = [e * C + UNIT for e in range(LAST_EXPERT)] + [LAST_EXPERT * C, T]
-        gate_starts = [0] + gate_ends[:-1]
-        gates = [sbuf("gates%d" % e, [P, gate_ends[e] - gate_starts[e]], F32) for e in range(E + 1)]
+        gate_rows = sbuf("gate_rows", [P, P], F32)
+        identity = sbuf("identity", [P, P], F32)
+        gates = {}
+        spreads = {}
         results = [sbuf("results%d" % nt, [P, T], F32) for nt in range(N_TILES)]
         last_sums = [sbuf("last_sums%d" % nt, [P, C], F32) for nt in range(N_TILES)]
         warm = sbuf("warm", [P, 2], F32)
@@ -107,6 +116,7 @@ def tile_moe_elr_gelu_kernel(
         h_mx = {}
         sums = {}
         late_sums = {}
+        upper = {}
 
         def slot_list(first, count):
             return offsets[:, first // 16 : (first + count) // 16]
@@ -120,9 +130,7 @@ def tile_moe_elr_gelu_kernel(
             return later_words[s][:, unit_slots(e - 1, u)]
 
         def unit_gate(e, u):
-            load = E if e == LAST_EXPERT else e + u
-            first = e * C + u * UNIT - gate_starts[load]
-            return gates[load][:, first : first + UNIT]
+            return gate_of(e * C + u * UNIT, UNIT)
 
         def unit_window(e, u, nt):
             return results[nt][:].indirect(slot_list(e * C + u * UNIT, UNIT))
@@ -138,8 +146,30 @@ def tile_moe_elr_gelu_kernel(
         def load_wb(e):
             nc.sync.dma_start(out=wb_raw[e][:], in_=wb[e].rearrange("(p t) n -> p t n", t=PACK))
 
-        def load_gate(e):
-            nc.sync.dma_start(out=gates[e][:], in_=gate[:, gate_starts[e] : gate_ends[e]])
+        def load_gate():
+            row = gate[0].rearrange("(c k) -> c k", k=GATE_RUN)
+            nc.sync.dma_start(out=gate_rows[0:GATE_PIECES, 0:GATE_RUN], in_=row)
+
+        def spread_gate():
+            turned = psum_once.tile([P, P], F32, name="turned", tag="second1")
+            nc.tensor.transpose(turned[:], gate_rows[:], identity[:])
+            gate_columns = sbuf("gate_columns", [P, GATE_PIECES], F32)
+            nc.scalar.copy(out=gate_columns[:], in_=turned[:, 0:GATE_PIECES])
+            count = GATE_PIECES // GATE_BANKS
+            for b in range(GATE_BANKS):
+                spread = psum_once.tile([P, count, P], F32, name="spread%d" % b, tag=("spare", "second2")[b])
+                for r in range(count):
+                    c = b * count + r
+                    nc.tensor.transpose(spread[:, r, :], gate_columns[:, c : c + 1].to_broadcast([P, P]), identity[:])
+                spreads[b] = spread
+
+        def keep_gate(b, tag):
+            gates[b] = sbuf("gates%d" % b, [P, T // GATE_BANKS], F32, tag=tag)
+            nc.scalar.copy(out=gates[b][:].rearrange("p (r k) -> p r k", k=GATE_RUN), in_=spreads[b][:, :, 0:GATE_RUN])
+
+        def gate_of(first, count):
+            b, start = divmod(first, T // GATE_BANKS)
+            return gates[b][:, start : start + count]
 
         def load_frozen_scales(e, queue):
             for r in range(SCALE_ROWS):
@@ -179,7 +209,17 @@ def tile_moe_elr_gelu_kernel(
                 nc.vector.tensor_copy(out=dst[:, 0:LAST_SHARE, :, HALF:PACK], in_=src[:, 0:LAST_SHARE, :, HALF:PACK])
                 nc.scalar.copy(out=dst[:, LAST_SHARE:P, :, HALF:PACK], in_=src[:, LAST_SHARE:P, :, HALF:PACK])
                 return
-            share = (FIRST_MIDDLE_SHARE if e == 0 else MIDDLE_SHARE) if s > 0 else (VERY_FIRST_SHARE if e == 0 else 0)
+            if e > 0 and s == 0:
+                upper[e] = sbuf("upper%d" % e, [P, HALF * H], BF16, tag="inner_bf16_%d" % (e - 1))
+                high = upper[e][:].rearrange("p (t m j) -> p t m j", t=HALF, j=PACK)
+                rows = wa_raw[e, s][:].rearrange("p j (m t) -> p t m j", t=PACK)[:, HALF:PACK]
+                nc.scalar.copy(out=dst[:, :, :, 0:HALF], in_=src[:, :, :, 0:HALF])
+                nc.gpsimd.tensor_scalar(high[:, :, 0:GPSIMD_SHARE], rows[:, :, 0:GPSIMD_SHARE], 1.0, 0.0, MULT, ADD)
+                if GPSIMD_SHARE < P:
+                    pairs = upper[e][:].rearrange("p (t m j) -> p m j t", t=HALF, j=PACK)
+                    nc.scalar.copy(out=pairs[:, GPSIMD_SHARE:P], in_=src[:, GPSIMD_SHARE:P, :, HALF:PACK])
+                return
+            share = MIDDLE_SHARES[e] if s > 0 else (VERY_FIRST_SHARE if e == 0 else FIRST_SHARE)
             if share:
                 nc.vector.tensor_copy(out=dst[:, 0:share, :, HALF:PACK], in_=src[:, 0:share, :, HALF:PACK])
             nc.scalar.copy(out=dst[:, :, :, 0:HALF], in_=src[:, :, :, 0:HALF])
@@ -199,6 +239,12 @@ def tile_moe_elr_gelu_kernel(
                     cuts, todo = [0, half], todo[:HALF]
                 else:
                     cuts, todo = [half, H + half, 2 * H], [(s - 1, t) for t in range(HALF, PACK)] + todo
+            if e > 0 and s == 0:
+                nc.vector.quantize_mx(
+                    out=codes[:, 0:half].bitcast(FP8X4), scales=scales[:, 0:half], in_=values[:, 0 : PACK * half]
+                )
+                nc.vector.quantize_mx(out=codes[:, half:H].bitcast(FP8X4), scales=scales[:, half:H], in_=upper[e][:])
+                cuts = [0]
             for first, end in zip(cuts, cuts[1:]):
                 nc.vector.quantize_mx(
                     out=codes[:, first:end].bitcast(FP8X4),
@@ -288,17 +334,19 @@ def tile_moe_elr_gelu_kernel(
 
         def scatter_last(e):
             places = slot_list(e * C, C)
-            nc.vector.tensor_tensor(results[0][:].indirect(places), last_sums[0][:], gates[E][:], MULT)
+            nc.vector.tensor_tensor(results[0][:].indirect(places), last_sums[0][:], gate_of(e * C, C), MULT)
             nc.scalar.activation(out=results[1][:].indirect(places), in_=last_sums[1][:], func=COPY)
 
         def copy_late(e):
-            late_sums[e] = sbuf("late%d" % e, [P, N_TILES, UNIT], F32, tag="wa_bf16%d0" % (e + 1))
+            late_sums[e] = sbuf("late%d" % e, [P, N_TILES, UNIT], F32, tag="wa_raw%d%d" % (e + 1, LAST_PASS))
             nc.scalar.copy(out=late_sums[e][:], in_=y_banks[e, 1][:])
 
         def scatter_late(e, nt):
             nc.vector.tensor_tensor(unit_window(e, 1, nt), late_sums[e][:, nt, :], unit_gate(e, 1), MULT)
 
         nc.vector.memset(token_scales[:].bitcast(I32), 0)
+        nc.vector.memset(gate_rows[:], 0.0)
+        nc.vector.memset(identity[:], 0.0)
         nc.vector.memset(warm[:, 0:1], 0.0)
         for e in range(E):
             nc.vector.memset(frozen_scales[e][:].rearrange("p s n -> p (s n)").bitcast(I32), 0)
@@ -310,11 +358,13 @@ def tile_moe_elr_gelu_kernel(
                 out=token_scales[QUADRANT * q : QUADRANT * q + SCALE_ROWS * PASSES, :].bitcast(I32),
                 in_=x_scales[:, SCALE_ROWS * q : SCALE_ROWS * (q + 1), :].bitcast(I32),
             )
+        make_identity(nc, identity[:], nomemset=True)
         nc.scalar.activation(out=warm[:, 1:2], in_=warm[:, 0:1], func=GELU)
         load_frozen_scales(0, nc.gpsimd)
 
         load_words(0)
         nc.sync.dma_start(offsets[:], offs)
+        load_gate()
         load_words(1)
         for s in range(LAST_PASS):
             load_wa(0, s)
@@ -332,24 +382,25 @@ def tile_moe_elr_gelu_kernel(
         move_scales(nc.sync, 0, C)
         move_scales(nc.gpsimd, C, T)
         load_frozen(0)
-        load_gate(0)
         for e in range(1, E):
             for s in range(PASSES):
                 load_wa(e, s)
                 if e < LAST_EXPERT and s == LAST_PASS - 1:
                     load_frozen_scales(e, nc.sync)
             load_wb(e)
-            load_gate(e)
             if e == LAST_EXPERT:
                 load_frozen_scales(e, nc.sync)
             load_frozen(e)
-        load_gate(E)
+        spread_gate()
+        keep_gate(0, "gates0")
         for s in range(LAST_PASS):
             round_wa(0, s)
             first_products(0, s)
 
         for e in range(E):
             round_wa(e, LAST_PASS)
+            if e > 0:
+                copy_late(e - 1)
             round_wb(e)
             if e == 0:
                 gather_first_words(LAST_PASS)
@@ -374,7 +425,8 @@ def tile_moe_elr_gelu_kernel(
                 for s in range(LAST_PASS):
                     round_wa(e + 1, s)
                     first_products(e + 1, s)
-                copy_late(e)
+                if e == 0:
+                    keep_gate(1, "wa_raw11")
         for u in range(2):
             return_by_scalar(LAST_EXPERT, u)
         scatter_last(LAST_EXPERT)

@@ -39,7 +39,7 @@ GATE_PIECES = 8
 GATE_RUN = T // GATE_PIECES
 FIRST_SHARE = 0
 MIDDLE_SHARES = (64, 64, 64)
-GPSIMD_SHARE = 112
+GPSIMD_SHARE = 96
 VERY_FIRST_SHARE = 32
 FIRST_MIDDLE_SHARE = 64
 MIDDLE_SHARE = 0
@@ -385,17 +385,15 @@ def tile_moe_elr_gelu_kernel(
         for e in range(1, E):
             for s in range(PASSES):
                 load_wa(e, s)
-                if e < LAST_EXPERT and s == LAST_PASS - 1:
-                    load_frozen_scales(e, nc.sync)
             load_wb(e)
-            if e == LAST_EXPERT:
-                load_frozen_scales(e, nc.sync)
+            load_frozen_scales(e, nc.sync)
             load_frozen(e)
         spread_gate()
         keep_gate(0, "gates0")
         for s in range(LAST_PASS):
             round_wa(0, s)
             first_products(0, s)
+        keep_gate(1, "wa_raw01")
 
         for e in range(E):
             round_wa(e, LAST_PASS)
@@ -425,8 +423,6 @@ def tile_moe_elr_gelu_kernel(
                 for s in range(LAST_PASS):
                     round_wa(e + 1, s)
                     first_products(e + 1, s)
-                if e == 0:
-                    keep_gate(1, "wa_raw11")
         for u in range(2):
             return_by_scalar(LAST_EXPERT, u)
         scatter_last(LAST_EXPERT)

@@ -17,7 +17,6 @@ FP4X4 = mybir.dt.float4_e2m1fn_x4
 GELU = mybir.ActivationFunctionType.Gelu_apprx_tanh
 COPY = mybir.ActivationFunctionType.Copy
 MULT = mybir.AluOpType.mult
-ADD = mybir.AluOpType.add
 
 P = 128
 PACK = 4
@@ -26,6 +25,7 @@ PASSES = K // K_PASS
 LAST_PASS = PASSES - 1
 LAST_EXPERT = E - 1
 UNIT = 128
+UNITS = C // UNIT
 N_TILES = N // P
 QUADRANT = 32
 QUADRANTS = P // QUADRANT
@@ -33,16 +33,14 @@ SCALE_ROWS = 4
 MOVED_ROWS = QUADRANT * (QUADRANTS - 1) + SCALE_ROWS
 RUN = 2
 HALF = PACK // 2
-LAST_SHARE = 32
-GATE_BANKS = 2
 GATE_PIECES = 8
 GATE_RUN = T // GATE_PIECES
-FIRST_SHARE = 0
-MIDDLE_SHARES = (64, 64, 64)
-GPSIMD_SHARE = 96
-VERY_FIRST_SHARE = 32
-FIRST_MIDDLE_SHARE = 64
-MIDDLE_SHARE = 0
+GATE_BANKS = 2
+HEAD_SHARES = (0, 64)
+FIRST_SHARE = 256
+MIDDLE_SHARE = 256
+LAST_SHARE = 160
+WB_SHARE = 52
 
 
 def tile_moe_elr_gelu_kernel(
@@ -51,72 +49,29 @@ def tile_moe_elr_gelu_kernel(
     nc = tc.nc
     with ExitStack() as ctx:
         keep = ctx.enter_context(tc.tile_pool(name="keep", bufs=1))
-        psum = ctx.enter_context(tc.psum_pool(name="psum", bufs=2))
-        psum_once = ctx.enter_context(tc.psum_pool(name="psum_once", bufs=1))
+        psum = ctx.enter_context(tc.psum_pool(name="psum", bufs=1))
 
         def sbuf(name, shape, dtype, tag=None):
             return keep.tile(shape, dtype, name=name, tag=tag or name, align_bytes=64)
 
-        def per_expert(name, shape, dtype):
-            return [sbuf("%s%d" % (name, e), shape, dtype) for e in range(E)]
-
-        def bank(kind, e, u, width, nt=0):
-            name = "%s%d%d%d" % (kind, e, u, nt)
-            if u == 0:
-                return psum.tile([P, width, UNIT], F32, name=name, tag=kind)
-            if kind == "y" and e == LAST_EXPERT:
-                return psum_once.tile([P, width, UNIT], F32, name=name, tag=("second0", "spare")[nt])
-            return psum_once.tile([P, width, UNIT], F32, name=name, tag="second%d" % e)
+        def bank(name, width, number):
+            return psum.tile([P, width, P], F32, name=name, tag="bank%d" % number)
 
         offsets = keep.tile([P, T // 16], U16, name="offsets")
         token_scales = sbuf("token_scales", [P, T], U8)
-        token_words = [sbuf("token_words%d" % s, [P, T], I32) for s in range(PASSES)]
         scales_from_zero = {s: sbuf("moved%d" % s, [P, T], U8) for s in range(1, PASSES)}
-        first_words = [sbuf("first_words%d" % s, [P, C], U32) for s in range(PASSES)]
-        later_words = [sbuf("later_words%d" % s, [P, T - C], U32) for s in range(LAST_PASS)]
-        frozen_scales = per_expert("frozen_scales", [P, PASSES, N], U8)
-        frozen_words = per_expert("frozen_words", [P, PASSES, 2 * N], U8)
-        wa_bf16 = {}
-        wa_codes = {}
-        wa_scales = {}
-        joint = {}
-        for e in range(E):
-            for s in range(PASSES if e == 0 else 1):
-                wa_bf16[e, s] = sbuf("wa_bf16%d%d" % (e, s), [P, PACK * H], BF16)
-                wa_codes[e, s] = sbuf("wa_codes%d%d" % (e, s), [P, H], U32)
-                wa_scales[e, s] = sbuf("wa_scales%d%d" % (e, s), [P, H], U8)
-        for e in range(1, E):
-            joint[e] = (
-                sbuf("joint_codes%d" % e, [P, 2 * H], U32),
-                sbuf("joint_scales%d" % e, [P, 2 * H], U8),
-                sbuf("joint_bf16%d" % e, [P, 2 * PACK * H], BF16),
-            )
-            for s in range(1, PASSES):
-                wa_codes[e, s] = joint[e][0][:, (s - 1) * H : s * H]
-                wa_scales[e, s] = joint[e][1][:, (s - 1) * H : s * H]
-                wa_bf16[e, s] = joint[e][2][:, (s - 1) * PACK * H : s * PACK * H]
-        wb_raw = per_expert("wb_raw", [P, PACK, N], F32)
-        inner_bf16 = per_expert("inner_bf16_", [P, PACK * (N + C)], BF16)
-        inner_codes = per_expert("inner_codes", [P, N + C], U32)
-        inner_scales = per_expert("inner_scales", [P, N + C], U8)
-        wb_bf16 = [values[:, 0 : PACK * N] for values in inner_bf16]
-        wb_codes = [codes[:, 0:N] for codes in inner_codes]
-        wb_scales = [scales[:, 0:N] for scales in inner_scales]
+        token_words = [sbuf("token_words%d" % s, [P, T], I32) for s in range(PASSES)]
+        frozen_scales = [sbuf("frozen_scales%d" % e, [P, PASSES, N], U8) for e in range(E)]
         gate_rows = sbuf("gate_rows", [P, P], F32)
         identity = sbuf("identity", [P, P], F32)
-        gates = {}
-        spreads = {}
         results = [sbuf("results%d" % nt, [P, T], F32) for nt in range(N_TILES)]
-        last_sums = [sbuf("last_sums%d" % nt, [P, C], F32) for nt in range(N_TILES)]
         warm = sbuf("warm", [P, 2], F32)
-        wa_raw = {}
-        h_banks = {}
-        y_banks = {}
-        y_tiles = {}
-        h_mx = {}
-        sums = {}
-        late_sums = {}
-        upper = {}
+        first_words, later_words, late = {}, {}, {}
+        frozen_words, wa_raw, wa_bf16, wa_mx, wb_raw, wb_mx = {}, {}, {}, {}, {}, {}
+        h_banks, h_mx, y_tiles, y_banks, sums, gates, spreads = {}, {}, {}, {}, {}, {}, {}
+
+        def staging(e, s):
+            return ["staging%d%d%d" % (e, s, half) for half in range(2)]
 
         def slot_list(first, count):
             return offsets[:, first // 16 : (first + count) // 16]
@@ -130,69 +85,30 @@ def tile_moe_elr_gelu_kernel(
             return later_words[s][:, unit_slots(e - 1, u)]
 
         def unit_gate(e, u):
-            return gate_of(e * C + u * UNIT, UNIT)
+            b, start = divmod(e * C + u * UNIT, T // GATE_BANKS)
+            return gates[b][:, start : start + UNIT]
 
         def unit_window(e, u, nt):
             return results[nt][:].indirect(slot_list(e * C + u * UNIT, UNIT))
+
+        def load_words(s):
+            nc.sync.dma_start(out=token_words[s][:], in_=x_words[s].rearrange("p t d -> p (t d)").bitcast(I32))
 
         def load_wa(e, s):
             wa_raw[e, s] = sbuf("wa_raw%d%d" % (e, s), [P, PACK, H], F32)
             rows = wa[e, s * K_PASS : (s + 1) * K_PASS, :].rearrange("(p j) i -> p j i", j=PACK)
             nc.sync.dma_start(out=wa_raw[e, s][:], in_=rows)
 
-        def load_words(s):
-            nc.sync.dma_start(out=token_words[s][:], in_=x_words[s].rearrange("p t d -> p (t d)").bitcast(I32))
-
-        def load_wb(e):
-            nc.sync.dma_start(out=wb_raw[e][:], in_=wb[e].rearrange("(p t) n -> p t n", t=PACK))
-
-        def load_gate():
-            row = gate[0].rearrange("(c k) -> c k", k=GATE_RUN)
-            nc.sync.dma_start(out=gate_rows[0:GATE_PIECES, 0:GATE_RUN], in_=row)
-
-        def spread_gate():
-            turned = psum_once.tile([P, P], F32, name="turned", tag="second1")
-            nc.tensor.transpose(turned[:], gate_rows[:], identity[:])
-            gate_columns = sbuf("gate_columns", [P, GATE_PIECES], F32)
-            nc.scalar.copy(out=gate_columns[:], in_=turned[:, 0:GATE_PIECES])
-            count = GATE_PIECES // GATE_BANKS
-            for b in range(GATE_BANKS):
-                spread = psum_once.tile([P, count, P], F32, name="spread%d" % b, tag=("spare", "second2")[b])
-                for r in range(count):
-                    c = b * count + r
-                    nc.tensor.transpose(spread[:, r, :], gate_columns[:, c : c + 1].to_broadcast([P, P]), identity[:])
-                spreads[b] = spread
-
-        def keep_gate(b, tag):
-            gates[b] = sbuf("gates%d" % b, [P, T // GATE_BANKS], F32, tag=tag)
-            nc.scalar.copy(out=gates[b][:].rearrange("p (r k) -> p r k", k=GATE_RUN), in_=spreads[b][:, :, 0:GATE_RUN])
-
-        def gate_of(first, count):
-            b, start = divmod(first, T // GATE_BANKS)
-            return gates[b][:, start : start + count]
+        def load_frozen(e):
+            frozen_words[e] = sbuf("frozen_words%d" % e, [P, PASSES, 2 * N], U8)
+            nc.sync.dma_start(
+                out=frozen_words[e][:].bitcast(I32), in_=w_words[e].rearrange("s p b -> p s b").bitcast(I32)
+            )
 
         def load_frozen_scales(e, queue):
             for r in range(SCALE_ROWS):
                 rows = w_scales[e].rearrange("s (q r) n -> r q s n", r=SCALE_ROWS)[r]
                 queue.dma_start(out=frozen_scales[e][r:P:QUADRANT, :, :].bitcast(I32), in_=rows.bitcast(I32))
-
-        def load_frozen(e):
-            nc.sync.dma_start(
-                out=frozen_words[e][:].bitcast(I32), in_=w_words[e].rearrange("s p b -> p s b").bitcast(I32)
-            )
-
-        def gather_first_words(s):
-            window = token_words[s][:].bitcast(U32)
-            nc.vector.tensor_copy(out=first_words[s][:], in_=window.indirect(slot_list(0, C)))
-
-        def gather_later_words(s):
-            window = token_words[s][:].bitcast(U32)
-            nc.vector.tensor_copy(out=later_words[s][:], in_=window.indirect(slot_list(C, T - C)))
-
-        def gather_scales(first, count):
-            nc.vector.tensor_copy(
-                out=slot_scales[:, first : first + count], in_=token_scales[:].indirect(slot_list(first, count))
-            )
 
         def move_scales(queue, first, end):
             for s in range(1, PASSES):
@@ -201,148 +117,148 @@ def tile_moe_elr_gelu_kernel(
                     in_=slot_scales[SCALE_ROWS * s : SCALE_ROWS * s + MOVED_ROWS, first:end].bitcast(I32),
                 )
 
-        def round_wa(e, s):
-            dst = wa_bf16[e, s][:].rearrange("p (t m j) -> p m j t", t=PACK, j=PACK)
+        def load_token_scales(q, queue):
+            queue.dma_start(
+                out=token_scales[QUADRANT * q : QUADRANT * q + SCALE_ROWS * PASSES, :].bitcast(I32),
+                in_=x_scales[:, SCALE_ROWS * q : SCALE_ROWS * (q + 1), :].bitcast(I32),
+            )
+
+        def load_wb(e):
+            wb_raw[e] = sbuf("wb_raw%d" % e, [P, PACK, N], F32)
+            nc.sync.dma_start(out=wb_raw[e][:], in_=wb[e].rearrange("(p t) n -> p t n", t=PACK))
+
+        def gather_first_words(s):
+            first_words[s] = sbuf("first_words%d" % s, [P, C], U32)
+            window = token_words[s][:].bitcast(U32)
+            nc.vector.tensor_copy(out=first_words[s][:], in_=window.indirect(slot_list(0, C)))
+
+        def gather_later_words(s, tag=None):
+            later_words[s] = sbuf("later_words%d" % s, [P, T - C], U32, tag=tag)
+            window = token_words[s][:].bitcast(U32)
+            nc.vector.tensor_copy(out=later_words[s][:], in_=window.indirect(slot_list(C, T - C)))
+
+        def spread_gate():
+            turned = psum.tile([P, P], F32, name="turned", tag="bank5")
+            nc.tensor.transpose(turned[:], gate_rows[:], identity[:])
+            gate_columns = sbuf("gate_columns", [P, GATE_PIECES], F32)
+            nc.scalar.copy(out=gate_columns[:], in_=turned[:, 0:GATE_PIECES])
+            count = GATE_PIECES // GATE_BANKS
+            for b in range(GATE_BANKS):
+                spreads[b] = bank("spread%d" % b, count, 6 + b)
+                for r in range(count):
+                    c = b * count + r
+                    column = gate_columns[:, c : c + 1].to_broadcast([P, P])
+                    nc.tensor.transpose(spreads[b][:, r, :], column, identity[:])
+
+        def keep_gate(b, tag=None):
+            gates[b] = sbuf("gates%d" % b, [P, T // GATE_BANKS], F32, tag=tag)
+            nc.scalar.copy(out=gates[b][:].rearrange("p (r k) -> p r k", k=GATE_RUN), in_=spreads[b][:, :, 0:GATE_RUN])
+
+        def round_wa(e, s, share, tags, upper_first=False):
             src = wa_raw[e, s][:].rearrange("p j (m t) -> p m j t", t=PACK)
-            if s == LAST_PASS:
-                nc.vector.tensor_copy(out=dst[:, :, :, 0:HALF], in_=src[:, :, :, 0:HALF])
-                nc.vector.tensor_copy(out=dst[:, 0:LAST_SHARE, :, HALF:PACK], in_=src[:, 0:LAST_SHARE, :, HALF:PACK])
-                nc.scalar.copy(out=dst[:, LAST_SHARE:P, :, HALF:PACK], in_=src[:, LAST_SHARE:P, :, HALF:PACK])
-                return
-            if e > 0 and s == 0:
-                upper[e] = sbuf("upper%d" % e, [P, HALF * H], BF16, tag="inner_bf16_%d" % (e - 1))
-                high = upper[e][:].rearrange("p (t m j) -> p t m j", t=HALF, j=PACK)
-                rows = wa_raw[e, s][:].rearrange("p j (m t) -> p t m j", t=PACK)[:, HALF:PACK]
-                nc.scalar.copy(out=dst[:, :, :, 0:HALF], in_=src[:, :, :, 0:HALF])
-                nc.gpsimd.tensor_scalar(high[:, :, 0:GPSIMD_SHARE], rows[:, :, 0:GPSIMD_SHARE], 1.0, 0.0, MULT, ADD)
-                if GPSIMD_SHARE < P:
-                    pairs = upper[e][:].rearrange("p (t m j) -> p m j t", t=HALF, j=PACK)
-                    nc.scalar.copy(out=pairs[:, GPSIMD_SHARE:P], in_=src[:, GPSIMD_SHARE:P, :, HALF:PACK])
-                return
-            share = MIDDLE_SHARES[e] if s > 0 else (VERY_FIRST_SHARE if e == 0 else FIRST_SHARE)
-            if share:
-                nc.vector.tensor_copy(out=dst[:, 0:share, :, HALF:PACK], in_=src[:, 0:share, :, HALF:PACK])
-            nc.scalar.copy(out=dst[:, :, :, 0:HALF], in_=src[:, :, :, 0:HALF])
-            nc.scalar.copy(out=dst[:, share:P, :, HALF:PACK], in_=src[:, share:P, :, HALF:PACK])
+            for half in (1, 0) if upper_first else (0, 1):
+                wa_bf16[e, s, half] = sbuf("wa_bf16%d%d%d" % (e, s, half), [P, HALF * H], BF16, tag=tags[half])
+                dst = wa_bf16[e, s, half][:].rearrange("p (t m j) -> p m j t", t=HALF, j=PACK)
+                rows = src[:, :, :, half * HALF : (half + 1) * HALF]
+                cut = min(max(share - half * P, 0), P)
+                if cut > 0:
+                    nc.vector.tensor_copy(out=dst[:, 0:cut], in_=rows[:, 0:cut])
+                if cut < P:
+                    nc.scalar.copy(out=dst[:, cut:P], in_=rows[:, cut:P])
+
+        def quantise(name, values):
+            words = values.shape[1] // PACK
+            codes, scales = sbuf(name + "_codes", [P, words], U32), sbuf(name + "_scales", [P, words], U8)
+            nc.vector.quantize_mx(out=codes[:].bitcast(FP8X4), scales=scales[:], in_=values)
+            return codes, scales
 
         def first_products(e, s):
+            halves = [quantise("wa%d%d%d" % (e, s, half), wa_bf16[e, s, half][:]) for half in range(2)]
             if s == 0:
-                for u in range(2):
-                    h_banks[e, u] = bank("h", e, u, PACK)
-            half = HALF * P
-            todo = [(s, t) for t in range(PACK)]
-            codes, scales, values = wa_codes[e, s], wa_scales[e, s], wa_bf16[e, s]
-            cuts = [0, half, H] if (e == 0 and s == LAST_PASS) else [0, H]
-            if e > 0 and s > 0:
-                codes, scales, values = joint[e]
-                if s < LAST_PASS:
-                    cuts, todo = [0, half], todo[:HALF]
-                else:
-                    cuts, todo = [half, H + half, 2 * H], [(s - 1, t) for t in range(HALF, PACK)] + todo
-            if e > 0 and s == 0:
-                nc.vector.quantize_mx(
-                    out=codes[:, 0:half].bitcast(FP8X4), scales=scales[:, 0:half], in_=values[:, 0 : PACK * half]
-                )
-                nc.vector.quantize_mx(out=codes[:, half:H].bitcast(FP8X4), scales=scales[:, half:H], in_=upper[e][:])
-                cuts = [0]
-            for first, end in zip(cuts, cuts[1:]):
-                nc.vector.quantize_mx(
-                    out=codes[:, first:end].bitcast(FP8X4),
-                    scales=scales[:, first:end],
-                    in_=values[:, PACK * first : PACK * end],
-                )
-            for u in range(2):
-                order = todo[-HALF:] + todo[:-HALF] if (u == 1 and len(cuts) > 2) else todo
-                for step, (k, t) in enumerate(order):
-                    cols = slice(t * P, (t + 1) * P)
+                for u in range(UNITS):
+                    h_banks[e, u] = bank("h%d%d" % (e, u), PACK, 3 * e + u)
+            for u in range(UNITS):
+                order = list(range(PACK))
+                if u == 1 and s == LAST_PASS:
+                    order = order[HALF:] + order[:HALF]
+                for step, t in enumerate(order):
+                    codes, scales = halves[t // HALF]
+                    cols = slice(t % HALF * P, (t % HALF + 1) * P)
                     nc.tensor.matmul_mx(
                         out=h_banks[e, u][:, t, :],
-                        lhsT=wa_codes[e, k][:, cols].bitcast(FP8X4),
-                        lhsT_scale=wa_scales[e, k][:, cols],
-                        rhs=unit_words(e, k, u).bitcast(FP8X4),
-                        rhs_scale=slot_scales[SCALE_ROWS * k :, unit_slots(e, u)],
+                        lhsT=codes[:, cols].bitcast(FP8X4),
+                        lhsT_scale=scales[:, cols],
+                        rhs=unit_words(e, s, u).bitcast(FP8X4),
+                        rhs_scale=slot_scales[SCALE_ROWS * s :, unit_slots(e, u)],
                         start=(s == 0 and step == 0),
-                        stop=(s == LAST_PASS and step == len(order) - 1),
+                        stop=(s == LAST_PASS and step == PACK - 1),
                     )
 
         def round_wb(e):
-            nc.scalar.copy(
-                out=wb_bf16[e].rearrange("p (c r j) -> p c j r", r=RUN, j=PACK),
-                in_=wb_raw[e][:].rearrange("p j (c r) -> p c j r", r=RUN),
-            )
+            values = sbuf("wb_bf16%d" % e, [P, PACK * N], BF16)
+            dst = values[:].rearrange("p (c r j) -> p c j r", r=RUN, j=PACK)
+            src = wb_raw[e][:].rearrange("p j (c r) -> p c j r", r=RUN)
+            nc.vector.tensor_copy(out=dst[:, 0:WB_SHARE], in_=src[:, 0:WB_SHARE])
+            nc.scalar.copy(out=dst[:, WB_SHARE:], in_=src[:, WB_SHARE:])
+            return values
 
-        def frozen_products(e, u):
+        def frozen_products(e, u, nt, number):
             apart = e == LAST_EXPERT
             if apart:
-                y_tiles[e, u] = [bank("y", e, u, 1, nt)[:, 0, :] for nt in range(N_TILES)]
+                y_tiles[e, u, nt] = bank("y%d%d%d" % (e, u, nt), 1, number)[:, 0, :]
             else:
-                y_banks[e, u] = bank("y", e, u, N_TILES)
-                y_tiles[e, u] = [y_banks[e, u][:, nt, :] for nt in range(N_TILES)]
-            for nt in range(N_TILES):
-                for s in range(PASSES):
-                    nc.tensor.matmul_mx(
-                        out=y_tiles[e, u][nt],
-                        lhsT=frozen_words[e][:, s, 2 * P * nt : 2 * P * (nt + 1)].bitcast(FP4X4),
-                        lhsT_scale=frozen_scales[e][:, s, P * nt : P * (nt + 1)],
-                        rhs=unit_words(e, s, u).bitcast(FP8X4),
-                        rhs_scale=scales_from_zero[s][:, unit_slots(e, u)],
-                        start=(s == 0 and (nt == 0 or apart)),
-                        stop=False,
-                    )
+                if nt == 0:
+                    y_banks[e, u] = bank("y%d%d" % (e, u), N_TILES, number)
+                y_tiles[e, u, nt] = y_banks[e, u][:, nt, :]
+            for s in range(PASSES):
+                nc.tensor.matmul_mx(
+                    out=y_tiles[e, u, nt],
+                    lhsT=frozen_words[e][:, s, 2 * P * nt : 2 * P * (nt + 1)].bitcast(FP4X4),
+                    lhsT_scale=frozen_scales[e][:, s, P * nt : P * (nt + 1)],
+                    rhs=unit_words(e, s, u).bitcast(FP8X4),
+                    rhs_scale=scales_from_zero[s][:, unit_slots(e, u)],
+                    start=(s == 0 and (nt == 0 or apart)),
+                    stop=False,
+                )
 
         def quantise_hidden(e, u):
-            start = N + u * UNIT
-            end = start + UNIT
+            values = sbuf("h_bf16%d%d" % (e, u), [P, PACK * UNIT], BF16)
             nc.scalar.activation(
-                out=inner_bf16[e][:, PACK * start : PACK * end].rearrange("p (c t) -> p c t", t=PACK),
+                out=values[:].rearrange("p (c t) -> p c t", t=PACK),
                 in_=h_banks[e, u][:].rearrange("p t c -> p c t"),
                 func=GELU,
             )
-            first = 0 if u == 0 else start
-            nc.vector.quantize_mx(
-                out=inner_codes[e][:, first:end].bitcast(FP8X4),
-                scales=inner_scales[e][:, first:end],
-                in_=inner_bf16[e][:, PACK * first : PACK * end],
-            )
-            h_mx[e, u] = (inner_codes[e][:, start:end], inner_scales[e][:, start:end])
+            h_mx[e, u] = quantise("h%d%d" % (e, u), values[:])
 
         def second_products(e, u):
-            h_codes, h_scales = h_mx[e, u]
             for nt in range(N_TILES):
                 cols = slice(nt * P, (nt + 1) * P)
                 nc.tensor.matmul_mx(
-                    out=y_tiles[e, u][nt],
-                    lhsT=wb_codes[e][:, cols].bitcast(FP8X4),
-                    lhsT_scale=wb_scales[e][:, cols],
-                    rhs=h_codes.bitcast(FP8X4),
-                    rhs_scale=h_scales,
+                    out=y_tiles[e, u, nt],
+                    lhsT=wb_mx[e][0][:, cols].bitcast(FP8X4),
+                    lhsT_scale=wb_mx[e][1][:, cols],
+                    rhs=h_mx[e, u][0][:].bitcast(FP8X4),
+                    rhs_scale=h_mx[e, u][1][:],
                     start=False,
                     stop=(nt == N_TILES - 1 or e == LAST_EXPERT),
                 )
 
-        def return_by_vector(e):
-            sums[e, 0] = sbuf("sums%d0" % e, [P, N_TILES, UNIT], F32)
-            for nt in range(N_TILES):
-                nc.vector.tensor_tensor(sums[e, 0][:, nt, :], y_banks[e, 0][:, nt, :], unit_gate(e, 0), MULT)
-            for nt in range(N_TILES):
-                nc.vector.tensor_copy(out=unit_window(e, 0, nt), in_=sums[e, 0][:, nt, :])
+        def leave_psum(e, u, tiles, tag=None):
+            sums[e, u] = sbuf("sums%d%d" % (e, u), [P, tiles, UNIT], F32, tag=tag)
+            both = unit_gate(e, u).unsqueeze(1).to_broadcast([P, tiles, UNIT])
+            nc.vector.tensor_tensor(sums[e, u][:], y_banks[e, u][:, 0:tiles, :], both, MULT)
 
-        def return_by_scalar(e, u):
-            cols = slice(u * UNIT, (u + 1) * UNIT)
-            nc.scalar.copy(out=last_sums[0][:, cols], in_=y_tiles[e, u][0])
-            nc.vector.tensor_tensor(last_sums[1][:, cols], y_tiles[e, u][1], unit_gate(e, u), MULT)
+        def scatter(e, u, tiles):
+            for nt in range(tiles):
+                nc.scalar.activation(out=unit_window(e, u, nt), in_=sums[e, u][:, nt, :], func=COPY)
 
-        def scatter_last(e):
-            places = slot_list(e * C, C)
-            nc.vector.tensor_tensor(results[0][:].indirect(places), last_sums[0][:], gate_of(e * C, C), MULT)
-            nc.scalar.activation(out=results[1][:].indirect(places), in_=last_sums[1][:], func=COPY)
-
-        def copy_late(e):
-            late_sums[e] = sbuf("late%d" % e, [P, N_TILES, UNIT], F32, tag="wa_raw%d%d" % (e + 1, LAST_PASS))
-            nc.scalar.copy(out=late_sums[e][:], in_=y_banks[e, 1][:])
-
-        def scatter_late(e, nt):
-            nc.vector.tensor_tensor(unit_window(e, 1, nt), late_sums[e][:, nt, :], unit_gate(e, 1), MULT)
+        def return_last(e, u):
+            plain = sbuf("plain%d" % u, [P, UNIT], F32)
+            gated = sbuf("gated%d" % u, [P, UNIT], F32)
+            nc.scalar.copy(out=plain[:], in_=y_tiles[e, u, 0])
+            nc.vector.tensor_tensor(gated[:], y_tiles[e, u, 1], unit_gate(e, u), MULT)
+            nc.vector.tensor_tensor(unit_window(e, u, 0), plain[:], unit_gate(e, u), MULT)
+            nc.scalar.activation(out=unit_window(e, u, 1), in_=gated[:], func=COPY)
 
         nc.vector.memset(token_scales[:].bitcast(I32), 0)
         nc.vector.memset(gate_rows[:], 0.0)
@@ -353,21 +269,21 @@ def tile_moe_elr_gelu_kernel(
         for s in range(1, PASSES):
             nc.vector.memset(scales_from_zero[s][:].bitcast(I32), 0)
 
-        for q in range(QUADRANTS):
-            (nc.gpsimd if q == 0 else nc.scalar).dma_start(
-                out=token_scales[QUADRANT * q : QUADRANT * q + SCALE_ROWS * PASSES, :].bitcast(I32),
-                in_=x_scales[:, SCALE_ROWS * q : SCALE_ROWS * (q + 1), :].bitcast(I32),
-            )
+        for q in range(1, QUADRANTS):
+            load_token_scales(q, nc.scalar)
         make_identity(nc, identity[:], nomemset=True)
         nc.scalar.activation(out=warm[:, 1:2], in_=warm[:, 0:1], func=GELU)
-        load_frozen_scales(0, nc.gpsimd)
 
         load_words(0)
         nc.sync.dma_start(offsets[:], offs)
-        load_gate()
+        load_token_scales(0, nc.sync)
         load_words(1)
-        for s in range(LAST_PASS):
-            load_wa(0, s)
+        load_wa(0, 0)
+        nc.sync.dma_start(
+            out=gate_rows[0:GATE_PIECES, 0:GATE_RUN], in_=gate[0].rearrange("(c k) -> c k", k=GATE_RUN)
+        )
+        load_wa(0, 1)
+        load_frozen_scales(0, nc.sync)
         load_words(LAST_PASS)
         load_wa(0, LAST_PASS)
 
@@ -376,11 +292,12 @@ def tile_moe_elr_gelu_kernel(
             gather_later_words(s)
         slot_scales = sbuf("slot_scales", [P, T], U8, tag="token_words1")
         scales_from_zero[0] = slot_scales
-        gather_scales(0, C)
-        gather_scales(C, T - C)
+        for first, count in ((0, C), (C, T - C)):
+            nc.vector.tensor_copy(
+                out=slot_scales[:, first : first + count], in_=token_scales[:].indirect(slot_list(first, count))
+            )
         load_wb(0)
-        move_scales(nc.sync, 0, C)
-        move_scales(nc.gpsimd, C, T)
+        move_scales(nc.sync, 0, T)
         load_frozen(0)
         for e in range(1, E):
             for s in range(PASSES):
@@ -388,44 +305,50 @@ def tile_moe_elr_gelu_kernel(
             load_wb(e)
             load_frozen_scales(e, nc.sync)
             load_frozen(e)
-        spread_gate()
-        keep_gate(0, "gates0")
+
         for s in range(LAST_PASS):
-            round_wa(0, s)
+            round_wa(0, s, HEAD_SHARES[s], staging(0, s), s == 0)
+            if s == 0:
+                spread_gate()
+            if s == LAST_PASS - 1:
+                gather_first_words(LAST_PASS)
             first_products(0, s)
-        keep_gate(1, "wa_raw01")
+        keep_gate(0, "wa_raw01")
+        keep_gate(1)
 
         for e in range(E):
-            round_wa(e, LAST_PASS)
-            if e > 0:
-                copy_late(e - 1)
-            round_wb(e)
-            if e == 0:
-                gather_first_words(LAST_PASS)
+            last = e == LAST_EXPERT
+            round_wa(e, LAST_PASS, LAST_SHARE, staging(e, LAST_PASS))
             first_products(e, LAST_PASS)
-            if e == 0:
-                later_words.append(sbuf("later_words%d" % LAST_PASS, [P, T - C], U32, tag="wa_bf160%d" % LAST_PASS))
-                gather_later_words(LAST_PASS)
-            if e > 0:
+            if last:
+                frozen_products(e, 0, 0, 1)
+                frozen_products(e, 0, 1, 2)
+                frozen_products(e, 1, 1, 4)
+            else:
                 for nt in range(N_TILES):
-                    scatter_late(e - 1, nt)
-            frozen_products(e, 0)
-            if e == LAST_EXPERT:
-                frozen_products(e, 1)
+                    frozen_products(e, 0, nt, 3 * e + 2)
+            values = round_wb(e)
+            if e == 0:
+                gather_later_words(LAST_PASS, staging(e, LAST_PASS)[1])
+            wb_mx[e] = quantise("wb%d" % e, values[:])
             quantise_hidden(e, 0)
             second_products(e, 0)
+            for nt in range(1 if last else N_TILES):
+                frozen_products(e, 1, nt, 3 * e)
             quantise_hidden(e, 1)
-            if e < LAST_EXPERT:
-                frozen_products(e, 1)
             second_products(e, 1)
-            if e < LAST_EXPERT:
-                return_by_vector(e)
-                for s in range(LAST_PASS):
-                    round_wa(e + 1, s)
-                    first_products(e + 1, s)
-        for u in range(2):
-            return_by_scalar(LAST_EXPERT, u)
-        scatter_last(LAST_EXPERT)
+            if last:
+                for u in range(UNITS):
+                    return_last(e, u)
+            else:
+                leave_psum(e, 0, N_TILES)
+                round_wa(e + 1, 0, FIRST_SHARE, staging(e + 1, 0))
+                leave_psum(e, 1, N_TILES)
+                first_products(e + 1, 0)
+                scatter(e, 0, N_TILES)
+                scatter(e, 1, N_TILES)
+                round_wa(e + 1, 1, MIDDLE_SHARE, staging(e + 1, 1))
+                first_products(e + 1, 1)
 
         for nt in range(N_TILES):
             nc.sync.dma_start(out=out[nt * P : (nt + 1) * P, :], in_=results[nt][:])

@@ -61,12 +61,14 @@ def tile_moe_elr_gelu_kernel(
         token_scales = sbuf("token_scales", [P, T], U8)
         scales_from_zero = {s: sbuf("moved%d" % s, [P, T], U8) for s in range(1, PASSES)}
         token_words = [sbuf("token_words%d" % s, [P, T], I32) for s in range(PASSES)]
-        frozen_scales = [sbuf("frozen_scales%d" % e, [P, PASSES, N], U8) for e in range(E)]
+        first_scales = sbuf("first_scales", [P, PASSES, N], U8)
+        later_scales = sbuf("later_scales", [P, LAST_EXPERT * PASSES, N], U8)
+        frozen_scales = [first_scales[:]] + [later_scales[:, e * PASSES : (e + 1) * PASSES] for e in range(LAST_EXPERT)]
         gate_rows = sbuf("gate_rows", [P, P], F32)
         identity = sbuf("identity", [P, P], F32)
         results = [sbuf("results%d" % nt, [P, T], F32) for nt in range(N_TILES)]
         warm = sbuf("warm", [P, 2], F32)
-        first_words, later_words, late = {}, {}, {}
+        first_words, later_words, last_words = {}, {}, {}
         frozen_words, wa_raw, wa_bf16, wa_mx, wb_raw, wb_mx = {}, {}, {}, {}, {}, {}
         h_banks, h_mx, y_tiles, y_banks, sums, gates, spreads = {}, {}, {}, {}, {}, {}, {}
 
@@ -82,6 +84,8 @@ def tile_moe_elr_gelu_kernel(
         def unit_words(e, s, u):
             if e == 0:
                 return first_words[s][:, unit_slots(0, u)]
+            if s == LAST_PASS:
+                return last_words[e][:, unit_slots(0, u)]
             return later_words[s][:, unit_slots(e - 1, u)]
 
         def unit_gate(e, u):
@@ -105,10 +109,10 @@ def tile_moe_elr_gelu_kernel(
                 out=frozen_words[e][:].bitcast(I32), in_=w_words[e].rearrange("s p b -> p s b").bitcast(I32)
             )
 
-        def load_frozen_scales(e, queue):
+        def load_frozen_scales(tile, experts, queue):
             for r in range(SCALE_ROWS):
-                rows = w_scales[e].rearrange("s (q r) n -> r q s n", r=SCALE_ROWS)[r]
-                queue.dma_start(out=frozen_scales[e][r:P:QUADRANT, :, :].bitcast(I32), in_=rows.bitcast(I32))
+                rows = w_scales[experts].rearrange("e s (q r) n -> r q (e s) n", r=SCALE_ROWS)[r]
+                queue.dma_start(out=tile[r:P:QUADRANT, :, :].bitcast(I32), in_=rows.bitcast(I32))
 
         def move_scales(queue, first, end):
             for s in range(1, PASSES):
@@ -132,10 +136,15 @@ def tile_moe_elr_gelu_kernel(
             window = token_words[s][:].bitcast(U32)
             nc.vector.tensor_copy(out=first_words[s][:], in_=window.indirect(slot_list(0, C)))
 
-        def gather_later_words(s, tag=None):
-            later_words[s] = sbuf("later_words%d" % s, [P, T - C], U32, tag=tag)
+        def gather_later_words(s):
+            later_words[s] = sbuf("later_words%d" % s, [P, T - C], U32)
             window = token_words[s][:].bitcast(U32)
             nc.vector.tensor_copy(out=later_words[s][:], in_=window.indirect(slot_list(C, T - C)))
+
+        def gather_last_words(e, tag):
+            last_words[e] = sbuf("last_words%d" % e, [P, C], U32, tag=tag)
+            window = token_words[LAST_PASS][:].bitcast(U32)
+            nc.vector.tensor_copy(out=last_words[e][:], in_=window.indirect(slot_list(e * C, C)))
 
         def spread_gate():
             turned = psum.tile([P, P], F32, name="turned", tag="bank5")
@@ -231,7 +240,7 @@ def tile_moe_elr_gelu_kernel(
             h_mx[e, u] = quantise("h%d%d" % (e, u), values[:])
 
         def second_products(e, u):
-            for nt in range(N_TILES):
+            for nt in reversed(range(N_TILES)):
                 cols = slice(nt * P, (nt + 1) * P)
                 nc.tensor.matmul_mx(
                     out=y_tiles[e, u, nt],
@@ -240,7 +249,7 @@ def tile_moe_elr_gelu_kernel(
                     rhs=h_mx[e, u][0][:].bitcast(FP8X4),
                     rhs_scale=h_mx[e, u][1][:],
                     start=False,
-                    stop=(nt == N_TILES - 1 or e == LAST_EXPERT),
+                    stop=(nt == 0 or e == LAST_EXPERT),
                 )
 
         def leave_psum(e, u, tiles, tag=None):
@@ -252,20 +261,21 @@ def tile_moe_elr_gelu_kernel(
             for nt in range(tiles):
                 nc.scalar.activation(out=unit_window(e, u, nt), in_=sums[e, u][:, nt, :], func=COPY)
 
-        def return_last(e, u):
-            plain = sbuf("plain%d" % u, [P, UNIT], F32)
-            gated = sbuf("gated%d" % u, [P, UNIT], F32)
-            nc.scalar.copy(out=plain[:], in_=y_tiles[e, u, 0])
-            nc.vector.tensor_tensor(gated[:], y_tiles[e, u, 1], unit_gate(e, u), MULT)
-            nc.vector.tensor_tensor(unit_window(e, u, 0), plain[:], unit_gate(e, u), MULT)
-            nc.scalar.activation(out=unit_window(e, u, 1), in_=gated[:], func=COPY)
+        def return_last(e):
+            gated = [sbuf("gated%d" % nt, [P, C], F32) for nt in range(N_TILES)]
+            for u in range(UNITS):
+                cols = unit_slots(0, u)
+                for nt in reversed(range(N_TILES)):
+                    nc.vector.tensor_tensor(gated[nt][:, cols], y_tiles[e, u, nt], unit_gate(e, u), MULT)
+                nc.scalar.activation(out=unit_window(e, u, 1), in_=gated[1][:, cols], func=COPY)
+            nc.vector.tensor_copy(out=results[0][:].indirect(slot_list(e * C, C)), in_=gated[0][:])
 
         nc.vector.memset(token_scales[:].bitcast(I32), 0)
         nc.vector.memset(gate_rows[:], 0.0)
         nc.vector.memset(identity[:], 0.0)
         nc.vector.memset(warm[:, 0:1], 0.0)
-        for e in range(E):
-            nc.vector.memset(frozen_scales[e][:].rearrange("p s n -> p (s n)").bitcast(I32), 0)
+        for tile in (later_scales, first_scales):
+            nc.vector.memset(tile[:].rearrange("p s n -> p (s n)").bitcast(I32), 0)
         for s in range(1, PASSES):
             nc.vector.memset(scales_from_zero[s][:].bitcast(I32), 0)
 
@@ -273,17 +283,18 @@ def tile_moe_elr_gelu_kernel(
             load_token_scales(q, nc.scalar)
         make_identity(nc, identity[:], nomemset=True)
         nc.scalar.activation(out=warm[:, 1:2], in_=warm[:, 0:1], func=GELU)
+        load_frozen_scales(later_scales, slice(1, E), nc.gpsimd)
 
         load_words(0)
         nc.sync.dma_start(offsets[:], offs)
-        load_token_scales(0, nc.sync)
         load_words(1)
+        load_token_scales(0, nc.sync)
         load_wa(0, 0)
         nc.sync.dma_start(
             out=gate_rows[0:GATE_PIECES, 0:GATE_RUN], in_=gate[0].rearrange("(c k) -> c k", k=GATE_RUN)
         )
         load_wa(0, 1)
-        load_frozen_scales(0, nc.sync)
+        load_frozen_scales(first_scales, slice(0, 1), nc.sync)
         load_words(LAST_PASS)
         load_wa(0, LAST_PASS)
 
@@ -297,13 +308,13 @@ def tile_moe_elr_gelu_kernel(
                 out=slot_scales[:, first : first + count], in_=token_scales[:].indirect(slot_list(first, count))
             )
         load_wb(0)
-        move_scales(nc.sync, 0, T)
+        move_scales(nc.sync, 0, C)
+        move_scales(nc.gpsimd, C, T)
         load_frozen(0)
         for e in range(1, E):
             for s in range(PASSES):
                 load_wa(e, s)
             load_wb(e)
-            load_frozen_scales(e, nc.sync)
             load_frozen(e)
 
         for s in range(LAST_PASS):
@@ -328,8 +339,8 @@ def tile_moe_elr_gelu_kernel(
                 for nt in range(N_TILES):
                     frozen_products(e, 0, nt, 3 * e + 2)
             values = round_wb(e)
-            if e == 0:
-                gather_later_words(LAST_PASS, staging(e, LAST_PASS)[1])
+            if not last:
+                gather_last_words(e + 1, staging(e, LAST_PASS)[1])
             wb_mx[e] = quantise("wb%d" % e, values[:])
             quantise_hidden(e, 0)
             second_products(e, 0)
@@ -338,8 +349,7 @@ def tile_moe_elr_gelu_kernel(
             quantise_hidden(e, 1)
             second_products(e, 1)
             if last:
-                for u in range(UNITS):
-                    return_last(e, u)
+                return_last(e)
             else:
                 leave_psum(e, 0, N_TILES)
                 round_wa(e + 1, 0, FIRST_SHARE, staging(e + 1, 0))
@@ -350,5 +360,5 @@ def tile_moe_elr_gelu_kernel(
                 round_wa(e + 1, 1, MIDDLE_SHARE, staging(e + 1, 1))
                 first_products(e + 1, 1)
 
-        for nt in range(N_TILES):
+        for nt in reversed(range(N_TILES)):
             nc.sync.dma_start(out=out[nt * P : (nt + 1) * P, :], in_=results[nt][:])

@@ -308,8 +308,7 @@ def tile_moe_elr_gelu_kernel(
                 out=slot_scales[:, first : first + count], in_=token_scales[:].indirect(slot_list(first, count))
             )
         load_wb(0)
-        move_scales(nc.sync, 0, C)
-        move_scales(nc.gpsimd, C, T)
+        move_scales(nc.sync, 0, T)
         load_frozen(0)
         for e in range(1, E):
             for s in range(PASSES):

@@ -37,10 +37,10 @@ GATE_PIECES = 8
 GATE_RUN = T // GATE_PIECES
 GATE_BANKS = 2
 HEAD_SHARES = (0, 64)
-FIRST_SHARE = 256
+FIRST_SHARES = (256, 128)
 MIDDLE_SHARE = 256
 LAST_SHARE = 160
-WB_SHARE = 52
+WB_SHARE = 40
 
 
 def tile_moe_elr_gelu_kernel(
@@ -61,14 +61,12 @@ def tile_moe_elr_gelu_kernel(
         token_scales = sbuf("token_scales", [P, T], U8)
         scales_from_zero = {s: sbuf("moved%d" % s, [P, T], U8) for s in range(1, PASSES)}
         token_words = [sbuf("token_words%d" % s, [P, T], I32) for s in range(PASSES)]
-        first_scales = sbuf("first_scales", [P, PASSES, N], U8)
-        later_scales = sbuf("later_scales", [P, LAST_EXPERT * PASSES, N], U8)
-        frozen_scales = [first_scales[:]] + [later_scales[:, e * PASSES : (e + 1) * PASSES] for e in range(LAST_EXPERT)]
+        frozen_scales = sbuf("frozen_scales", [P, E * PASSES, N], U8)
         gate_rows = sbuf("gate_rows", [P, P], F32)
         identity = sbuf("identity", [P, P], F32)
         results = [sbuf("results%d" % nt, [P, T], F32) for nt in range(N_TILES)]
         warm = sbuf("warm", [P, 2], F32)
-        first_words, later_words, last_words = {}, {}, {}
+        first_words, later_words, last_words, late = {}, {}, {}, {}
         frozen_words, wa_raw, wa_bf16, wa_mx, wb_raw, wb_mx = {}, {}, {}, {}, {}, {}
         h_banks, h_mx, y_tiles, y_banks, sums, gates, spreads = {}, {}, {}, {}, {}, {}, {}
 
@@ -109,10 +107,10 @@ def tile_moe_elr_gelu_kernel(
                 out=frozen_words[e][:].bitcast(I32), in_=w_words[e].rearrange("s p b -> p s b").bitcast(I32)
             )
 
-        def load_frozen_scales(tile, experts, queue):
+        def load_frozen_scales():
             for r in range(SCALE_ROWS):
-                rows = w_scales[experts].rearrange("e s (q r) n -> r q (e s) n", r=SCALE_ROWS)[r]
-                queue.dma_start(out=tile[r:P:QUADRANT, :, :].bitcast(I32), in_=rows.bitcast(I32))
+                rows = w_scales.rearrange("e s (q r) n -> r q (e s) n", r=SCALE_ROWS)[r]
+                nc.sync.dma_start(out=frozen_scales[r:P:QUADRANT, :, :].bitcast(I32), in_=rows.bitcast(I32))
 
         def move_scales(queue, first, end):
             for s in range(1, PASSES):
@@ -223,7 +221,7 @@ def tile_moe_elr_gelu_kernel(
                 nc.tensor.matmul_mx(
                     out=y_tiles[e, u, nt],
                     lhsT=frozen_words[e][:, s, 2 * P * nt : 2 * P * (nt + 1)].bitcast(FP4X4),
-                    lhsT_scale=frozen_scales[e][:, s, P * nt : P * (nt + 1)],
+                    lhsT_scale=frozen_scales[:, e * PASSES + s, P * nt : P * (nt + 1)],
                     rhs=unit_words(e, s, u).bitcast(FP8X4),
                     rhs_scale=scales_from_zero[s][:, unit_slots(e, u)],
                     start=(s == 0 and (nt == 0 or apart)),
@@ -261,6 +259,13 @@ def tile_moe_elr_gelu_kernel(
             for nt in range(tiles):
                 nc.scalar.activation(out=unit_window(e, u, nt), in_=sums[e, u][:, nt, :], func=COPY)
 
+        def copy_late(e):
+            late[e] = sbuf("late%d" % e, [P, UNIT], F32, tag="wa_raw%d%d" % (e + 1, LAST_PASS))
+            nc.scalar.copy(out=late[e][:], in_=y_tiles[e, 1, 1])
+
+        def scatter_late(e):
+            nc.vector.tensor_tensor(unit_window(e, 1, 1), late[e][:], unit_gate(e, 1), MULT)
+
         def return_last(e):
             gated = [sbuf("gated%d" % nt, [P, C], F32) for nt in range(N_TILES)]
             for u in range(UNITS):
@@ -274,8 +279,7 @@ def tile_moe_elr_gelu_kernel(
         nc.vector.memset(gate_rows[:], 0.0)
         nc.vector.memset(identity[:], 0.0)
         nc.vector.memset(warm[:, 0:1], 0.0)
-        for tile in (later_scales, first_scales):
-            nc.vector.memset(tile[:].rearrange("p s n -> p (s n)").bitcast(I32), 0)
+        nc.vector.memset(frozen_scales[:].rearrange("p s n -> p (s n)").bitcast(I32), 0)
         for s in range(1, PASSES):
             nc.vector.memset(scales_from_zero[s][:].bitcast(I32), 0)
 
@@ -283,7 +287,6 @@ def tile_moe_elr_gelu_kernel(
             load_token_scales(q, nc.scalar)
         make_identity(nc, identity[:], nomemset=True)
         nc.scalar.activation(out=warm[:, 1:2], in_=warm[:, 0:1], func=GELU)
-        load_frozen_scales(later_scales, slice(1, E), nc.gpsimd)
 
         load_words(0)
         nc.sync.dma_start(offsets[:], offs)
@@ -294,7 +297,7 @@ def tile_moe_elr_gelu_kernel(
             out=gate_rows[0:GATE_PIECES, 0:GATE_RUN], in_=gate[0].rearrange("(c k) -> c k", k=GATE_RUN)
         )
         load_wa(0, 1)
-        load_frozen_scales(first_scales, slice(0, 1), nc.sync)
+        load_frozen_scales()
         load_words(LAST_PASS)
         load_wa(0, LAST_PASS)
 
@@ -312,9 +315,11 @@ def tile_moe_elr_gelu_kernel(
         load_frozen(0)
         for e in range(1, E):
             for s in range(PASSES):
+                if e < LAST_EXPERT and s == LAST_PASS:
+                    load_frozen(e)
                 load_wa(e, s)
             load_wb(e)
-            load_frozen(e)
+        load_frozen(LAST_EXPERT)
 
         for s in range(LAST_PASS):
             round_wa(0, s, HEAD_SHARES[s], staging(0, s), s == 0)
@@ -329,6 +334,8 @@ def tile_moe_elr_gelu_kernel(
         for e in range(E):
             last = e == LAST_EXPERT
             round_wa(e, LAST_PASS, LAST_SHARE, staging(e, LAST_PASS))
+            if last:
+                copy_late(e - 1)
             first_products(e, LAST_PASS)
             if last:
                 frozen_products(e, 0, 0, 1)
@@ -340,6 +347,8 @@ def tile_moe_elr_gelu_kernel(
             values = round_wb(e)
             if not last:
                 gather_last_words(e + 1, staging(e, LAST_PASS)[1])
+            if last:
+                scatter_late(e - 1)
             wb_mx[e] = quantise("wb%d" % e, values[:])
             quantise_hidden(e, 0)
             second_products(e, 0)
@@ -350,12 +359,13 @@ def tile_moe_elr_gelu_kernel(
             if last:
                 return_last(e)
             else:
+                early = N_TILES if e == 0 else 1
+                round_wa(e + 1, 0, FIRST_SHARES[e], staging(e + 1, 0))
                 leave_psum(e, 0, N_TILES)
-                round_wa(e + 1, 0, FIRST_SHARE, staging(e + 1, 0))
-                leave_psum(e, 1, N_TILES)
+                leave_psum(e, 1, early)
                 first_products(e + 1, 0)
                 scatter(e, 0, N_TILES)
-                scatter(e, 1, N_TILES)
+                scatter(e, 1, early)
                 round_wa(e + 1, 1, MIDDLE_SHARE, staging(e + 1, 1))
                 first_products(e + 1, 1)
 

@@ -28,19 +28,18 @@ UNIT = 128
 UNITS = C // UNIT
 N_TILES = N // P
 QUADRANT = 32
-QUADRANTS = P // QUADRANT
 SCALE_ROWS = 4
-MOVED_ROWS = QUADRANT * (QUADRANTS - 1) + SCALE_ROWS
 RUN = 2
 HALF = PACK // 2
 GATE_PIECES = 8
 GATE_RUN = T // GATE_PIECES
 GATE_BANKS = 2
-HEAD_SHARES = (0, 64)
-FIRST_SHARES = (256, 128)
+HEAD_SHARES = (0, 0)
+FIRST_SHARE = 128
+LEAD = 64
 MIDDLE_SHARE = 256
 LAST_SHARE = 160
-WB_SHARE = 40
+WB_SHARES = (8, 8, 40)
 
 
 def tile_moe_elr_gelu_kernel(
@@ -58,15 +57,14 @@ def tile_moe_elr_gelu_kernel(
             return psum.tile([P, width, P], F32, name=name, tag="bank%d" % number)
 
         offsets = keep.tile([P, T // 16], U16, name="offsets")
-        token_scales = sbuf("token_scales", [P, T], U8)
-        scales_from_zero = {s: sbuf("moved%d" % s, [P, T], U8) for s in range(1, PASSES)}
+        token_scales = sbuf("token_scales", [P, PASSES, T], U8)
         token_words = [sbuf("token_words%d" % s, [P, T], I32) for s in range(PASSES)]
         frozen_scales = sbuf("frozen_scales", [P, E * PASSES, N], U8)
         gate_rows = sbuf("gate_rows", [P, P], F32)
         identity = sbuf("identity", [P, P], F32)
         results = [sbuf("results%d" % nt, [P, T], F32) for nt in range(N_TILES)]
         warm = sbuf("warm", [P, 2], F32)
-        first_words, later_words, last_words, late = {}, {}, {}, {}
+        slot_words, slot_scales, late = {}, {}, {}
         frozen_words, wa_raw, wa_bf16, wa_mx, wb_raw, wb_mx = {}, {}, {}, {}, {}, {}
         h_banks, h_mx, y_tiles, y_banks, sums, gates, spreads = {}, {}, {}, {}, {}, {}, {}
 
@@ -78,13 +76,6 @@ def tile_moe_elr_gelu_kernel(
 
         def unit_slots(e, u):
             return slice(e * C + u * UNIT, e * C + (u + 1) * UNIT)
-
-        def unit_words(e, s, u):
-            if e == 0:
-                return first_words[s][:, unit_slots(0, u)]
-            if s == LAST_PASS:
-                return last_words[e][:, unit_slots(0, u)]
-            return later_words[s][:, unit_slots(e - 1, u)]
 
         def unit_gate(e, u):
             b, start = divmod(e * C + u * UNIT, T // GATE_BANKS)
@@ -112,37 +103,24 @@ def tile_moe_elr_gelu_kernel(
                 rows = w_scales.rearrange("e s (q r) n -> r q (e s) n", r=SCALE_ROWS)[r]
                 nc.sync.dma_start(out=frozen_scales[r:P:QUADRANT, :, :].bitcast(I32), in_=rows.bitcast(I32))
 
-        def move_scales(queue, first, end):
-            for s in range(1, PASSES):
-                queue.dma_start(
-                    out=scales_from_zero[s][0:MOVED_ROWS, first:end].bitcast(I32),
-                    in_=slot_scales[SCALE_ROWS * s : SCALE_ROWS * s + MOVED_ROWS, first:end].bitcast(I32),
-                )
-
-        def load_token_scales(q, queue):
-            queue.dma_start(
-                out=token_scales[QUADRANT * q : QUADRANT * q + SCALE_ROWS * PASSES, :].bitcast(I32),
-                in_=x_scales[:, SCALE_ROWS * q : SCALE_ROWS * (q + 1), :].bitcast(I32),
-            )
+        def load_token_scales(r, queue):
+            rows = x_scales.rearrange("s (q r) t -> r q s t", r=SCALE_ROWS)[r]
+            queue.dma_start(out=token_scales[r:P:QUADRANT, :, :].bitcast(I32), in_=rows.bitcast(I32))
 
         def load_wb(e):
             wb_raw[e] = sbuf("wb_raw%d" % e, [P, PACK, N], F32)
             nc.sync.dma_start(out=wb_raw[e][:], in_=wb[e].rearrange("(p t) n -> p t n", t=PACK))
 
-        def gather_first_words(s):
-            first_words[s] = sbuf("first_words%d" % s, [P, C], U32)
-            window = token_words[s][:].bitcast(U32)
-            nc.vector.tensor_copy(out=first_words[s][:], in_=window.indirect(slot_list(0, C)))
-
-        def gather_later_words(s):
-            later_words[s] = sbuf("later_words%d" % s, [P, T - C], U32)
-            window = token_words[s][:].bitcast(U32)
-            nc.vector.tensor_copy(out=later_words[s][:], in_=window.indirect(slot_list(C, T - C)))
-
-        def gather_last_words(e, tag):
-            last_words[e] = sbuf("last_words%d" % e, [P, C], U32, tag=tag)
-            window = token_words[LAST_PASS][:].bitcast(U32)
-            nc.vector.tensor_copy(out=last_words[e][:], in_=window.indirect(slot_list(e * C, C)))
+        def gather(kind, s, experts, tag=None):
+            window, dtype, found = {
+                "words": (token_words[s][:].bitcast(U32), U32, slot_words),
+                "scales": (token_scales[:, s, :], U8, slot_scales),
+            }[kind]
+            count = len(experts) * C
+            tile = sbuf("slot_%s%d%d" % (kind, s, experts[0]), [P, count], dtype, tag=tag)
+            nc.vector.tensor_copy(out=tile[:], in_=window.indirect(slot_list(experts[0] * C, count)))
+            for n, e in enumerate(experts):
+                found[e, s] = tile[:, n * C : (n + 1) * C]
 
         def spread_gate():
             turned = psum.tile([P, P], F32, name="turned", tag="bank5")
@@ -161,14 +139,18 @@ def tile_moe_elr_gelu_kernel(
             gates[b] = sbuf("gates%d" % b, [P, T // GATE_BANKS], F32, tag=tag)
             nc.scalar.copy(out=gates[b][:].rearrange("p (r k) -> p r k", k=GATE_RUN), in_=spreads[b][:, :, 0:GATE_RUN])
 
-        def round_wa(e, s, share, tags, upper_first=False):
+        def round_wa(e, s, share, tags, upper_first=False, between=None):
             src = wa_raw[e, s][:].rearrange("p j (m t) -> p m j t", t=PACK)
             for half in (1, 0) if upper_first else (0, 1):
                 wa_bf16[e, s, half] = sbuf("wa_bf16%d%d%d" % (e, s, half), [P, HALF * H], BF16, tag=tags[half])
                 dst = wa_bf16[e, s, half][:].rearrange("p (t m j) -> p m j t", t=HALF, j=PACK)
                 rows = src[:, :, :, half * HALF : (half + 1) * HALF]
                 cut = min(max(share - half * P, 0), P)
-                if cut > 0:
+                if between and half == 0:
+                    nc.vector.tensor_copy(out=dst[:, 0:LEAD], in_=rows[:, 0:LEAD])
+                    between()
+                    nc.vector.tensor_copy(out=dst[:, LEAD:cut], in_=rows[:, LEAD:cut])
+                elif cut > 0:
                     nc.vector.tensor_copy(out=dst[:, 0:cut], in_=rows[:, 0:cut])
                 if cut < P:
                     nc.scalar.copy(out=dst[:, cut:P], in_=rows[:, cut:P])
@@ -195,8 +177,8 @@ def tile_moe_elr_gelu_kernel(
                         out=h_banks[e, u][:, t, :],
                         lhsT=codes[:, cols].bitcast(FP8X4),
                         lhsT_scale=scales[:, cols],
-                        rhs=unit_words(e, s, u).bitcast(FP8X4),
-                        rhs_scale=slot_scales[SCALE_ROWS * s :, unit_slots(e, u)],
+                        rhs=slot_words[e, s][:, unit_slots(0, u)].bitcast(FP8X4),
+                        rhs_scale=slot_scales[e, s][:, unit_slots(0, u)],
                         start=(s == 0 and step == 0),
                         stop=(s == LAST_PASS and step == PACK - 1),
                     )
@@ -205,8 +187,8 @@ def tile_moe_elr_gelu_kernel(
             values = sbuf("wb_bf16%d" % e, [P, PACK * N], BF16)
             dst = values[:].rearrange("p (c r j) -> p c j r", r=RUN, j=PACK)
             src = wb_raw[e][:].rearrange("p j (c r) -> p c j r", r=RUN)
-            nc.vector.tensor_copy(out=dst[:, 0:WB_SHARE], in_=src[:, 0:WB_SHARE])
-            nc.scalar.copy(out=dst[:, WB_SHARE:], in_=src[:, WB_SHARE:])
+            nc.vector.tensor_copy(out=dst[:, 0 : WB_SHARES[e]], in_=src[:, 0 : WB_SHARES[e]])
+            nc.scalar.copy(out=dst[:, WB_SHARES[e] :], in_=src[:, WB_SHARES[e] :])
             return values
 
         def frozen_products(e, u, nt, number):
@@ -222,8 +204,8 @@ def tile_moe_elr_gelu_kernel(
                     out=y_tiles[e, u, nt],
                     lhsT=frozen_words[e][:, s, 2 * P * nt : 2 * P * (nt + 1)].bitcast(FP4X4),
                     lhsT_scale=frozen_scales[:, e * PASSES + s, P * nt : P * (nt + 1)],
-                    rhs=unit_words(e, s, u).bitcast(FP8X4),
-                    rhs_scale=scales_from_zero[s][:, unit_slots(e, u)],
+                    rhs=slot_words[e, s][:, unit_slots(0, u)].bitcast(FP8X4),
+                    rhs_scale=slot_scales[e, s][:, unit_slots(0, u)],
                     start=(s == 0 and (nt == 0 or apart)),
                     stop=False,
                 )
@@ -275,16 +257,14 @@ def tile_moe_elr_gelu_kernel(
                 nc.scalar.activation(out=unit_window(e, u, 1), in_=gated[1][:, cols], func=COPY)
             nc.vector.tensor_copy(out=results[0][:].indirect(slot_list(e * C, C)), in_=gated[0][:])
 
-        nc.vector.memset(token_scales[:].bitcast(I32), 0)
+        nc.vector.memset(token_scales[:].rearrange("p s t -> p (s t)").bitcast(I32), 0)
         nc.vector.memset(gate_rows[:], 0.0)
         nc.vector.memset(identity[:], 0.0)
         nc.vector.memset(warm[:, 0:1], 0.0)
         nc.vector.memset(frozen_scales[:].rearrange("p s n -> p (s n)").bitcast(I32), 0)
-        for s in range(1, PASSES):
-            nc.vector.memset(scales_from_zero[s][:].bitcast(I32), 0)
 
-        for q in range(1, QUADRANTS):
-            load_token_scales(q, nc.scalar)
+        for r in range(1, SCALE_ROWS):
+            load_token_scales(r, nc.scalar)
         make_identity(nc, identity[:], nomemset=True)
         nc.scalar.activation(out=warm[:, 1:2], in_=warm[:, 0:1], func=GELU)
 
@@ -299,20 +279,15 @@ def tile_moe_elr_gelu_kernel(
         load_wa(0, 1)
         load_frozen_scales()
         load_words(LAST_PASS)
+        load_frozen(0)
         load_wa(0, LAST_PASS)
 
-        for s in range(LAST_PASS):
-            gather_first_words(s)
-            gather_later_words(s)
-        slot_scales = sbuf("slot_scales", [P, T], U8, tag="token_words1")
-        scales_from_zero[0] = slot_scales
-        for first, count in ((0, C), (C, T - C)):
-            nc.vector.tensor_copy(
-                out=slot_scales[:, first : first + count], in_=token_scales[:].indirect(slot_list(first, count))
-            )
+        for kind in ("words", "scales"):
+            for s in range(LAST_PASS):
+                gather(kind, s, [0])
+                gather(kind, s, [1, 2])
+        gather("scales", LAST_PASS, [0])
         load_wb(0)
-        move_scales(nc.sync, 0, T)
-        load_frozen(0)
         for e in range(1, E):
             for s in range(PASSES):
                 if e < LAST_EXPERT and s == LAST_PASS:
@@ -326,7 +301,7 @@ def tile_moe_elr_gelu_kernel(
             if s == 0:
                 spread_gate()
             if s == LAST_PASS - 1:
-                gather_first_words(LAST_PASS)
+                gather("words", LAST_PASS, [0])
             first_products(0, s)
         keep_gate(0, "wa_raw01")
         keep_gate(1)
@@ -346,7 +321,8 @@ def tile_moe_elr_gelu_kernel(
                     frozen_products(e, 0, nt, 3 * e + 2)
             values = round_wb(e)
             if not last:
-                gather_last_words(e + 1, staging(e, LAST_PASS)[1])
+                for half, kind in enumerate(("scales", "words")):
+                    gather(kind, LAST_PASS, [e + 1], staging(e, LAST_PASS)[half])
             if last:
                 scatter_late(e - 1)
             wb_mx[e] = quantise("wb%d" % e, values[:])
@@ -360,8 +336,7 @@ def tile_moe_elr_gelu_kernel(
                 return_last(e)
             else:
                 early = N_TILES if e == 0 else 1
-                round_wa(e + 1, 0, FIRST_SHARES[e], staging(e + 1, 0))
-                leave_psum(e, 0, N_TILES)
+                round_wa(e + 1, 0, FIRST_SHARE, staging(e + 1, 0), between=lambda: leave_psum(e, 0, N_TILES))
                 leave_psum(e, 1, early)
                 first_products(e + 1, 0)
                 scatter(e, 0, N_TILES)

@@ -59,7 +59,9 @@ def tile_moe_elr_gelu_kernel(
         offsets = keep.tile([P, T // 16], U16, name="offsets")
         token_scales = sbuf("token_scales", [P, PASSES, T], U8)
         token_words = [sbuf("token_words%d" % s, [P, T], I32) for s in range(PASSES)]
-        frozen_scales = sbuf("frozen_scales", [P, E * PASSES, N], U8)
+        early_scales = sbuf("early_scales", [P, LAST_EXPERT * PASSES, N], U8)
+        last_scales = sbuf("last_scales", [P, PASSES, N], U8)
+        frozen_scales = [early_scales[:, e * PASSES : (e + 1) * PASSES] for e in range(LAST_EXPERT)] + [last_scales[:]]
         gate_rows = sbuf("gate_rows", [P, P], F32)
         identity = sbuf("identity", [P, P], F32)
         results = [sbuf("results%d" % nt, [P, T], F32) for nt in range(N_TILES)]
@@ -98,10 +100,10 @@ def tile_moe_elr_gelu_kernel(
                 out=frozen_words[e][:].bitcast(I32), in_=w_words[e].rearrange("s p b -> p s b").bitcast(I32)
             )
 
-        def load_frozen_scales():
+        def load_frozen_scales(tile, experts, queue):
             for r in range(SCALE_ROWS):
-                rows = w_scales.rearrange("e s (q r) n -> r q (e s) n", r=SCALE_ROWS)[r]
-                nc.sync.dma_start(out=frozen_scales[r:P:QUADRANT, :, :].bitcast(I32), in_=rows.bitcast(I32))
+                rows = w_scales[experts].rearrange("e s (q r) n -> r q (e s) n", r=SCALE_ROWS)[r]
+                queue.dma_start(out=tile[r:P:QUADRANT, :, :].bitcast(I32), in_=rows.bitcast(I32))
 
         def load_token_scales(r, queue):
             rows = x_scales.rearrange("s (q r) t -> r q s t", r=SCALE_ROWS)[r]
@@ -203,7 +205,7 @@ def tile_moe_elr_gelu_kernel(
                 nc.tensor.matmul_mx(
                     out=y_tiles[e, u, nt],
                     lhsT=frozen_words[e][:, s, 2 * P * nt : 2 * P * (nt + 1)].bitcast(FP4X4),
-                    lhsT_scale=frozen_scales[:, e * PASSES + s, P * nt : P * (nt + 1)],
+                    lhsT_scale=frozen_scales[e][:, s, P * nt : P * (nt + 1)],
                     rhs=slot_words[e, s][:, unit_slots(0, u)].bitcast(FP8X4),
                     rhs_scale=slot_scales[e, s][:, unit_slots(0, u)],
                     start=(s == 0 and (nt == 0 or apart)),
@@ -261,7 +263,8 @@ def tile_moe_elr_gelu_kernel(
         nc.vector.memset(gate_rows[:], 0.0)
         nc.vector.memset(identity[:], 0.0)
         nc.vector.memset(warm[:, 0:1], 0.0)
-        nc.vector.memset(frozen_scales[:].rearrange("p s n -> p (s n)").bitcast(I32), 0)
+        for tile in (early_scales, last_scales):
+            nc.vector.memset(tile[:].rearrange("p s n -> p (s n)").bitcast(I32), 0)
 
         for r in range(1, SCALE_ROWS):
             load_token_scales(r, nc.scalar)
@@ -277,7 +280,7 @@ def tile_moe_elr_gelu_kernel(
             out=gate_rows[0:GATE_PIECES, 0:GATE_RUN], in_=gate[0].rearrange("(c k) -> c k", k=GATE_RUN)
         )
         load_wa(0, 1)
-        load_frozen_scales()
+        load_frozen_scales(early_scales, slice(0, LAST_EXPERT), nc.sync)
         load_words(LAST_PASS)
         load_frozen(0)
         load_wa(0, LAST_PASS)
@@ -295,6 +298,7 @@ def tile_moe_elr_gelu_kernel(
                 load_wa(e, s)
             load_wb(e)
         load_frozen(LAST_EXPERT)
+        load_frozen_scales(last_scales, slice(LAST_EXPERT, E), nc.sync)
 
         for s in range(LAST_PASS):
             round_wa(0, s, HEAD_SHARES[s], staging(0, s), s == 0)

@@ -34,12 +34,16 @@ HALF = PACK // 2
 GATE_PIECES = 8
 GATE_RUN = T // GATE_PIECES
 GATE_BANKS = 2
-HEAD_SHARES = (0, 0)
-FIRST_SHARE = 128
+
+ALL_GROUPS = 2 * P
+LAST_SHARE = 168
 LEAD = 64
-MIDDLE_SHARE = 256
-LAST_SHARE = 160
-WB_SHARES = (8, 8, 40)
+WB_SHARE = 8
+LAST_WB_SHARE = 56
+
+LAST_Y_BANKS = {(0, 0): 1, (0, 1): 2, (1, 1): 4, (1, 0): 3 * LAST_EXPERT}
+TURNED_BANK = 5
+SPREAD_BANK = 6
 
 
 def tile_moe_elr_gelu_kernel(
@@ -66,18 +70,18 @@ def tile_moe_elr_gelu_kernel(
         identity = sbuf("identity", [P, P], F32)
         results = [sbuf("results%d" % nt, [P, T], F32) for nt in range(N_TILES)]
         warm = sbuf("warm", [P, 2], F32)
-        slot_words, slot_scales, late = {}, {}, {}
-        frozen_words, wa_raw, wa_bf16, wa_mx, wb_raw, wb_mx = {}, {}, {}, {}, {}, {}
+        slot_words, slot_scales = {}, {}
+        frozen_words, wa_raw, wa_bf16, wb_raw, wb_mx = {}, {}, {}, {}, {}
         h_banks, h_mx, y_tiles, y_banks, sums, gates, spreads = {}, {}, {}, {}, {}, {}, {}
 
-        def staging(e, s):
-            return ["staging%d%d%d" % (e, s, half) for half in range(2)]
+        def half_name(e, s, half):
+            return "wa_bf16%d%d%d" % (e, s, half)
 
         def slot_list(first, count):
             return offsets[:, first // 16 : (first + count) // 16]
 
-        def unit_slots(e, u):
-            return slice(e * C + u * UNIT, e * C + (u + 1) * UNIT)
+        def unit_columns(u):
+            return slice(u * UNIT, (u + 1) * UNIT)
 
         def unit_gate(e, u):
             b, start = divmod(e * C + u * UNIT, T // GATE_BANKS)
@@ -100,10 +104,10 @@ def tile_moe_elr_gelu_kernel(
                 out=frozen_words[e][:].bitcast(I32), in_=w_words[e].rearrange("s p b -> p s b").bitcast(I32)
             )
 
-        def load_frozen_scales(tile, experts, queue):
+        def load_frozen_scales(tile, experts):
             for r in range(SCALE_ROWS):
                 rows = w_scales[experts].rearrange("e s (q r) n -> r q (e s) n", r=SCALE_ROWS)[r]
-                queue.dma_start(out=tile[r:P:QUADRANT, :, :].bitcast(I32), in_=rows.bitcast(I32))
+                nc.sync.dma_start(out=tile[r:P:QUADRANT, :, :].bitcast(I32), in_=rows.bitcast(I32))
 
         def load_token_scales(r, queue):
             rows = x_scales.rearrange("s (q r) t -> r q s t", r=SCALE_ROWS)[r]
@@ -125,13 +129,13 @@ def tile_moe_elr_gelu_kernel(
                 found[e, s] = tile[:, n * C : (n + 1) * C]
 
         def spread_gate():
-            turned = psum.tile([P, P], F32, name="turned", tag="bank5")
+            turned = psum.tile([P, P], F32, name="turned", tag="bank%d" % TURNED_BANK)
             nc.tensor.transpose(turned[:], gate_rows[:], identity[:])
             gate_columns = sbuf("gate_columns", [P, GATE_PIECES], F32)
             nc.scalar.copy(out=gate_columns[:], in_=turned[:, 0:GATE_PIECES])
             count = GATE_PIECES // GATE_BANKS
             for b in range(GATE_BANKS):
-                spreads[b] = bank("spread%d" % b, count, 6 + b)
+                spreads[b] = bank("spread%d" % b, count, SPREAD_BANK + b)
                 for r in range(count):
                     c = b * count + r
                     column = gate_columns[:, c : c + 1].to_broadcast([P, P])
@@ -141,21 +145,19 @@ def tile_moe_elr_gelu_kernel(
             gates[b] = sbuf("gates%d" % b, [P, T // GATE_BANKS], F32, tag=tag)
             nc.scalar.copy(out=gates[b][:].rearrange("p (r k) -> p r k", k=GATE_RUN), in_=spreads[b][:, :, 0:GATE_RUN])
 
-        def round_wa(e, s, share, tags, upper_first=False, between=None):
-            src = wa_raw[e, s][:].rearrange("p j (m t) -> p m j t", t=PACK)
-            for half in (1, 0) if upper_first else (0, 1):
-                wa_bf16[e, s, half] = sbuf("wa_bf16%d%d%d" % (e, s, half), [P, HALF * H], BF16, tag=tags[half])
-                dst = wa_bf16[e, s, half][:].rearrange("p (t m j) -> p m j t", t=HALF, j=PACK)
-                rows = src[:, :, :, half * HALF : (half + 1) * HALF]
+        def round_half(e, s, half, cuts):
+            if (e, s, half) not in wa_bf16:
+                wa_bf16[e, s, half] = sbuf(half_name(e, s, half), [P, HALF * H], BF16)
+            dst = wa_bf16[e, s, half][:].rearrange("p (t m j) -> p m j t", t=HALF, j=PACK)
+            src = wa_raw[e, s][:].rearrange("p j (m t) -> p m j t", t=PACK)[:, :, :, half * HALF : (half + 1) * HALF]
+            for copy, first, end in cuts:
+                copy(out=dst[:, first:end], in_=src[:, first:end])
+
+        def round_wa(e, s, share, halves=(0, 1)):
+            for half in halves:
                 cut = min(max(share - half * P, 0), P)
-                if between and half == 0:
-                    nc.vector.tensor_copy(out=dst[:, 0:LEAD], in_=rows[:, 0:LEAD])
-                    between()
-                    nc.vector.tensor_copy(out=dst[:, LEAD:cut], in_=rows[:, LEAD:cut])
-                elif cut > 0:
-                    nc.vector.tensor_copy(out=dst[:, 0:cut], in_=rows[:, 0:cut])
-                if cut < P:
-                    nc.scalar.copy(out=dst[:, cut:P], in_=rows[:, cut:P])
+                cuts = [(nc.vector.tensor_copy, 0, cut), (nc.scalar.copy, cut, P)]
+                round_half(e, s, half, [part for part in cuts if part[1] < part[2]])
 
         def quantise(name, values):
             words = values.shape[1] // PACK
@@ -179,8 +181,8 @@ def tile_moe_elr_gelu_kernel(
                         out=h_banks[e, u][:, t, :],
                         lhsT=codes[:, cols].bitcast(FP8X4),
                         lhsT_scale=scales[:, cols],
-                        rhs=slot_words[e, s][:, unit_slots(0, u)].bitcast(FP8X4),
-                        rhs_scale=slot_scales[e, s][:, unit_slots(0, u)],
+                        rhs=slot_words[e, s][:, unit_columns(u)].bitcast(FP8X4),
+                        rhs_scale=slot_scales[e, s][:, unit_columns(u)],
                         start=(s == 0 and step == 0),
                         stop=(s == LAST_PASS and step == PACK - 1),
                     )
@@ -189,25 +191,26 @@ def tile_moe_elr_gelu_kernel(
             values = sbuf("wb_bf16%d" % e, [P, PACK * N], BF16)
             dst = values[:].rearrange("p (c r j) -> p c j r", r=RUN, j=PACK)
             src = wb_raw[e][:].rearrange("p j (c r) -> p c j r", r=RUN)
-            nc.vector.tensor_copy(out=dst[:, 0 : WB_SHARES[e]], in_=src[:, 0 : WB_SHARES[e]])
-            nc.scalar.copy(out=dst[:, WB_SHARES[e] :], in_=src[:, WB_SHARES[e] :])
+            share = LAST_WB_SHARE if e == LAST_EXPERT else WB_SHARE
+            nc.vector.tensor_copy(out=dst[:, 0:share], in_=src[:, 0:share])
+            nc.scalar.copy(out=dst[:, share:], in_=src[:, share:])
             return values
 
-        def frozen_products(e, u, nt, number):
+        def frozen_products(e, u, nt):
             apart = e == LAST_EXPERT
             if apart:
-                y_tiles[e, u, nt] = bank("y%d%d%d" % (e, u, nt), 1, number)[:, 0, :]
+                y_tiles[e, u, nt] = bank("y%d%d%d" % (e, u, nt), 1, LAST_Y_BANKS[u, nt])[:, 0, :]
             else:
                 if nt == 0:
-                    y_banks[e, u] = bank("y%d%d" % (e, u), N_TILES, number)
+                    y_banks[e, u] = bank("y%d%d" % (e, u), N_TILES, 3 * e + 2 if u == 0 else 3 * e)
                 y_tiles[e, u, nt] = y_banks[e, u][:, nt, :]
             for s in range(PASSES):
                 nc.tensor.matmul_mx(
                     out=y_tiles[e, u, nt],
                     lhsT=frozen_words[e][:, s, 2 * P * nt : 2 * P * (nt + 1)].bitcast(FP4X4),
                     lhsT_scale=frozen_scales[e][:, s, P * nt : P * (nt + 1)],
-                    rhs=slot_words[e, s][:, unit_slots(0, u)].bitcast(FP8X4),
-                    rhs_scale=slot_scales[e, s][:, unit_slots(0, u)],
+                    rhs=slot_words[e, s][:, unit_columns(u)].bitcast(FP8X4),
+                    rhs_scale=slot_scales[e, s][:, unit_columns(u)],
                     start=(s == 0 and (nt == 0 or apart)),
                     stop=False,
                 )
@@ -234,8 +237,8 @@ def tile_moe_elr_gelu_kernel(
                     stop=(nt == 0 or e == LAST_EXPERT),
                 )
 
-        def leave_psum(e, u, tiles, tag=None):
-            sums[e, u] = sbuf("sums%d%d" % (e, u), [P, tiles, UNIT], F32, tag=tag)
+        def leave_psum(e, u, tiles):
+            sums[e, u] = sbuf("sums%d%d" % (e, u), [P, tiles, UNIT], F32)
             both = unit_gate(e, u).unsqueeze(1).to_broadcast([P, tiles, UNIT])
             nc.vector.tensor_tensor(sums[e, u][:], y_banks[e, u][:, 0:tiles, :], both, MULT)
 
@@ -244,16 +247,14 @@ def tile_moe_elr_gelu_kernel(
                 nc.scalar.activation(out=unit_window(e, u, nt), in_=sums[e, u][:, nt, :], func=COPY)
 
         def copy_late(e):
-            late[e] = sbuf("late%d" % e, [P, UNIT], F32, tag="wa_raw%d%d" % (e + 1, LAST_PASS))
-            nc.scalar.copy(out=late[e][:], in_=y_tiles[e, 1, 1])
-
-        def scatter_late(e):
-            nc.vector.tensor_tensor(unit_window(e, 1, 1), late[e][:], unit_gate(e, 1), MULT)
+            late = sbuf("late", [P, UNIT], F32, tag="wa_raw%d%d" % (e + 1, LAST_PASS))
+            nc.scalar.copy(out=late[:], in_=y_tiles[e, 1, 1])
+            return late
 
         def return_last(e):
             gated = [sbuf("gated%d" % nt, [P, C], F32) for nt in range(N_TILES)]
             for u in range(UNITS):
-                cols = unit_slots(0, u)
+                cols = unit_columns(u)
                 for nt in reversed(range(N_TILES)):
                     nc.vector.tensor_tensor(gated[nt][:, cols], y_tiles[e, u, nt], unit_gate(e, u), MULT)
                 nc.scalar.activation(out=unit_window(e, u, 1), in_=gated[1][:, cols], func=COPY)
@@ -280,7 +281,7 @@ def tile_moe_elr_gelu_kernel(
             out=gate_rows[0:GATE_PIECES, 0:GATE_RUN], in_=gate[0].rearrange("(c k) -> c k", k=GATE_RUN)
         )
         load_wa(0, 1)
-        load_frozen_scales(early_scales, slice(0, LAST_EXPERT), nc.sync)
+        load_frozen_scales(early_scales, slice(0, LAST_EXPERT))
         load_words(LAST_PASS)
         load_frozen(0)
         load_wa(0, LAST_PASS)
@@ -298,10 +299,10 @@ def tile_moe_elr_gelu_kernel(
                 load_wa(e, s)
             load_wb(e)
         load_frozen(LAST_EXPERT)
-        load_frozen_scales(last_scales, slice(LAST_EXPERT, E), nc.sync)
+        load_frozen_scales(last_scales, slice(LAST_EXPERT, E))
 
         for s in range(LAST_PASS):
-            round_wa(0, s, HEAD_SHARES[s], staging(0, s), s == 0)
+            round_wa(0, s, 0, (1, 0) if s == 0 else (0, 1))
             if s == 0:
                 spread_gate()
             if s == LAST_PASS - 1:
@@ -312,40 +313,38 @@ def tile_moe_elr_gelu_kernel(
 
         for e in range(E):
             last = e == LAST_EXPERT
-            round_wa(e, LAST_PASS, LAST_SHARE, staging(e, LAST_PASS))
+            round_wa(e, LAST_PASS, LAST_SHARE)
             if last:
-                copy_late(e - 1)
+                late = copy_late(e - 1)
             first_products(e, LAST_PASS)
-            if last:
-                frozen_products(e, 0, 0, 1)
-                frozen_products(e, 0, 1, 2)
-                frozen_products(e, 1, 1, 4)
-            else:
-                for nt in range(N_TILES):
-                    frozen_products(e, 0, nt, 3 * e + 2)
+            for nt in reversed(range(N_TILES)) if last else range(N_TILES):
+                frozen_products(e, 0, nt)
             values = round_wb(e)
-            if not last:
-                for half, kind in enumerate(("scales", "words")):
-                    gather(kind, LAST_PASS, [e + 1], staging(e, LAST_PASS)[half])
             if last:
-                scatter_late(e - 1)
+                nc.vector.tensor_tensor(unit_window(e - 1, 1, 1), late[:], unit_gate(e - 1, 1), MULT)
+            else:
+                for half, kind in enumerate(("scales", "words")):
+                    gather(kind, LAST_PASS, [e + 1], half_name(e, LAST_PASS, half))
             wb_mx[e] = quantise("wb%d" % e, values[:])
             quantise_hidden(e, 0)
             second_products(e, 0)
-            for nt in range(1 if last else N_TILES):
-                frozen_products(e, 1, nt, 3 * e)
+            for nt in reversed(range(N_TILES)) if last else range(N_TILES):
+                frozen_products(e, 1, nt)
             quantise_hidden(e, 1)
             second_products(e, 1)
             if last:
                 return_last(e)
             else:
-                early = N_TILES if e == 0 else 1
-                round_wa(e + 1, 0, FIRST_SHARE, staging(e + 1, 0), between=lambda: leave_psum(e, 0, N_TILES))
-                leave_psum(e, 1, early)
+                second_tiles = N_TILES - 1 if e == LAST_EXPERT - 1 else N_TILES
+                round_half(e + 1, 0, 0, [(nc.vector.tensor_copy, 0, LEAD)])
+                leave_psum(e, 0, N_TILES)
+                round_half(e + 1, 0, 0, [(nc.vector.tensor_copy, LEAD, P)])
+                round_half(e + 1, 0, 1, [(nc.scalar.copy, 0, P)])
+                leave_psum(e, 1, second_tiles)
                 first_products(e + 1, 0)
                 scatter(e, 0, N_TILES)
-                scatter(e, 1, early)
-                round_wa(e + 1, 1, MIDDLE_SHARE, staging(e + 1, 1))
+                scatter(e, 1, second_tiles)
+                round_wa(e + 1, 1, ALL_GROUPS)
                 first_products(e + 1, 1)
 
         for nt in reversed(range(N_TILES)):

@@ -55,7 +55,7 @@ def tile_moe_elr_gelu_kernel(
         psum = ctx.enter_context(tc.psum_pool(name="psum", bufs=1))
 
         def sbuf(name, shape, dtype, tag=None):
-            return keep.tile(shape, dtype, name=name, tag=tag or name, align_bytes=64)
+            return keep.tile(shape, dtype, name=name, tag=tag or name, align_bytes=256)
 
         def bank(name, width, number):
             return psum.tile([P, width, P], F32, name=name, tag="bank%d" % number)

from contextlib import ExitStack

import concourse.mybir as mybir
from concourse.masks import make_identity

K, T, E, C, H, N = 1536, 768, 3, 256, 512, 256
FLOPS = 2 * E * C * (K * N + K * H + H * N)

F32 = mybir.dt.float32
BF16 = mybir.dt.bfloat16
I32 = mybir.dt.int32
U32 = mybir.dt.uint32
U16 = mybir.dt.uint16
U8 = mybir.dt.uint8
FP8X4 = mybir.dt.float8_e4m3fn_x4
FP4X4 = mybir.dt.float4_e2m1fn_x4
GELU = mybir.ActivationFunctionType.Gelu_apprx_tanh
COPY = mybir.ActivationFunctionType.Copy
MULT = mybir.AluOpType.mult

P = 128
PACK = 4
K_PASS = P * PACK
PASSES = K // K_PASS
LAST_PASS = PASSES - 1
LAST_EXPERT = E - 1
UNIT = 128
UNITS = C // UNIT
N_TILES = N // P
QUADRANT = 32
SCALE_ROWS = 4
RUN = 2
HALF = PACK // 2
GATE_PIECES = 8
GATE_RUN = T // GATE_PIECES
GATE_BANKS = 2

ALL_GROUPS = 2 * P
LAST_SHARE = 168
LEAD = 64
WB_SHARE = 8
LAST_WB_SHARE = 56

LAST_Y_BANKS = {(0, 0): 1, (0, 1): 2, (1, 1): 4, (1, 0): 3 * LAST_EXPERT}
TURNED_BANK = 5
SPREAD_BANK = 6


def tile_moe_elr_gelu_kernel(
    tc, x_words, x_scales, w_words, w_scales, wa, wb, gate, offs, out
):
    nc = tc.nc
    with ExitStack() as ctx:
        keep = ctx.enter_context(tc.tile_pool(name="keep", bufs=1))
        psum = ctx.enter_context(tc.psum_pool(name="psum", bufs=1))

        def sbuf(name, shape, dtype, tag=None):
            return keep.tile(shape, dtype, name=name, tag=tag or name, align_bytes=256)

        def bank(name, width, number):
            return psum.tile([P, width, P], F32, name=name, tag="bank%d" % number)

        offsets = keep.tile([P, T // 16], U16, name="offsets")
        token_scales = sbuf("token_scales", [P, PASSES, T], U8)
        token_words = [sbuf("token_words%d" % s, [P, T], I32) for s in range(PASSES)]
        early_scales = sbuf("early_scales", [P, LAST_EXPERT * PASSES, N], U8)
        last_scales = sbuf("last_scales", [P, PASSES, N], U8)
        frozen_scales = [early_scales[:, e * PASSES : (e + 1) * PASSES] for e in range(LAST_EXPERT)] + [last_scales[:]]
        gate_rows = sbuf("gate_rows", [P, P], F32)
        identity = sbuf("identity", [P, P], F32)
        results = [sbuf("results%d" % nt, [P, T], F32) for nt in range(N_TILES)]
        warm = sbuf("warm", [P, 2], F32)
        slot_words, slot_scales = {}, {}
        frozen_words, wa_raw, wa_bf16, wb_raw, wb_mx = {}, {}, {}, {}, {}
        h_banks, h_mx, y_tiles, y_banks, sums, gates, spreads = {}, {}, {}, {}, {}, {}, {}

        def half_name(e, s, half):
            return "wa_bf16%d%d%d" % (e, s, half)

        def slot_list(first, count):
            return offsets[:, first // 16 : (first + count) // 16]

        def unit_columns(u):
            return slice(u * UNIT, (u + 1) * UNIT)

        def unit_gate(e, u):
            b, start = divmod(e * C + u * UNIT, T // GATE_BANKS)
            return gates[b][:, start : start + UNIT]

        def unit_window(e, u, nt):
            return results[nt][:].indirect(slot_list(e * C + u * UNIT, UNIT))

        def load_words(s):
            nc.sync.dma_start(out=token_words[s][:], in_=x_words[s].rearrange("p t d -> p (t d)").bitcast(I32))

        def load_wa(e, s):
            wa_raw[e, s] = sbuf("wa_raw%d%d" % (e, s), [P, PACK, H], F32)
            rows = wa[e, s * K_PASS : (s + 1) * K_PASS, :].rearrange("(p j) i -> p j i", j=PACK)
            nc.sync.dma_start(out=wa_raw[e, s][:], in_=rows)

        def load_frozen(e):
            frozen_words[e] = sbuf("frozen_words%d" % e, [P, PASSES, 2 * N], U8)
            nc.sync.dma_start(
                out=frozen_words[e][:].bitcast(I32), in_=w_words[e].rearrange("s p b -> p s b").bitcast(I32)
            )

        def load_frozen_scales(tile, experts):
            for r in range(SCALE_ROWS):
                rows = w_scales[experts].rearrange("e s (q r) n -> r q (e s) n", r=SCALE_ROWS)[r]
                nc.sync.dma_start(out=tile[r:P:QUADRANT, :, :].bitcast(I32), in_=rows.bitcast(I32))

        def load_token_scales(r, queue):
            rows = x_scales.rearrange("s (q r) t -> r q s t", r=SCALE_ROWS)[r]
            queue.dma_start(out=token_scales[r:P:QUADRANT, :, :].bitcast(I32), in_=rows.bitcast(I32))

        def load_wb(e):
            wb_raw[e] = sbuf("wb_raw%d" % e, [P, PACK, N], F32)
            nc.sync.dma_start(out=wb_raw[e][:], in_=wb[e].rearrange("(p t) n -> p t n", t=PACK))

        def gather(kind, s, experts, tag=None):
            window, dtype, found = {
                "words": (token_words[s][:].bitcast(U32), U32, slot_words),
                "scales": (token_scales[:, s, :], U8, slot_scales),
            }[kind]
            count = len(experts) * C
            tile = sbuf("slot_%s%d%d" % (kind, s, experts[0]), [P, count], dtype, tag=tag)
            nc.vector.tensor_copy(out=tile[:], in_=window.indirect(slot_list(experts[0] * C, count)))
            for n, e in enumerate(experts):
                found[e, s] = tile[:, n * C : (n + 1) * C]

        def spread_gate():
            turned = psum.tile([P, P], F32, name="turned", tag="bank%d" % TURNED_BANK)
            nc.tensor.transpose(turned[:], gate_rows[:], identity[:])
            gate_columns = sbuf("gate_columns", [P, GATE_PIECES], F32)
            nc.scalar.copy(out=gate_columns[:], in_=turned[:, 0:GATE_PIECES])
            count = GATE_PIECES // GATE_BANKS
            for b in range(GATE_BANKS):
                spreads[b] = bank("spread%d" % b, count, SPREAD_BANK + b)
                for r in range(count):
                    c = b * count + r
                    column = gate_columns[:, c : c + 1].to_broadcast([P, P])
                    nc.tensor.transpose(spreads[b][:, r, :], column, identity[:])

        def keep_gate(b, tag=None):
            gates[b] = sbuf("gates%d" % b, [P, T // GATE_BANKS], F32, tag=tag)
            nc.scalar.copy(out=gates[b][:].rearrange("p (r k) -> p r k", k=GATE_RUN), in_=spreads[b][:, :, 0:GATE_RUN])

        def round_half(e, s, half, cuts):
            if (e, s, half) not in wa_bf16:
                wa_bf16[e, s, half] = sbuf(half_name(e, s, half), [P, HALF * H], BF16)
            dst = wa_bf16[e, s, half][:].rearrange("p (t m j) -> p m j t", t=HALF, j=PACK)
            src = wa_raw[e, s][:].rearrange("p j (m t) -> p m j t", t=PACK)[:, :, :, half * HALF : (half + 1) * HALF]
            for copy, first, end in cuts:
                copy(out=dst[:, first:end], in_=src[:, first:end])

        def round_wa(e, s, share, halves=(0, 1)):
            for half in halves:
                cut = min(max(share - half * P, 0), P)
                cuts = [(nc.vector.tensor_copy, 0, cut), (nc.scalar.copy, cut, P)]
                round_half(e, s, half, [part for part in cuts if part[1] < part[2]])

        def quantise(name, values):
            words = values.shape[1] // PACK
            codes, scales = sbuf(name + "_codes", [P, words], U32), sbuf(name + "_scales", [P, words], U8)
            nc.vector.quantize_mx(out=codes[:].bitcast(FP8X4), scales=scales[:], in_=values)
            return codes, scales

        def first_products(e, s):
            halves = [quantise("wa%d%d%d" % (e, s, half), wa_bf16[e, s, half][:]) for half in range(2)]
            if s == 0:
                for u in range(UNITS):
                    h_banks[e, u] = bank("h%d%d" % (e, u), PACK, 3 * e + u)
            for u in range(UNITS):
                order = list(range(PACK))
                if u == 1 and s == LAST_PASS:
                    order = order[HALF:] + order[:HALF]
                for step, t in enumerate(order):
                    codes, scales = halves[t // HALF]
                    cols = slice(t % HALF * P, (t % HALF + 1) * P)
                    nc.tensor.matmul_mx(
                        out=h_banks[e, u][:, t, :],
                        lhsT=codes[:, cols].bitcast(FP8X4),
                        lhsT_scale=scales[:, cols],
                        rhs=slot_words[e, s][:, unit_columns(u)].bitcast(FP8X4),
                        rhs_scale=slot_scales[e, s][:, unit_columns(u)],
                        start=(s == 0 and step == 0),
                        stop=(s == LAST_PASS and step == PACK - 1),
                    )

        def round_wb(e):
            values = sbuf("wb_bf16%d" % e, [P, PACK * N], BF16)
            dst = values[:].rearrange("p (c r j) -> p c j r", r=RUN, j=PACK)
            src = wb_raw[e][:].rearrange("p j (c r) -> p c j r", r=RUN)
            share = LAST_WB_SHARE if e == LAST_EXPERT else WB_SHARE
            nc.vector.tensor_copy(out=dst[:, 0:share], in_=src[:, 0:share])
            nc.scalar.copy(out=dst[:, share:], in_=src[:, share:])
            return values

        def frozen_products(e, u, nt):
            apart = e == LAST_EXPERT
            if apart:
                y_tiles[e, u, nt] = bank("y%d%d%d" % (e, u, nt), 1, LAST_Y_BANKS[u, nt])[:, 0, :]
            else:
                if nt == 0:
                    y_banks[e, u] = bank("y%d%d" % (e, u), N_TILES, 3 * e + 2 if u == 0 else 3 * e)
                y_tiles[e, u, nt] = y_banks[e, u][:, nt, :]
            for s in range(PASSES):
                nc.tensor.matmul_mx(
                    out=y_tiles[e, u, nt],
                    lhsT=frozen_words[e][:, s, 2 * P * nt : 2 * P * (nt + 1)].bitcast(FP4X4),
                    lhsT_scale=frozen_scales[e][:, s, P * nt : P * (nt + 1)],
                    rhs=slot_words[e, s][:, unit_columns(u)].bitcast(FP8X4),
                    rhs_scale=slot_scales[e, s][:, unit_columns(u)],
                    start=(s == 0 and (nt == 0 or apart)),
                    stop=False,
                )

        def quantise_hidden(e, u):
            values = sbuf("h_bf16%d%d" % (e, u), [P, PACK * UNIT], BF16)
            nc.scalar.activation(
                out=values[:].rearrange("p (c t) -> p c t", t=PACK),
                in_=h_banks[e, u][:].rearrange("p t c -> p c t"),
                func=GELU,
            )
            h_mx[e, u] = quantise("h%d%d" % (e, u), values[:])

        def second_products(e, u):
            for nt in reversed(range(N_TILES)):
                cols = slice(nt * P, (nt + 1) * P)
                nc.tensor.matmul_mx(
                    out=y_tiles[e, u, nt],
                    lhsT=wb_mx[e][0][:, cols].bitcast(FP8X4),
                    lhsT_scale=wb_mx[e][1][:, cols],
                    rhs=h_mx[e, u][0][:].bitcast(FP8X4),
                    rhs_scale=h_mx[e, u][1][:],
                    start=False,
                    stop=(nt == 0 or e == LAST_EXPERT),
                )

        def leave_psum(e, u, tiles):
            sums[e, u] = sbuf("sums%d%d" % (e, u), [P, tiles, UNIT], F32)
            both = unit_gate(e, u).unsqueeze(1).to_broadcast([P, tiles, UNIT])
            nc.vector.tensor_tensor(sums[e, u][:], y_banks[e, u][:, 0:tiles, :], both, MULT)

        def scatter(e, u, tiles):
            for nt in range(tiles):
                nc.scalar.activation(out=unit_window(e, u, nt), in_=sums[e, u][:, nt, :], func=COPY)

        def copy_late(e):
            late = sbuf("late", [P, UNIT], F32, tag="wa_raw%d%d" % (e + 1, LAST_PASS))
            nc.scalar.copy(out=late[:], in_=y_tiles[e, 1, 1])
            return late

        def return_last(e):
            gated = [sbuf("gated%d" % nt, [P, C], F32) for nt in range(N_TILES)]
            for u in range(UNITS):
                cols = unit_columns(u)
                for nt in reversed(range(N_TILES)):
                    nc.vector.tensor_tensor(gated[nt][:, cols], y_tiles[e, u, nt], unit_gate(e, u), MULT)
                nc.scalar.activation(out=unit_window(e, u, 1), in_=gated[1][:, cols], func=COPY)
            nc.vector.tensor_copy(out=results[0][:].indirect(slot_list(e * C, C)), in_=gated[0][:])

        nc.vector.memset(token_scales[:].rearrange("p s t -> p (s t)").bitcast(I32), 0)
        nc.vector.memset(gate_rows[:], 0.0)
        nc.vector.memset(identity[:], 0.0)
        nc.vector.memset(warm[:, 0:1], 0.0)
        for tile in (early_scales, last_scales):
            nc.vector.memset(tile[:].rearrange("p s n -> p (s n)").bitcast(I32), 0)

        for r in range(1, SCALE_ROWS):
            load_token_scales(r, nc.scalar)
        make_identity(nc, identity[:], nomemset=True)
        nc.scalar.activation(out=warm[:, 1:2], in_=warm[:, 0:1], func=GELU)

        load_words(0)
        nc.sync.dma_start(offsets[:], offs)
        load_words(1)
        load_token_scales(0, nc.sync)
        load_wa(0, 0)
        nc.sync.dma_start(
            out=gate_rows[0:GATE_PIECES, 0:GATE_RUN], in_=gate[0].rearrange("(c k) -> c k", k=GATE_RUN)
        )
        load_wa(0, 1)
        load_frozen_scales(early_scales, slice(0, LAST_EXPERT))
        load_words(LAST_PASS)
        load_frozen(0)
        load_wa(0, LAST_PASS)

        for kind in ("words", "scales"):
            for s in range(LAST_PASS):
                gather(kind, s, [0])
                gather(kind, s, [1, 2])
        gather("scales", LAST_PASS, [0])
        load_wb(0)
        for e in range(1, E):
            for s in range(PASSES):
                if e < LAST_EXPERT and s == LAST_PASS:
                    load_frozen(e)
                load_wa(e, s)
            load_wb(e)
        load_frozen(LAST_EXPERT)
        load_frozen_scales(last_scales, slice(LAST_EXPERT, E))

        for s in range(LAST_PASS):
            round_wa(0, s, 0, (1, 0) if s == 0 else (0, 1))
            if s == 0:
                spread_gate()
            if s == LAST_PASS - 1:
                gather("words", LAST_PASS, [0])
            first_products(0, s)
        keep_gate(0, "wa_raw01")
        keep_gate(1)

        for e in range(E):
            last = e == LAST_EXPERT
            round_wa(e, LAST_PASS, LAST_SHARE)
            if last:
                late = copy_late(e - 1)
            first_products(e, LAST_PASS)
            for nt in reversed(range(N_TILES)) if last else range(N_TILES):
                frozen_products(e, 0, nt)
            values = round_wb(e)
            if last:
                nc.vector.tensor_tensor(unit_window(e - 1, 1, 1), late[:], unit_gate(e - 1, 1), MULT)
            else:
                for half, kind in enumerate(("scales", "words")):
                    gather(kind, LAST_PASS, [e + 1], half_name(e, LAST_PASS, half))
            wb_mx[e] = quantise("wb%d" % e, values[:])
            quantise_hidden(e, 0)
            second_products(e, 0)
            for nt in reversed(range(N_TILES)) if last else range(N_TILES):
                frozen_products(e, 1, nt)
            quantise_hidden(e, 1)
            second_products(e, 1)
            if last:
                return_last(e)
            else:
                second_tiles = N_TILES - 1 if e == LAST_EXPERT - 1 else N_TILES
                round_half(e + 1, 0, 0, [(nc.vector.tensor_copy, 0, LEAD)])
                leave_psum(e, 0, N_TILES)
                round_half(e + 1, 0, 0, [(nc.vector.tensor_copy, LEAD, P)])
                round_half(e + 1, 0, 1, [(nc.scalar.copy, 0, P)])
                leave_psum(e, 1, second_tiles)
                first_products(e + 1, 0)
                scatter(e, 0, N_TILES)
                scatter(e, 1, second_tiles)
                round_wa(e + 1, 1, ALL_GROUPS)
                first_products(e + 1, 1)

        for nt in reversed(range(N_TILES)):
            nc.sync.dma_start(out=out[nt * P : (nt + 1) * P, :], in_=results[nt][:])
